import numpy as np
import ml_dtypes


def mxq(x, axis, fmt="e4m3"):
    dtype, down = {"e4m3": (ml_dtypes.float8_e4m3fn, 7), "e5m2": (ml_dtypes.float8_e5m2, 14)}[fmt]
    v = np.moveaxis(np.asarray(x, np.float32).astype(ml_dtypes.bfloat16).astype(np.float64), axis, -1)
    blocks = v.reshape(v.shape[:-1] + (-1, 32))
    amax = np.abs(blocks).max(-1, keepdims=True)
    byte = np.maximum(np.where(amax > 0, np.frexp(amax)[1] - 1 + 127, 0) - down, 1)
    scale = np.exp2(byte - 127.0)
    codes = (blocks / scale).astype(np.float32).astype(dtype).astype(np.float64)
    return np.moveaxis((codes * scale).reshape(v.shape), -1, axis)


WIDE = False


def mx_kscale(k):
    if not WIDE:
        return np.ones(k)
    levels = np.array([10, -10, 5, -5, 0])
    if k % 512:
        return np.exp2(np.random.permutation(np.resize(levels, k // 32))).repeat(32)
    a = np.empty((k // 512, 16))
    for p in range(k // 512):
        a[p, :8] = np.random.permutation(np.resize(levels, 8))
        for g in range(8):
            far = levels[np.abs(levels - a[p, g]) >= 10]
            a[p, g + 8] = far[np.random.randint(len(far))]
    return np.exp2(a.ravel()).repeat(32)


def f64(x):
    return np.asarray(x).astype(np.float64)


def striped(idx):
    return np.tile(idx.reshape(-1, 16).T, (8, 1)).astype(np.uint16)


def unstriped(offs):
    return offs[:16].T.reshape(-1).astype(np.int64)


def gelu(v):
    return 0.5 * v * (1.0 + np.tanh(np.sqrt(2.0 / np.pi) * (v + 0.044715 * v**3)))


K, T, E, C, H, N = 512, 512, 12, 128, 512, 128
TOP = 3


def by_expert(wq, xq):
    return np.concatenate([wq[e].T @ xq[:, e * C:(e + 1) * C] for e in range(E)], axis=1)


def setup_inputs():
    n = np.random.standard_normal
    s = mx_kscale(K)[:, None]
    u = mx_kscale(H)
    deal = np.repeat(np.arange(E), C).reshape(TOP, T)[:, np.random.permutation(T)]
    deal = np.take_along_axis(deal, np.argsort(np.random.rand(TOP, T), axis=0), axis=0)
    for _ in range(8):
        s_, t_ = np.random.permutation(T).reshape(2, -1); r = np.random.randint(TOP, size=T // 2); x, y = deal[r, s_].copy(), deal[r, t_].copy()
        ok = ~((deal[:, s_] == y).any(0) | (deal[:, t_] == x).any(0)); deal[r[ok], s_[ok]] = y[ok]; deal[r[ok], t_[ok]] = x[ok]
    order = np.lexsort((np.random.rand(TOP * T), deal.reshape(-1)))
    slot_token = order % T; pos = np.empty(TOP * T, np.int64); pos[order] = np.arange(TOP * T); pos = pos.reshape(TOP, T)
    g = np.random.uniform(0.5, 1.5, (TOP, T)); g = g / g.sum(0)
    return {
        "xT": (n((K, T)) * s).astype(np.float32),
        "w1": (n((E, K, H)) / np.sqrt(K) / s[None]).astype(np.float32),
        "w3": (n((E, K, H)) / np.sqrt(K) / s[None] * u[None, None, :]).astype(np.float32),
        "w2": (n((E, H, N)) / np.sqrt(H) / u[None, :, None]).astype(np.float32),
        "gate": np.stack([np.tile(r, (N, 1)) for r in g]).astype(np.float32),
        "offs": striped(slot_token),
        "pos1": striped(pos[0]),
        "pos2": striped(pos[1]),
        "pos3": striped(pos[2]),
    }


def reference(xT, w1, w3, w2, gate, offs, pos1, pos2, pos3):
    idx = unstriped(offs)
    xq = mxq(f64(xT)[:, idx], 0, "e4m3")
    h = gelu(by_expert(mxq(f64(w1), 1, "e4m3"), xq))
    h = h * by_expert(mxq(f64(w3), 1, "e4m3"), xq)
    y = by_expert(mxq(f64(w2), 1, "e4m3"), mxq(h, 0, "e4m3"))
    return sum(f64(gate[r]) * y[:, unstriped(p)] for r, p in enumerate((pos1, pos2, pos3)))

@@ -1,0 +1,243 @@
+from contextlib import ExitStack
+
+import concourse.mybir as mybir
+
+K, T, E, C, H, N = 512, 512, 12, 128, 512, 128
+FLOPS = 2 * E * C * (2 * K * H + H * N)
+
+P = 128
+F32 = mybir.dt.float32
+BF16 = mybir.dt.bfloat16
+U32 = mybir.dt.uint32
+U16 = mybir.dt.uint16
+U8 = mybir.dt.uint8
+FP8X4 = mybir.dt.float8_e4m3fn_x4
+MULT = mybir.AluOpType.mult
+ADD = mybir.AluOpType.add
+GELU = mybir.ActivationFunctionType.Gelu_apprx_tanh
+
+PLAN = {'dma': [('3', 0, 2), ('1', 0, 1), ('1', 1, 1), ('3', 2, 2), ('1', 2, 1), ('1', 3, 1), ('3', 4, 2), ('1', 4, 1), ('1', 5, 1), ('p',), ('3', 6, 2), ('1', 6, 1), ('1', 7, 1), ('3', 8, 2), ('1', 8, 1), ('1', 9, 1), ('1', 10, 1), ('3', 10, 1), ('1', 11, 1), ('3', 11, 1), ('2', 0, 4), ('2', 4, 2), ('2', 6, 2), ('2', 8, 2), ('2', 10, 2), ('g', 0), ('g', 1), ('g', 2)], 'ops': [('C3', 0, 0), ('C3', 1, 4), ('C1', 0, 4), ('C1', 1, 0), ('Q', 0), ('A', 0), ('B', 0), ('Q', 1), ('A', 1), ('B', 1), ('M', 0), ('M', 1), ('H', 0), ('H', 1), ('C3', 2, 0), ('C3', 3, 4), ('C1', 2, 4), ('C1', 3, 0), ('Q', 2), ('A', 2), ('B', 2), ('Q', 3), ('A', 3), ('B', 3), ('M', 2), ('M', 3), ('H', 2), ('H', 3), ('C3', 4, 0), ('C3', 5, 4), ('C1', 4, 4), ('C1', 5, 0), ('Q', 4), ('A', 4), ('B', 4), ('Q', 5), ('A', 5), ('B', 5), ('M', 4), ('M', 5), ('H', 4), ('H', 5), ('C3', 6, 0), ('C3', 7, 4), ('C1', 6, 4), ('C1', 7, 0), ('Q', 6), ('A', 6), ('B', 6), ('Q', 7), ('A', 7), ('B', 7), ('M', 6), ('M', 7), ('H', 6), ('H', 7), ('C3', 8, 0), ('C3', 9, 4), ('C1', 8, 4), ('C1', 9, 0), ('Q', 8), ('A', 8), ('B', 8), ('Q', 9), ('A', 9), ('B', 9), ('M', 8), ('M', 9), ('H', 8), ('H', 9), ('C3', 10, 0), ('C3', 11, 0), ('C1', 10, 4), ('C1', 11, 4), ('Q1', 10), ('A', 10), ('Q3', 10), ('B', 10), ('Q1', 11), ('A', 11), ('Q3', 11), ('B', 11), ('M', 10), ('M', 11), ('H', 10), ('H', 11), ('W', 0, 4, 'VSVV'), ('WQ', 0), ('Y', 0), ('Y', 1), ('Y', 2), ('Y', 3), ('YO', 0, 4, 'S'), ('W', 4, 2, 'SS'), ('WQ', 4), ('Y', 4), ('Y', 5), ('YO', 4, 2, 'S'), ('W', 6, 2, 'VS'), ('WQ', 6), ('Y', 6), ('Y', 7), ('YO', 6, 2, 'S'), ('W', 8, 2, 'VV'), ('WQ', 8), ('Y', 8), ('Y', 9), ('YO', 8, 2, 'S'), ('W', 10, 2, 'SV'), ('WQ', 10), ('Y', 10), ('Y', 11), ('YO', 10, 2, 'S')]}
+GATHERS = ((0, 384), (384, 384), (768, 384), (1152, 384))
+
+
+def tile_moe_tk_glu_gelu_kernel(tc, xT, w1, w3, w2, gate, offs, pos1, pos2, pos3, out):
+    nc = tc.nc
+    with ExitStack() as ctx:
+        keep = ctx.enter_context(tc.tile_pool(name="keep", bufs=1))
+        raws = ctx.enter_context(tc.tile_pool(name="raws", bufs=6))
+        rounds = ctx.enter_context(tc.tile_pool(name="rounds", bufs=3))
+        codes_pool = ctx.enter_context(tc.tile_pool(name="codes", bufs=3))
+        h_pool = ctx.enter_context(tc.tile_pool(name="h_codes", bufs=12))
+        hidden = ctx.enter_context(tc.tile_pool(name="hidden", bufs=3))
+        psum = ctx.enter_context(tc.psum_pool(name="psum", bufs=3))
+        psum_y = ctx.enter_context(tc.psum_pool(name="psum_y", bufs=2))
+
+        offs_t = keep.tile([P, E * C // 16], U16, name="offs_t")
+        pos_t = [keep.tile([P, T // 16], U16, name=f"pos_t{r}") for r in range(3)]
+        x_raw = keep.tile([P, 4, T], F32, name="x_raw")
+        x_bf = keep.tile([P, T, 4], BF16, align_bytes=64, name="x_bf")
+        x_codes = keep.tile([P, T], U32, align_bytes=64, name="x_codes")
+        x_scales = keep.tile([P, T], U8, align_bytes=64, name="x_scales")
+        g_codes = keep.tile([P, E * C], U32, align_bytes=64, name="g_codes")
+        g_scales = keep.tile([P, E * C], U8, align_bytes=64, name="g_scales")
+        y_all = keep.tile([P, E * C], F32, name="y_all")
+        prods = keep.tile([P, 3, T], F32, name="prods")
+        part = keep.tile([P, T], F32, name="part")
+        result = keep.tile([P, T], F32, name="result")
+        warm = keep.tile([P, 8], F32, name="warm")
+
+        nc.gpsimd.memset(x_scales[:], 0)
+        nc.vector.memset(warm[:], 0.0)
+        nc.scalar.activation(warm[:], warm[:], GELU)
+
+        nc.sync.dma_start(x_raw[:], xT.rearrange("(p j) t -> p j t", j=4))
+        nc.sync.dma_start(offs_t[:], offs)
+
+        raw1 = {}
+        raw3 = {}
+        raw2 = {}
+
+        def load(where, source, first, count):
+            tile = raws.tile([P, count, 4, source.shape[2]], F32, name="raw", tag="raw")
+            nc.sync.dma_start(tile[:], source[first : first + count].rearrange("e (p j) i -> p e j i", j=4))
+            for i in range(count):
+                where[first + i] = tile[:, i]
+
+        def interleave_hidden(engine_copy, dst, src, t0, t1):
+            engine_copy(
+                dst.rearrange("p (t m j) -> p m j t", t=4, j=4)[:, :, :, t0:t1],
+                src.rearrange("p j (m t) -> p m j t", t=4)[:, :, :, t0:t1],
+            )
+
+        def interleave(engine_copy, dst, src):
+            engine_copy(
+                dst.rearrange("p (c i j) -> p c j i", i=4, j=4),
+                src.rearrange("p j (c i) -> p c j i", i=4),
+            )
+
+        vcopy, scopy = nc.vector.tensor_copy, nc.scalar.copy
+
+        for item in PLAN["dma"]:
+            kind = item[0]
+            if kind == "p":
+                for tile, source in zip(pos_t, (pos1, pos2, pos3)):
+                    nc.sync.dma_start(tile[:], source)
+            elif kind == "g":
+                if item[1] == 0:
+                    gate_t = []
+                tile = raws.tile([P, T], F32, name="gate_tile", tag="raw")
+                gate_t.append(tile)
+                nc.sync.dma_start(tile[:], gate[item[1]])
+            else:
+                load({"1": raw1, "2": raw2, "3": raw3}[kind], {"1": w1, "2": w2, "3": w3}[kind], item[1], item[2])
+
+        split = 320
+        xb = x_bf[:].rearrange("p t j -> p (t j)")
+        interleave(vcopy, xb[:, : 4 * split], x_raw[:, :, :split])
+        interleave(scopy, xb[:, 4 * split :], x_raw[:, :, split:])
+        nc.vector.quantize_mx(out=x_codes[:].bitcast(FP8X4), scales=x_scales[:], in_=xb)
+        for s, n in GATHERS:
+            lists = offs_t[:, s // 16 : (s + n) // 16]
+            nc.vector.tensor_copy(g_codes[:, s : s + n], x_codes[:].indirect(lists))
+            nc.vector.tensor_copy(g_scales[:, s : s + n], x_scales[:].indirect(lists))
+
+        q1 = {}
+        q3 = {}
+        q2 = {}
+        qh = {}
+        acc_a = {}
+        acc_b = {}
+        act = {}
+        hb = {}
+        y_banks = {}
+
+        def quantise(src, tag, pool=codes_pool):
+            width = src.shape[1] // 4
+            codes = pool.tile([P, width], U32, align_bytes=64, name=f"codes_{tag}")
+            scales = pool.tile([P, width], U8, align_bytes=64, name=f"scales_{tag}")
+            nc.vector.quantize_mx(out=codes[:].bitcast(FP8X4), scales=scales[:], in_=src)
+            return codes, scales
+
+        def product(bank, q, e):
+            codes, scales, at = q
+            for t in range(4):
+                cols = slice(at + t * P, at + (t + 1) * P)
+                nc.tensor.matmul_mx(
+                    out=bank[:, t, :],
+                    lhsT=codes[:, cols].bitcast(FP8X4),
+                    lhsT_scale=scales[:, cols],
+                    rhs=g_codes[:, e * C : (e + 1) * C].bitcast(FP8X4),
+                    rhs_scale=g_scales[:, e * C : (e + 1) * C],
+                    start=True,
+                    stop=True,
+                )
+
+        def stage_a(e):
+            acc_a[e] = psum.tile([P, 4, C], F32, name="acc_a")
+            product(acc_a[e], q1[e], e)
+
+        def stage_b(e):
+            acc_b[e] = psum.tile([P, 4, C], F32, name="acc_b")
+            product(acc_b[e], q3[e], e)
+
+        def stage_gelu(e):
+            act[e] = hidden.tile([P, C, 4], F32, name="act")
+            nc.scalar.activation(act[e][:], acc_a[e][:].rearrange("p t n -> p n t"), GELU)
+
+        def stage_mult(e):
+            hb[e] = hidden.tile([P, C * 4], BF16, align_bytes=64, name="hb")
+            nc.vector.tensor_tensor(
+                hb[e][:].rearrange("p (n t) -> p n t", t=4), act[e][:], acc_b[e][:].rearrange("p t n -> p n t"), MULT
+            )
+
+        def stage_h(e):
+            qh[e] = quantise(hb[e][:], "h", h_pool)
+
+        def stage_y(e):
+            h_codes, h_scales = qh[e]
+            g = e // 4
+            if e % 4 == 0:
+                y_banks[g] = psum_y.tile([P, 4, C], F32, name="y_bank")
+            codes, scales, at = q2[e]
+            nc.tensor.matmul_mx(
+                out=y_banks[g][:, e % 4, :],
+                lhsT=codes[:, at : at + N].bitcast(FP8X4),
+                lhsT_scale=scales[:, at : at + N],
+                rhs=h_codes[:].bitcast(FP8X4),
+                rhs_scale=h_scales[:],
+                start=True,
+                stop=True,
+            )
+
+        def y_out(first, count, copy):
+            copy(
+                y_all[:, first * C : (first + count) * C],
+                y_banks[first // 4][:, first % 4 : first % 4 + count, :].rearrange("p e n -> p (e n)"),
+            )
+
+        def copy_w2(engines, first):
+            bf = rounds.tile([P, len(engines) * 4 * N], BF16, align_bytes=64, name="bf2")
+            for i, engine in enumerate(engines):
+                interleave(engine, bf[:, i * 4 * N : (i + 1) * 4 * N], raw2[first + i])
+            return bf
+
+        def quantise_w2(src, first):
+            codes, scales = quantise(src, "w2")
+            for i in range(src.shape[1] // (4 * N)):
+                q2[first + i] = (codes, scales, i * N)
+
+        bf = {}
+        bf2 = {}
+
+        def get_bf(e):
+            if e not in bf:
+                bf[e] = rounds.tile([P, 8 * H], BF16, align_bytes=64, name="bf")
+            return bf[e]
+
+        for op in PLAN["ops"]:
+            k, e = op[0], op[1]
+            if k in ("C1", "C3"):
+                share = op[2]
+                dst = get_bf(e)[:, : 4 * H] if k == "C1" else get_bf(e)[:, 4 * H :]
+                src = (raw1 if k == "C1" else raw3)[e]
+                if share > 0:
+                    interleave_hidden(vcopy, dst, src, 0, share)
+                if share < 4:
+                    interleave_hidden(scopy, dst, src, share, 4)
+            elif k == "Q":
+                codes, scales = quantise(bf[e][:], "w")
+                q1[e] = (codes, scales, 0)
+                q3[e] = (codes, scales, H)
+            elif k == "Q1":
+                q1[e] = quantise(bf[e][:, : 4 * H], "w1") + (0,)
+            elif k == "Q3":
+                q3[e] = quantise(bf[e][:, 4 * H :], "w3") + (0,)
+            elif k == "A":
+                stage_a(e)
+                stage_gelu(e)
+            elif k == "B":
+                stage_b(e)
+            elif k == "M":
+                stage_mult(e)
+            elif k == "H":
+                stage_h(e)
+            elif k == "W":
+                bf2[e] = copy_w2([vcopy if c == "V" else scopy for c in op[3]], e)
+            elif k == "WQ":
+                quantise_w2(bf2[e][:], e)
+            elif k == "Y":
+                stage_y(e)
+            elif k == "YO":
+                y_out(e, op[2], vcopy if op[3] == "V" else scopy)
+
+        for r in range(2):
+            nc.vector.tensor_tensor(prods[:, r, :], y_all[:].indirect(pos_t[r][:]), gate_t[r][:], MULT)
+        halves = ((0, 256), (256, 256))
+        for i, (s, n) in enumerate(halves):
+            nc.vector.tensor_tensor(
+                prods[:, 2, s : s + n], y_all[:].indirect(pos_t[2][:, s // 16 : (s + n) // 16]), gate_t[2][:, s : s + n], MULT
+            )
+            if i == 0:
+                nc.vector.tensor_tensor(part[:], prods[:, 0, :], prods[:, 1, :], ADD)
+            nc.vector.tensor_tensor(result[:, s : s + n], part[:, s : s + n], prods[:, 2, s : s + n], ADD)
+            nc.sync.dma_start(out[:, s : s + n], result[:, s : s + n])

@@ -3,6 +3,7 @@ from contextlib import ExitStack
 import concourse.mybir as mybir
 
 K, T, E, C, H, N = 512, 512, 12, 128, 512, 128
+TOP = 3
 FLOPS = 2 * E * C * (2 * K * H + H * N)
 
 P = 128
@@ -16,100 +17,48 @@ MULT = mybir.AluOpType.mult
 ADD = mybir.AluOpType.add
 GELU = mybir.ActivationFunctionType.Gelu_apprx_tanh
 
-PLAN = {'dma': [('3', 0, 2), ('1', 0, 1), ('1', 1, 1), ('3', 2, 2), ('1', 2, 1), ('1', 3, 1), ('3', 4, 2), ('1', 4, 1), ('1', 5, 1), ('p',), ('3', 6, 2), ('1', 6, 1), ('1', 7, 1), ('3', 8, 2), ('1', 8, 1), ('1', 9, 1), ('1', 10, 1), ('3', 10, 1), ('1', 11, 1), ('3', 11, 1), ('2', 0, 4), ('2', 4, 2), ('2', 6, 2), ('2', 8, 2), ('2', 10, 2), ('g', 0), ('g', 1), ('g', 2)], 'ops': [('C3', 0, 0), ('C3', 1, 4), ('C1', 0, 4), ('C1', 1, 0), ('Q', 0), ('A', 0), ('B', 0), ('Q', 1), ('A', 1), ('B', 1), ('M', 0), ('M', 1), ('H', 0), ('H', 1), ('C3', 2, 0), ('C3', 3, 4), ('C1', 2, 4), ('C1', 3, 0), ('Q', 2), ('A', 2), ('B', 2), ('Q', 3), ('A', 3), ('B', 3), ('M', 2), ('M', 3), ('H', 2), ('H', 3), ('C3', 4, 0), ('C3', 5, 4), ('C1', 4, 4), ('C1', 5, 0), ('Q', 4), ('A', 4), ('B', 4), ('Q', 5), ('A', 5), ('B', 5), ('M', 4), ('M', 5), ('H', 4), ('H', 5), ('C3', 6, 0), ('C3', 7, 4), ('C1', 6, 4), ('C1', 7, 0), ('Q', 6), ('A', 6), ('B', 6), ('Q', 7), ('A', 7), ('B', 7), ('M', 6), ('M', 7), ('H', 6), ('H', 7), ('C3', 8, 0), ('C3', 9, 4), ('C1', 8, 4), ('C1', 9, 0), ('Q', 8), ('A', 8), ('B', 8), ('Q', 9), ('A', 9), ('B', 9), ('M', 8), ('M', 9), ('H', 8), ('H', 9), ('C3', 10, 0), ('C3', 11, 0), ('C1', 10, 4), ('C1', 11, 4), ('Q1', 10), ('A', 10), ('Q3', 10), ('B', 10), ('Q1', 11), ('A', 11), ('Q3', 11), ('B', 11), ('M', 10), ('M', 11), ('H', 10), ('H', 11), ('W', 0, 4, 'VSVV'), ('WQ', 0), ('Y', 0), ('Y', 1), ('Y', 2), ('Y', 3), ('YO', 0, 4, 'S'), ('W', 4, 2, 'SS'), ('WQ', 4), ('Y', 4), ('Y', 5), ('YO', 4, 2, 'S'), ('W', 6, 2, 'VS'), ('WQ', 6), ('Y', 6), ('Y', 7), ('YO', 6, 2, 'S'), ('W', 8, 2, 'VV'), ('WQ', 8), ('Y', 8), ('Y', 9), ('YO', 8, 2, 'S'), ('W', 10, 2, 'SV'), ('WQ', 10), ('Y', 10), ('Y', 11), ('YO', 10, 2, 'S')]}
-GATHERS = ((0, 384), (384, 384), (768, 384), (1152, 384))
+GATHER = 384
+X_SPLIT = 320
+LAST = E - 1
 
 
 def tile_moe_tk_glu_gelu_kernel(tc, xT, w1, w3, w2, gate, offs, pos1, pos2, pos3, out):
     nc = tc.nc
     with ExitStack() as ctx:
         keep = ctx.enter_context(tc.tile_pool(name="keep", bufs=1))
-        raws = ctx.enter_context(tc.tile_pool(name="raws", bufs=6))
+        raws = ctx.enter_context(tc.tile_pool(name="raws", bufs=14))
         rounds = ctx.enter_context(tc.tile_pool(name="rounds", bufs=3))
         codes_pool = ctx.enter_context(tc.tile_pool(name="codes", bufs=3))
-        h_pool = ctx.enter_context(tc.tile_pool(name="h_codes", bufs=12))
-        hidden = ctx.enter_context(tc.tile_pool(name="hidden", bufs=3))
+        h_pool = ctx.enter_context(tc.tile_pool(name="h_codes", bufs=E))
+        hidden = ctx.enter_context(tc.tile_pool(name="hidden", bufs=2))
         psum = ctx.enter_context(tc.psum_pool(name="psum", bufs=3))
         psum_y = ctx.enter_context(tc.psum_pool(name="psum_y", bufs=2))
 
         offs_t = keep.tile([P, E * C // 16], U16, name="offs_t")
-        pos_t = [keep.tile([P, T // 16], U16, name=f"pos_t{r}") for r in range(3)]
+        pos_t = [keep.tile([P, T // 16], U16, name=f"pos_t{r}") for r in range(TOP)]
         x_raw = keep.tile([P, 4, T], F32, name="x_raw")
-        x_bf = keep.tile([P, T, 4], BF16, align_bytes=64, name="x_bf")
+        x_bf = keep.tile([P, T * 4], BF16, align_bytes=64, name="x_bf")
         x_codes = keep.tile([P, T], U32, align_bytes=64, name="x_codes")
         x_scales = keep.tile([P, T], U8, align_bytes=64, name="x_scales")
         g_codes = keep.tile([P, E * C], U32, align_bytes=64, name="g_codes")
         g_scales = keep.tile([P, E * C], U8, align_bytes=64, name="g_scales")
         y_all = keep.tile([P, E * C], F32, name="y_all")
-        prods = keep.tile([P, 3, T], F32, name="prods")
+        prods = keep.tile([P, TOP, T], F32, name="prods")
         part = keep.tile([P, T], F32, name="part")
         result = keep.tile([P, T], F32, name="result")
-        warm = keep.tile([P, 8], F32, name="warm")
-
-        nc.gpsimd.memset(x_scales[:], 0)
-        nc.vector.memset(warm[:], 0.0)
-        nc.scalar.activation(warm[:], warm[:], GELU)
-
-        nc.sync.dma_start(x_raw[:], xT.rearrange("(p j) t -> p j t", j=4))
-        nc.sync.dma_start(offs_t[:], offs)
-
-        raw1 = {}
-        raw3 = {}
-        raw2 = {}
-
-        def load(where, source, first, count):
-            tile = raws.tile([P, count, 4, source.shape[2]], F32, name="raw", tag="raw")
-            nc.sync.dma_start(tile[:], source[first : first + count].rearrange("e (p j) i -> p e j i", j=4))
-            for i in range(count):
-                where[first + i] = tile[:, i]
-
-        def interleave_hidden(engine_copy, dst, src, t0, t1):
-            engine_copy(
-                dst.rearrange("p (t m j) -> p m j t", t=4, j=4)[:, :, :, t0:t1],
-                src.rearrange("p j (m t) -> p m j t", t=4)[:, :, :, t0:t1],
-            )
-
-        def interleave(engine_copy, dst, src):
-            engine_copy(
-                dst.rearrange("p (c i j) -> p c j i", i=4, j=4),
-                src.rearrange("p j (c i) -> p c j i", i=4),
-            )
 
         vcopy, scopy = nc.vector.tensor_copy, nc.scalar.copy
 
-        for item in PLAN["dma"]:
-            kind = item[0]
-            if kind == "p":
-                for tile, source in zip(pos_t, (pos1, pos2, pos3)):
-                    nc.sync.dma_start(tile[:], source)
-            elif kind == "g":
-                if item[1] == 0:
-                    gate_t = []
-                tile = raws.tile([P, T], F32, name="gate_tile", tag="raw")
-                gate_t.append(tile)
-                nc.sync.dma_start(tile[:], gate[item[1]])
-            else:
-                load({"1": raw1, "2": raw2, "3": raw3}[kind], {"1": w1, "2": w2, "3": w3}[kind], item[1], item[2])
+        def load(source, first, count=1):
+            tile = raws.tile([P, count, 4, source.shape[2]], F32, align_bytes=64, name="raw", tag="raw")
+            nc.sync.dma_start(tile[:], source[first : first + count].rearrange("e (p j) i -> p e j i", j=4))
+            return tile
 
-        split = 320
-        xb = x_bf[:].rearrange("p t j -> p (t j)")
-        interleave(vcopy, xb[:, : 4 * split], x_raw[:, :, :split])
-        interleave(scopy, xb[:, 4 * split :], x_raw[:, :, split:])
-        nc.vector.quantize_mx(out=x_codes[:].bitcast(FP8X4), scales=x_scales[:], in_=xb)
-        for s, n in GATHERS:
-            lists = offs_t[:, s // 16 : (s + n) // 16]
-            nc.vector.tensor_copy(g_codes[:, s : s + n], x_codes[:].indirect(lists))
-            nc.vector.tensor_copy(g_scales[:, s : s + n], x_scales[:].indirect(lists))
+        def interleave_hidden(copy, dst, src):
+            copy(dst.rearrange("p (t m j) -> p m j t", t=4, j=4), src.rearrange("p j (m t) -> p m j t", t=4))
 
-        q1 = {}
-        q3 = {}
-        q2 = {}
-        qh = {}
-        acc_a = {}
-        acc_b = {}
-        act = {}
-        hb = {}
-        y_banks = {}
+        def interleave(copy, dst, src):
+            copy(dst.rearrange("p (c i j) -> p c j i", i=4, j=4), src.rearrange("p j (c i) -> p c j i", i=4))
 
         def quantise(src, tag, pool=codes_pool):
             width = src.shape[1] // 4
@@ -118,8 +67,9 @@ def tile_moe_tk_glu_gelu_kernel(tc, xT, w1, w3, w2, gate, offs, pos1, pos2, pos3
             nc.vector.quantize_mx(out=codes[:].bitcast(FP8X4), scales=scales[:], in_=src)
             return codes, scales
 
-        def product(bank, q, e):
-            codes, scales, at = q
+        def first_layer(name, quantised, at, e):
+            codes, scales = quantised
+            bank = psum.tile([P, 4, C], F32, name=name)
             for t in range(4):
                 cols = slice(at + t * P, at + (t + 1) * P)
                 nc.tensor.matmul_mx(
@@ -131,113 +81,128 @@ def tile_moe_tk_glu_gelu_kernel(tc, xT, w1, w3, w2, gate, offs, pos1, pos2, pos3
                     start=True,
                     stop=True,
                 )
+            return bank
 
-        def stage_a(e):
-            acc_a[e] = psum.tile([P, 4, C], F32, name="acc_a")
-            product(acc_a[e], q1[e], e)
+        def gelu(act, bank):
+            nc.scalar.activation(act.rearrange("p (n t) -> p n t", t=4), bank[:].rearrange("p t n -> p n t"), GELU)
 
-        def stage_b(e):
-            acc_b[e] = psum.tile([P, 4, C], F32, name="acc_b")
-            product(acc_b[e], q3[e], e)
-
-        def stage_gelu(e):
-            act[e] = hidden.tile([P, C, 4], F32, name="act")
-            nc.scalar.activation(act[e][:], acc_a[e][:].rearrange("p t n -> p n t"), GELU)
-
-        def stage_mult(e):
-            hb[e] = hidden.tile([P, C * 4], BF16, align_bytes=64, name="hb")
+        def gated(hb, act, bank):
             nc.vector.tensor_tensor(
-                hb[e][:].rearrange("p (n t) -> p n t", t=4), act[e][:], acc_b[e][:].rearrange("p t n -> p n t"), MULT
+                hb.rearrange("p (n t) -> p n t", t=4),
+                act.rearrange("p (n t) -> p n t", t=4),
+                bank[:].rearrange("p t n -> p n t"),
+                MULT,
             )
 
-        def stage_h(e):
-            qh[e] = quantise(hb[e][:], "h", h_pool)
+        h_quantised = {}
 
-        def stage_y(e):
-            h_codes, h_scales = qh[e]
-            g = e // 4
-            if e % 4 == 0:
-                y_banks[g] = psum_y.tile([P, 4, C], F32, name="y_bank")
-            codes, scales, at = q2[e]
+        def second_layer(raw, first, count, copy):
+            rounded = rounds.tile([P, count * 4 * N], BF16, align_bytes=64, name="rounded_w2")
+            for i in range(count):
+                interleave(copy, rounded[:, i * 4 * N : (i + 1) * 4 * N], raw[:, i])
+            return rounded
+
+        def second_products(rounded, first, count):
+            codes, scales = quantise(rounded[:], "w2")
+            bank = psum_y.tile([P, count, C], F32, name="y_bank")
+            for i in range(count):
+                y_product(bank, codes, scales, i, first + i)
+            scopy(y_all[:, first * C : (first + count) * C], bank[:].rearrange("p e n -> p (e n)"))
+
+        def y_product(bank, codes, scales, i, e):
+            h_codes, h_scales = h_quantised[e]
             nc.tensor.matmul_mx(
-                out=y_banks[g][:, e % 4, :],
-                lhsT=codes[:, at : at + N].bitcast(FP8X4),
-                lhsT_scale=scales[:, at : at + N],
+                out=bank[:, i, :],
+                lhsT=codes[:, i * N : (i + 1) * N].bitcast(FP8X4),
+                lhsT_scale=scales[:, i * N : (i + 1) * N],
                 rhs=h_codes[:].bitcast(FP8X4),
                 rhs_scale=h_scales[:],
                 start=True,
                 stop=True,
             )
 
-        def y_out(first, count, copy):
-            copy(
-                y_all[:, first * C : (first + count) * C],
-                y_banks[first // 4][:, first % 4 : first % 4 + count, :].rearrange("p e n -> p (e n)"),
-            )
+        nc.gpsimd.memset(x_scales[:], 0)
+        nc.sync.dma_start(x_raw[:], xT.rearrange("(p j) t -> p j t", j=4))
+        nc.sync.dma_start(offs_t[:], offs)
 
-        def copy_w2(engines, first):
-            bf = rounds.tile([P, len(engines) * 4 * N], BF16, align_bytes=64, name="bf2")
-            for i, engine in enumerate(engines):
-                interleave(engine, bf[:, i * 4 * N : (i + 1) * 4 * N], raw2[first + i])
-            return bf
+        raw1, raw3, raw2 = {}, {}, {}
+        early = {3: 0, 6: 2}
+        before_last = ((4, 2, scopy), (6, 2, scopy))
+        late = ((10, 2, scopy), (8, 1, scopy), (9, 1, scopy))
+        raw1[0] = load(w1, 0)
+        for e in range(LAST):
+            raw1[e + 1] = load(w1, e + 1)
+            raw3[e] = load(w3, e)
+            if e in early:
+                raw2[early[e]] = load(w2, early[e], 2)
+            if e == 5:
+                for tile, source in zip(pos_t, (pos1, pos2, pos3)):
+                    nc.sync.dma_start(tile[:], source)
+        for first, count, copy in before_last:
+            raw2[first] = load(w2, first, count)
+        raw3[LAST] = load(w3, LAST)
+        for first, count, copy in late:
+            raw2[first] = load(w2, first, count)
+        gate_t = []
+        for r in range(TOP):
+            tile = raws.tile([P, T], F32, align_bytes=64, name="gate_tile", tag="raw")
+            nc.sync.dma_start(tile[:], gate[r])
+            gate_t.append(tile)
 
-        def quantise_w2(src, first):
-            codes, scales = quantise(src, "w2")
-            for i in range(src.shape[1] // (4 * N)):
-                q2[first + i] = (codes, scales, i * N)
+        interleave(vcopy, x_bf[:, : 4 * X_SPLIT], x_raw[:, :, :X_SPLIT])
+        interleave(scopy, x_bf[:, 4 * X_SPLIT :], x_raw[:, :, X_SPLIT:])
+        nc.vector.quantize_mx(out=x_codes[:].bitcast(FP8X4), scales=x_scales[:], in_=x_bf[:])
+        for s in range(0, E * C, GATHER):
+            lists = offs_t[:, s // 16 : (s + GATHER) // 16]
+            vcopy(g_codes[:, s : s + GATHER], x_codes[:].indirect(lists))
+            vcopy(g_scales[:, s : s + GATHER], x_scales[:].indirect(lists))
 
-        bf = {}
-        bf2 = {}
+        banks_a, banks_b, acts = {}, {}, {}
+        rounded = rounds.tile([P, 4 * H], BF16, align_bytes=64, name="rounded")
+        interleave_hidden(scopy, rounded[:], raw1[0][:, 0])
+        banks_a[0] = first_layer("bank_a", quantise(rounded[:], "w13"), 0, 0)
+        for e in range(LAST):
+            rounded = rounds.tile([P, 8 * H], BF16, align_bytes=64, name="rounded")
+            interleave_hidden(scopy, rounded[:, : 4 * H], raw1[e + 1][:, 0])
+            acts[e] = raw1[e + 1][:, 0, 0, :]
+            gelu(acts[e], banks_a[e])
+            interleave_hidden(vcopy if e > 0 else scopy, rounded[:, 4 * H :], raw3[e][:, 0])
+            if e > 0:
+                hb = raw3[e][:, 0, 0, : 2 * C].bitcast(BF16)
+                gated(hb, acts[e - 1], banks_b[e - 1])
+            quantised = quantise(rounded[:], "w13")
+            banks_b[e] = first_layer("bank_b", quantised, H, e)
+            banks_a[e + 1] = first_layer("bank_a", quantised, 0, e + 1)
+            if e > 0:
+                h_quantised[e - 1] = quantise(hb, "h", h_pool)
+            if e in early:
+                second_products(second_layer(raw2[early[e]], early[e], 2, scopy), early[e], 2)
 
-        def get_bf(e):
-            if e not in bf:
-                bf[e] = rounds.tile([P, 8 * H], BF16, align_bytes=64, name="bf")
-            return bf[e]
+        def hidden_codes(e):
+            hb = hidden.tile([P, 4 * C], BF16, align_bytes=64, name="hb")
+            gated(hb[:], acts[e], banks_b[e])
+            h_quantised[e] = quantise(hb[:], "h", h_pool)
 
-        for op in PLAN["ops"]:
-            k, e = op[0], op[1]
-            if k in ("C1", "C3"):
-                share = op[2]
-                dst = get_bf(e)[:, : 4 * H] if k == "C1" else get_bf(e)[:, 4 * H :]
-                src = (raw1 if k == "C1" else raw3)[e]
-                if share > 0:
-                    interleave_hidden(vcopy, dst, src, 0, share)
-                if share < 4:
-                    interleave_hidden(scopy, dst, src, share, 4)
-            elif k == "Q":
-                codes, scales = quantise(bf[e][:], "w")
-                q1[e] = (codes, scales, 0)
-                q3[e] = (codes, scales, H)
-            elif k == "Q1":
-                q1[e] = quantise(bf[e][:, : 4 * H], "w1") + (0,)
-            elif k == "Q3":
-                q3[e] = quantise(bf[e][:, 4 * H :], "w3") + (0,)
-            elif k == "A":
-                stage_a(e)
-                stage_gelu(e)
-            elif k == "B":
-                stage_b(e)
-            elif k == "M":
-                stage_mult(e)
-            elif k == "H":
-                stage_h(e)
-            elif k == "W":
-                bf2[e] = copy_w2([vcopy if c == "V" else scopy for c in op[3]], e)
-            elif k == "WQ":
-                quantise_w2(bf2[e][:], e)
-            elif k == "Y":
-                stage_y(e)
-            elif k == "YO":
-                y_out(e, op[2], vcopy if op[3] == "V" else scopy)
+        hidden_codes(LAST - 1)
+        acts[LAST] = hidden.tile([P, 4 * C], F32, name="act")[:]
+        gelu(acts[LAST], banks_a[LAST])
+        for first, count, copy in before_last:
+            second_products(second_layer(raw2[first], first, count, copy), first, count)
+
+        rounded = rounds.tile([P, 4 * H], BF16, align_bytes=64, name="rounded")
+        interleave_hidden(vcopy, rounded[:], raw3[LAST][:, 0])
+        banks_b[LAST] = first_layer("bank_b", quantise(rounded[:], "w13"), 0, LAST)
+        hidden_codes(LAST)
+        for first, count, copy in late:
+            second_products(second_layer(raw2[first], first, count, copy), first, count)
 
         for r in range(2):
             nc.vector.tensor_tensor(prods[:, r, :], y_all[:].indirect(pos_t[r][:]), gate_t[r][:], MULT)
-        halves = ((0, 256), (256, 256))
-        for i, (s, n) in enumerate(halves):
-            nc.vector.tensor_tensor(
-                prods[:, 2, s : s + n], y_all[:].indirect(pos_t[2][:, s // 16 : (s + n) // 16]), gate_t[2][:, s : s + n], MULT
-            )
-            if i == 0:
+        for s in range(0, T, T // 2):
+            cols = slice(s, s + T // 2)
+            lists = pos_t[2][:, s // 16 : (s + T // 2) // 16]
+            nc.vector.tensor_tensor(prods[:, 2, cols], y_all[:].indirect(lists), gate_t[2][:, cols], MULT)
+            if s == 0:
                 nc.vector.tensor_tensor(part[:], prods[:, 0, :], prods[:, 1, :], ADD)
-            nc.vector.tensor_tensor(result[:, s : s + n], part[:, s : s + n], prods[:, 2, s : s + n], ADD)
-            nc.sync.dma_start(out[:, s : s + n], result[:, s : s + n])
+            nc.vector.tensor_tensor(result[:, cols], part[:, cols], prods[:, 2, cols], ADD)
+            nc.sync.dma_start(out[:, cols], result[:, cols])

@@ -20,6 +20,7 @@ GELU = mybir.ActivationFunctionType.Gelu_apprx_tanh
 GATHER = 384
 X_SPLIT = 320
 LAST = E - 1
+SKEWED = 9
 
 
 def tile_moe_tk_glu_gelu_kernel(tc, xT, w1, w3, w2, gate, offs, pos1, pos2, pos3, out):
@@ -28,11 +29,12 @@ def tile_moe_tk_glu_gelu_kernel(tc, xT, w1, w3, w2, gate, offs, pos1, pos2, pos3
         keep = ctx.enter_context(tc.tile_pool(name="keep", bufs=1))
         raws = ctx.enter_context(tc.tile_pool(name="raws", bufs=14))
         rounds = ctx.enter_context(tc.tile_pool(name="rounds", bufs=3))
-        codes_pool = ctx.enter_context(tc.tile_pool(name="codes", bufs=3))
+        codes_pool = ctx.enter_context(tc.tile_pool(name="codes", bufs=4))
         h_pool = ctx.enter_context(tc.tile_pool(name="h_codes", bufs=E))
+        slots = ctx.enter_context(tc.tile_pool(name="slots", bufs=2))
         hidden = ctx.enter_context(tc.tile_pool(name="hidden", bufs=2))
-        psum = ctx.enter_context(tc.psum_pool(name="psum", bufs=3))
-        psum_y = ctx.enter_context(tc.psum_pool(name="psum_y", bufs=2))
+        single = ctx.enter_context(tc.tile_pool(name="single", bufs=1))
+        psum = ctx.enter_context(tc.psum_pool(name="psum", bufs=2))
 
         offs_t = keep.tile([P, E * C // 16], U16, name="offs_t")
         pos_t = [keep.tile([P, T // 16], U16, name=f"pos_t{r}") for r in range(TOP)]
@@ -40,8 +42,6 @@ def tile_moe_tk_glu_gelu_kernel(tc, xT, w1, w3, w2, gate, offs, pos1, pos2, pos3
         x_bf = keep.tile([P, T * 4], BF16, align_bytes=64, name="x_bf")
         x_codes = keep.tile([P, T], U32, align_bytes=64, name="x_codes")
         x_scales = keep.tile([P, T], U8, align_bytes=64, name="x_scales")
-        g_codes = keep.tile([P, E * C], U32, align_bytes=64, name="g_codes")
-        g_scales = keep.tile([P, E * C], U8, align_bytes=64, name="g_scales")
         y_all = keep.tile([P, E * C], F32, name="y_all")
         prods = keep.tile([P, TOP, T], F32, name="prods")
         part = keep.tile([P, T], F32, name="part")
@@ -54,33 +54,50 @@ def tile_moe_tk_glu_gelu_kernel(tc, xT, w1, w3, w2, gate, offs, pos1, pos2, pos3
             nc.sync.dma_start(tile[:], source[first : first + count].rearrange("e (p j) i -> p e j i", j=4))
             return tile
 
-        def interleave_hidden(copy, dst, src):
-            copy(dst.rearrange("p (t m j) -> p m j t", t=4, j=4), src.rearrange("p j (m t) -> p m j t", t=4))
+        def interleave_hidden(copy, dst, src, part=slice(0, P)):
+            copy(
+                dst.rearrange("p (t m j) -> p m j t", t=4, j=4)[:, part],
+                src.rearrange("p j (m t) -> p m j t", t=4)[:, part],
+            )
 
         def interleave(copy, dst, src):
             copy(dst.rearrange("p (c i j) -> p c j i", i=4, j=4), src.rearrange("p j (c i) -> p c j i", i=4))
 
-        def quantise(src, tag, pool=codes_pool):
+        def quantise(src, tag, pool=codes_pool, codes=None):
             width = src.shape[1] // 4
-            codes = pool.tile([P, width], U32, align_bytes=64, name=f"codes_{tag}")
+            if codes is None:
+                codes = pool.tile([P, width], U32, align_bytes=64, name=f"codes_{tag}")
             scales = pool.tile([P, width], U8, align_bytes=64, name=f"scales_{tag}")
             nc.vector.quantize_mx(out=codes[:].bitcast(FP8X4), scales=scales[:], in_=src)
             return codes, scales
 
-        def first_layer(name, quantised, at, e):
-            codes, scales = quantised
-            bank = psum.tile([P, 4, C], F32, name=name)
+        def product(bank, stationary, at, moving, start):
+            nc.tensor.matmul_mx(
+                out=bank,
+                lhsT=stationary[0][:, at : at + P].bitcast(FP8X4),
+                lhsT_scale=stationary[1][:, at : at + P],
+                rhs=moving[0][:, start : start + C].bitcast(FP8X4),
+                rhs_scale=moving[1][:, start : start + C],
+                start=True,
+                stop=True,
+            )
+
+        gathered = {}
+
+        def gather_tokens(piece):
+            lists = offs_t[:, piece * GATHER // 16 : (piece + 1) * GATHER // 16]
+            g_codes = slots.tile([P, GATHER], U32, align_bytes=64, name="g_codes")
+            g_scales = slots.tile([P, GATHER], U8, align_bytes=64, name="g_scales")
+            vcopy(g_codes[:], x_codes[:].indirect(lists))
+            vcopy(g_scales[:], x_scales[:].indirect(lists))
+            return g_codes, g_scales
+
+        def first_layer(bank, quantised, at, e):
+            piece, place = divmod(e * C, GATHER)
+            if piece not in gathered:
+                gathered[piece] = gather_tokens(piece)
             for t in range(4):
-                cols = slice(at + t * P, at + (t + 1) * P)
-                nc.tensor.matmul_mx(
-                    out=bank[:, t, :],
-                    lhsT=codes[:, cols].bitcast(FP8X4),
-                    lhsT_scale=scales[:, cols],
-                    rhs=g_codes[:, e * C : (e + 1) * C].bitcast(FP8X4),
-                    rhs_scale=g_scales[:, e * C : (e + 1) * C],
-                    start=True,
-                    stop=True,
-                )
+                product(bank[:, t, :], quantised, at + t * P, gathered[piece], place)
             return bank
 
         def gelu(act, bank):
@@ -94,55 +111,42 @@ def tile_moe_tk_glu_gelu_kernel(tc, xT, w1, w3, w2, gate, offs, pos1, pos2, pos3
                 MULT,
             )
 
+        raw1, raw3, raw2 = {}, {}, {}
         h_quantised = {}
 
-        def second_layer(raw, first, count, copy):
-            rounded = rounds.tile([P, count * 4 * N], BF16, align_bytes=64, name="rounded_w2")
+        def load_w2(first, count):
+            tile = load(w2, first, count)
             for i in range(count):
-                interleave(copy, rounded[:, i * 4 * N : (i + 1) * 4 * N], raw[:, i])
-            return rounded
+                raw2[first + i] = tile[:, i]
 
-        def second_products(rounded, first, count):
-            codes, scales = quantise(rounded[:], "w2")
-            bank = psum_y.tile([P, count, C], F32, name="y_bank")
+        def round_w2(rounded, first, experts, copy=scopy):
+            for e in experts:
+                at = (e - first) * 4 * N
+                interleave(copy, rounded[:, at : at + 4 * N], raw2[e])
+
+        def second_layer(bank, quantised, first, count, copy=scopy):
             for i in range(count):
-                y_product(bank, codes, scales, i, first + i)
-            scopy(y_all[:, first * C : (first + count) * C], bank[:].rearrange("p e n -> p (e n)"))
-
-        def y_product(bank, codes, scales, i, e):
-            h_codes, h_scales = h_quantised[e]
-            nc.tensor.matmul_mx(
-                out=bank[:, i, :],
-                lhsT=codes[:, i * N : (i + 1) * N].bitcast(FP8X4),
-                lhsT_scale=scales[:, i * N : (i + 1) * N],
-                rhs=h_codes[:].bitcast(FP8X4),
-                rhs_scale=h_scales[:],
-                start=True,
-                stop=True,
-            )
+                product(bank[:, i, :], quantised, i * N, h_quantised[first + i], 0)
+            copy(y_all[:, first * C : (first + count) * C], bank[:].rearrange("p e n -> p (e n)"))
 
         nc.gpsimd.memset(x_scales[:], 0)
         nc.sync.dma_start(x_raw[:], xT.rearrange("(p j) t -> p j t", j=4))
         nc.sync.dma_start(offs_t[:], offs)
 
-        raw1, raw3, raw2 = {}, {}, {}
-        early = {3: 0, 6: 2}
-        before_last = ((4, 2, scopy), (6, 2, scopy))
-        late = ((10, 2, scopy), (8, 1, scopy), (9, 1, scopy))
         raw1[0] = load(w1, 0)
         for e in range(LAST):
             raw1[e + 1] = load(w1, e + 1)
             raw3[e] = load(w3, e)
-            if e in early:
-                raw2[early[e]] = load(w2, early[e], 2)
+            if e == SKEWED:
+                load_w2(0, 2)
             if e == 5:
                 for tile, source in zip(pos_t, (pos1, pos2, pos3)):
                     nc.sync.dma_start(tile[:], source)
-        for first, count, copy in before_last:
-            raw2[first] = load(w2, first, count)
+        for first in (2, 4, 6):
+            load_w2(first, 2)
         raw3[LAST] = load(w3, LAST)
-        for first, count, copy in late:
-            raw2[first] = load(w2, first, count)
+        for e in (10, 11, 8, 9):
+            load_w2(e, 1)
         gate_t = []
         for r in range(TOP):
             tile = raws.tile([P, T], F32, align_bytes=64, name="gate_tile", tag="raw")
@@ -152,49 +156,66 @@ def tile_moe_tk_glu_gelu_kernel(tc, xT, w1, w3, w2, gate, offs, pos1, pos2, pos3
         interleave(vcopy, x_bf[:, : 4 * X_SPLIT], x_raw[:, :, :X_SPLIT])
         interleave(scopy, x_bf[:, 4 * X_SPLIT :], x_raw[:, :, X_SPLIT:])
         nc.vector.quantize_mx(out=x_codes[:].bitcast(FP8X4), scales=x_scales[:], in_=x_bf[:])
-        for s in range(0, E * C, GATHER):
-            lists = offs_t[:, s // 16 : (s + GATHER) // 16]
-            vcopy(g_codes[:, s : s + GATHER], x_codes[:].indirect(lists))
-            vcopy(g_scales[:, s : s + GATHER], x_scales[:].indirect(lists))
 
         banks_a, banks_b, acts = {}, {}, {}
         rounded = rounds.tile([P, 4 * H], BF16, align_bytes=64, name="rounded")
         interleave_hidden(scopy, rounded[:], raw1[0][:, 0])
-        banks_a[0] = first_layer("bank_a", quantise(rounded[:], "w13"), 0, 0)
+        banks_a[0] = first_layer(psum.tile([P, 4, C], F32, name="bank_a"), quantise(rounded[:], "w13"), 0, 0)
         for e in range(LAST):
             rounded = rounds.tile([P, 8 * H], BF16, align_bytes=64, name="rounded")
             interleave_hidden(scopy, rounded[:, : 4 * H], raw1[e + 1][:, 0])
             acts[e] = raw1[e + 1][:, 0, 0, :]
             gelu(acts[e], banks_a[e])
-            interleave_hidden(vcopy if e > 0 else scopy, rounded[:, 4 * H :], raw3[e][:, 0])
-            if e > 0:
+            interleave_hidden(vcopy, rounded[:, 4 * H :], raw3[e][:, 0])
+            if 0 < e <= SKEWED:
                 hb = raw3[e][:, 0, 0, : 2 * C].bitcast(BF16)
                 gated(hb, acts[e - 1], banks_b[e - 1])
             quantised = quantise(rounded[:], "w13")
-            banks_b[e] = first_layer("bank_b", quantised, H, e)
-            banks_a[e + 1] = first_layer("bank_a", quantised, 0, e + 1)
-            if e > 0:
+            banks_b[e] = first_layer(psum.tile([P, 4, C], F32, name="bank_b"), quantised, H, e)
+            banks_a[e + 1] = first_layer(psum.tile([P, 4, C], F32, name="bank_a"), quantised, 0, e + 1)
+            if 0 < e <= SKEWED:
                 h_quantised[e - 1] = quantise(hb, "h", h_pool)
-            if e in early:
-                second_products(second_layer(raw2[early[e]], early[e], 2, scopy), early[e], 2)
+            if e >= SKEWED:
+                own = hidden.tile([P, 4 * C], BF16, align_bytes=64, name="hb")
+                gated(own[:], acts[e], banks_b[e])
+                h_quantised[e] = quantise(own[:], "h", h_pool)
+            if e == SKEWED:
+                rounded = rounds.tile([P, 2 * 4 * N], BF16, align_bytes=64, name="rounded_w2")
+                round_w2(rounded, 0, (0, 1))
+                second_layer(psum.tile([P, 2, C], F32, name="bank_y"), quantise(rounded[:], "w2"), 0, 2)
 
-        def hidden_codes(e):
-            hb = hidden.tile([P, 4 * C], BF16, align_bytes=64, name="hb")
-            gated(hb[:], acts[e], banks_b[e])
-            h_quantised[e] = quantise(hb[:], "h", h_pool)
-
-        hidden_codes(LAST - 1)
-        acts[LAST] = hidden.tile([P, 4 * C], F32, name="act")[:]
+        rounded = rounds.tile([P, 4 * 4 * N], BF16, align_bytes=64, name="rounded_w2")
+        round_w2(rounded, 2, range(2, 6))
+        w2_a = quantise(rounded[:], "w2")
+        rounded = rounds.tile([P, 2 * 4 * N], BF16, align_bytes=64, name="rounded_w2")
+        round_w2(rounded, 6, (6, 7))
+        w2_b = quantise(rounded[:], "w2")
+        acts[LAST] = raw2[7].rearrange("p j n -> p (j n)")
         gelu(acts[LAST], banks_a[LAST])
-        for first, count, copy in before_last:
-            second_products(second_layer(raw2[first], first, count, copy), first, count)
+        second_layer(psum.tile([P, 4, C], F32, name="bank_y"), w2_a, 2, 4)
 
         rounded = rounds.tile([P, 4 * H], BF16, align_bytes=64, name="rounded")
         interleave_hidden(vcopy, rounded[:], raw3[LAST][:, 0])
-        banks_b[LAST] = first_layer("bank_b", quantise(rounded[:], "w13"), 0, LAST)
-        hidden_codes(LAST)
-        for first, count, copy in late:
-            second_products(second_layer(raw2[first], first, count, copy), first, count)
+        bank = psum.tile([P, 4, C], F32, name="bank_b")
+        banks_b[LAST] = first_layer(bank, quantise(rounded[:], "w13"), 0, LAST)
+
+        rounded = single.tile([P, 2 * 4 * N], BF16, align_bytes=64, name="rounded_c", tag="before_gated")
+        round_w2(rounded, 10, (10, 11))
+        w2_d = quantise(rounded[:], "w2")
+        hb = single.tile([P, 4 * C], BF16, align_bytes=64, name="hb_last", tag="before_gated")
+        gated(hb[:], acts[LAST], banks_b[LAST])
+        rounded = single.tile([P, 2 * 4 * N], BF16, align_bytes=64, name="rounded_d", tag="before_h")
+        round_w2(rounded, 8, (8, 9))
+        w2_c = quantise(rounded[:], "w2")
+        codes = single.tile([P, C], U32, align_bytes=64, name="codes_last", tag="before_h")
+        h_quantised[LAST] = quantise(hb[:], "h", h_pool, codes)
+        bank = psum.tile([P, 4, C], F32, name="bank_y")
+        for i in range(2):
+            product(bank[:, i, :], w2_b, i * N, h_quantised[6 + i], 0)
+        for i in range(2):
+            product(bank[:, 2 + i, :], w2_c, i * N, h_quantised[8 + i], 0)
+        scopy(y_all[:, 6 * C : 10 * C], bank[:].rearrange("p e n -> p (e n)"))
+        second_layer(psum.tile([P, 2, C], F32, name="bank_y"), w2_d, 10, 2, vcopy)
 
         for r in range(2):
             nc.vector.tensor_tensor(prods[:, r, :], y_all[:].indirect(pos_t[r][:]), gate_t[r][:], MULT)

@@ -21,15 +21,17 @@ GATHER = 384
 X_SPLIT = 320
 LAST = E - 1
 SKEWED = 9
+PAIRED = 8
 
 
 def tile_moe_tk_glu_gelu_kernel(tc, xT, w1, w3, w2, gate, offs, pos1, pos2, pos3, out):
     nc = tc.nc
     with ExitStack() as ctx:
         keep = ctx.enter_context(tc.tile_pool(name="keep", bufs=1))
-        raws = ctx.enter_context(tc.tile_pool(name="raws", bufs=14))
+        raws = ctx.enter_context(tc.tile_pool(name="raws", bufs=10))
         rounds = ctx.enter_context(tc.tile_pool(name="rounds", bufs=3))
-        codes_pool = ctx.enter_context(tc.tile_pool(name="codes", bufs=4))
+        codes_pool = ctx.enter_context(tc.tile_pool(name="codes", bufs=2))
+        w2_pool = ctx.enter_context(tc.tile_pool(name="w2_codes", bufs=4))
         h_pool = ctx.enter_context(tc.tile_pool(name="h_codes", bufs=E))
         slots = ctx.enter_context(tc.tile_pool(name="slots", bufs=2))
         hidden = ctx.enter_context(tc.tile_pool(name="hidden", bufs=2))
@@ -38,14 +40,11 @@ def tile_moe_tk_glu_gelu_kernel(tc, xT, w1, w3, w2, gate, offs, pos1, pos2, pos3
 
         offs_t = keep.tile([P, E * C // 16], U16, name="offs_t")
         pos_t = [keep.tile([P, T // 16], U16, name=f"pos_t{r}") for r in range(TOP)]
-        x_raw = keep.tile([P, 4, T], F32, name="x_raw")
-        x_bf = keep.tile([P, T * 4], BF16, align_bytes=64, name="x_bf")
+        x_raw = raws.tile([P, 4, T], F32, align_bytes=64, name="x_raw", tag="raw")
+        x_bf = rounds.tile([P, T * 4], BF16, align_bytes=64, name="x_bf", tag="rounded")
         x_codes = keep.tile([P, T], U32, align_bytes=64, name="x_codes")
         x_scales = keep.tile([P, T], U8, align_bytes=64, name="x_scales")
         y_all = keep.tile([P, E * C], F32, name="y_all")
-        prods = keep.tile([P, TOP, T], F32, name="prods")
-        part = keep.tile([P, T], F32, name="part")
-        result = keep.tile([P, T], F32, name="result")
 
         vcopy, scopy = nc.vector.tensor_copy, nc.scalar.copy
 
@@ -133,10 +132,17 @@ def tile_moe_tk_glu_gelu_kernel(tc, xT, w1, w3, w2, gate, offs, pos1, pos2, pos3
         nc.sync.dma_start(x_raw[:], xT.rearrange("(p j) t -> p j t", j=4))
         nc.sync.dma_start(offs_t[:], offs)
 
-        raw1[0] = load(w1, 0)
+        def load_first(where, source, first, count):
+            tile = load(source, first, count)
+            for i in range(count):
+                where[first + i] = tile[:, i]
+
+        load_first(raw1, w1, 0, 1)
         for e in range(LAST):
-            raw1[e + 1] = load(w1, e + 1)
-            raw3[e] = load(w3, e)
+            if e not in raw3:
+                count = 2 if e < PAIRED else 1
+                load_first(raw1, w1, e + 1, count)
+                load_first(raw3, w3, e, count)
             if e == SKEWED:
                 load_w2(0, 2)
             if e == 5:
@@ -144,14 +150,11 @@ def tile_moe_tk_glu_gelu_kernel(tc, xT, w1, w3, w2, gate, offs, pos1, pos2, pos3
                     nc.sync.dma_start(tile[:], source)
         for first in (2, 4, 6):
             load_w2(first, 2)
-        raw3[LAST] = load(w3, LAST)
+        load_first(raw3, w3, LAST, 1)
         for e in (10, 11, 8, 9):
             load_w2(e, 1)
-        gate_t = []
-        for r in range(TOP):
-            tile = raws.tile([P, T], F32, align_bytes=64, name="gate_tile", tag="raw")
-            nc.sync.dma_start(tile[:], gate[r])
-            gate_t.append(tile)
+        gate_t = raws.tile([P, TOP, T], F32, align_bytes=64, name="gate_t", tag="raw")
+        nc.sync.dma_start(gate_t[:], gate.rearrange("r p t -> p r t"))
 
         interleave(vcopy, x_bf[:, : 4 * X_SPLIT], x_raw[:, :, :X_SPLIT])
         interleave(scopy, x_bf[:, 4 * X_SPLIT :], x_raw[:, :, X_SPLIT:])
@@ -159,16 +162,16 @@ def tile_moe_tk_glu_gelu_kernel(tc, xT, w1, w3, w2, gate, offs, pos1, pos2, pos3
 
         banks_a, banks_b, acts = {}, {}, {}
         rounded = rounds.tile([P, 4 * H], BF16, align_bytes=64, name="rounded")
-        interleave_hidden(scopy, rounded[:], raw1[0][:, 0])
+        interleave_hidden(scopy, rounded[:], raw1[0])
         banks_a[0] = first_layer(psum.tile([P, 4, C], F32, name="bank_a"), quantise(rounded[:], "w13"), 0, 0)
         for e in range(LAST):
             rounded = rounds.tile([P, 8 * H], BF16, align_bytes=64, name="rounded")
-            interleave_hidden(scopy, rounded[:, : 4 * H], raw1[e + 1][:, 0])
-            acts[e] = raw1[e + 1][:, 0, 0, :]
+            interleave_hidden(scopy, rounded[:, : 4 * H], raw1[e + 1])
+            acts[e] = raw1[e + 1][:, 0, :]
             gelu(acts[e], banks_a[e])
-            interleave_hidden(vcopy, rounded[:, 4 * H :], raw3[e][:, 0])
+            interleave_hidden(vcopy, rounded[:, 4 * H :], raw3[e])
             if 0 < e <= SKEWED:
-                hb = raw3[e][:, 0, 0, : 2 * C].bitcast(BF16)
+                hb = raw3[e][:, 0, : 2 * C].bitcast(BF16)
                 gated(hb, acts[e - 1], banks_b[e - 1])
             quantised = quantise(rounded[:], "w13")
             banks_b[e] = first_layer(psum.tile([P, 4, C], F32, name="bank_b"), quantised, H, e)
@@ -180,33 +183,33 @@ def tile_moe_tk_glu_gelu_kernel(tc, xT, w1, w3, w2, gate, offs, pos1, pos2, pos3
                 gated(own[:], acts[e], banks_b[e])
                 h_quantised[e] = quantise(own[:], "h", h_pool)
             if e == SKEWED:
-                rounded = rounds.tile([P, 2 * 4 * N], BF16, align_bytes=64, name="rounded_w2")
+                rounded = hidden.tile([P, 2 * 4 * N], BF16, align_bytes=64, name="rounded_w2")
                 round_w2(rounded, 0, (0, 1))
-                second_layer(psum.tile([P, 2, C], F32, name="bank_y"), quantise(rounded[:], "w2"), 0, 2)
+                second_layer(psum.tile([P, 2, C], F32, name="bank_y"), quantise(rounded[:], "w2", w2_pool), 0, 2)
 
-        rounded = rounds.tile([P, 4 * 4 * N], BF16, align_bytes=64, name="rounded_w2")
+        rounded = hidden.tile([P, 4 * 4 * N], BF16, align_bytes=64, name="rounded_w2")
         round_w2(rounded, 2, range(2, 6))
-        w2_a = quantise(rounded[:], "w2")
-        rounded = rounds.tile([P, 2 * 4 * N], BF16, align_bytes=64, name="rounded_w2")
+        w2_a = quantise(rounded[:], "w2", w2_pool)
+        rounded = hidden.tile([P, 2 * 4 * N], BF16, align_bytes=64, name="rounded_w2")
         round_w2(rounded, 6, (6, 7))
-        w2_b = quantise(rounded[:], "w2")
+        w2_b = quantise(rounded[:], "w2", w2_pool)
         acts[LAST] = raw2[7].rearrange("p j n -> p (j n)")
         gelu(acts[LAST], banks_a[LAST])
         second_layer(psum.tile([P, 4, C], F32, name="bank_y"), w2_a, 2, 4)
 
         rounded = rounds.tile([P, 4 * H], BF16, align_bytes=64, name="rounded")
-        interleave_hidden(vcopy, rounded[:], raw3[LAST][:, 0])
+        interleave_hidden(vcopy, rounded[:], raw3[LAST])
         bank = psum.tile([P, 4, C], F32, name="bank_b")
         banks_b[LAST] = first_layer(bank, quantise(rounded[:], "w13"), 0, LAST)
 
         rounded = single.tile([P, 2 * 4 * N], BF16, align_bytes=64, name="rounded_c", tag="before_gated")
         round_w2(rounded, 10, (10, 11))
-        w2_d = quantise(rounded[:], "w2")
+        w2_d = quantise(rounded[:], "w2", w2_pool)
         hb = single.tile([P, 4 * C], BF16, align_bytes=64, name="hb_last", tag="before_gated")
         gated(hb[:], acts[LAST], banks_b[LAST])
         rounded = single.tile([P, 2 * 4 * N], BF16, align_bytes=64, name="rounded_d", tag="before_h")
         round_w2(rounded, 8, (8, 9))
-        w2_c = quantise(rounded[:], "w2")
+        w2_c = quantise(rounded[:], "w2", w2_pool)
         codes = single.tile([P, C], U32, align_bytes=64, name="codes_last", tag="before_h")
         h_quantised[LAST] = quantise(hb[:], "h", h_pool, codes)
         bank = psum.tile([P, 4, C], F32, name="bank_y")
@@ -217,13 +220,16 @@ def tile_moe_tk_glu_gelu_kernel(tc, xT, w1, w3, w2, gate, offs, pos1, pos2, pos3
         scopy(y_all[:, 6 * C : 10 * C], bank[:].rearrange("p e n -> p (e n)"))
         second_layer(psum.tile([P, 2, C], F32, name="bank_y"), w2_d, 10, 2, vcopy)
 
+        prods = raws.tile([P, TOP, T], F32, align_bytes=64, name="prods", tag="raw")
+        sums = raws.tile([P, 2, T], F32, align_bytes=64, name="sums", tag="raw")
+        part, result = sums[:, 0, :], sums[:, 1, :]
         for r in range(2):
-            nc.vector.tensor_tensor(prods[:, r, :], y_all[:].indirect(pos_t[r][:]), gate_t[r][:], MULT)
+            nc.vector.tensor_tensor(prods[:, r, :], y_all[:].indirect(pos_t[r][:]), gate_t[:, r, :], MULT)
         for s in range(0, T, T // 2):
             cols = slice(s, s + T // 2)
             lists = pos_t[2][:, s // 16 : (s + T // 2) // 16]
-            nc.vector.tensor_tensor(prods[:, 2, cols], y_all[:].indirect(lists), gate_t[2][:, cols], MULT)
+            nc.vector.tensor_tensor(prods[:, 2, cols], y_all[:].indirect(lists), gate_t[:, 2, cols], MULT)
             if s == 0:
-                nc.vector.tensor_tensor(part[:], prods[:, 0, :], prods[:, 1, :], ADD)
+                nc.vector.tensor_tensor(part, prods[:, 0, :], prods[:, 1, :], ADD)
             nc.vector.tensor_tensor(result[:, cols], part[:, cols], prods[:, 2, cols], ADD)
             nc.sync.dma_start(out[:, cols], result[:, cols])

@@ -20,7 +20,6 @@ GELU = mybir.ActivationFunctionType.Gelu_apprx_tanh
 GATHER = 384
 X_SPLIT = 320
 LAST = E - 1
-SKEWED = 9
 PAIRED = 8
 
 
@@ -28,13 +27,14 @@ def tile_moe_tk_glu_gelu_kernel(tc, xT, w1, w3, w2, gate, offs, pos1, pos2, pos3
     nc = tc.nc
     with ExitStack() as ctx:
         keep = ctx.enter_context(tc.tile_pool(name="keep", bufs=1))
-        raws = ctx.enter_context(tc.tile_pool(name="raws", bufs=10))
+        raws = ctx.enter_context(tc.tile_pool(name="raws", bufs=9))
         rounds = ctx.enter_context(tc.tile_pool(name="rounds", bufs=3))
         codes_pool = ctx.enter_context(tc.tile_pool(name="codes", bufs=2))
         w2_pool = ctx.enter_context(tc.tile_pool(name="w2_codes", bufs=4))
         h_pool = ctx.enter_context(tc.tile_pool(name="h_codes", bufs=E))
         slots = ctx.enter_context(tc.tile_pool(name="slots", bufs=2))
         hidden = ctx.enter_context(tc.tile_pool(name="hidden", bufs=2))
+        act_pool = ctx.enter_context(tc.tile_pool(name="acts", bufs=3))
         single = ctx.enter_context(tc.tile_pool(name="single", bufs=1))
         psum = ctx.enter_context(tc.psum_pool(name="psum", bufs=2))
 
@@ -143,7 +143,7 @@ def tile_moe_tk_glu_gelu_kernel(tc, xT, w1, w3, w2, gate, offs, pos1, pos2, pos3
                 count = 2 if e < PAIRED else 1
                 load_first(raw1, w1, e + 1, count)
                 load_first(raw3, w3, e, count)
-            if e == SKEWED:
+            if e == PAIRED + 1:
                 load_w2(0, 2)
             if e == 5:
                 for tile, source in zip(pos_t, (pos1, pos2, pos3)):
@@ -166,23 +166,27 @@ def tile_moe_tk_glu_gelu_kernel(tc, xT, w1, w3, w2, gate, offs, pos1, pos2, pos3
         banks_a[0] = first_layer(psum.tile([P, 4, C], F32, name="bank_a"), quantise(rounded[:], "w13"), 0, 0)
         for e in range(LAST):
             rounded = rounds.tile([P, 8 * H], BF16, align_bytes=64, name="rounded")
-            interleave_hidden(scopy, rounded[:, : 4 * H], raw1[e + 1])
-            acts[e] = raw1[e + 1][:, 0, :]
+            swapped = e < PAIRED and e % 2 == 1
+            interleave_hidden(vcopy if swapped else scopy, rounded[:, : 4 * H], raw1[e + 1])
+            if e >= PAIRED:
+                acts[e] = raw1[e + 1][:, 0, :]
+            else:
+                acts[e] = act_pool.tile([P, 4 * C], F32, name="act")[:]
             gelu(acts[e], banks_a[e])
-            interleave_hidden(vcopy, rounded[:, 4 * H :], raw3[e])
-            if 0 < e <= SKEWED:
+            interleave_hidden(scopy if swapped else vcopy, rounded[:, 4 * H :], raw3[e])
+            if e == PAIRED + 1:
                 hb = raw3[e][:, 0, : 2 * C].bitcast(BF16)
                 gated(hb, acts[e - 1], banks_b[e - 1])
             quantised = quantise(rounded[:], "w13")
             banks_b[e] = first_layer(psum.tile([P, 4, C], F32, name="bank_b"), quantised, H, e)
             banks_a[e + 1] = first_layer(psum.tile([P, 4, C], F32, name="bank_a"), quantised, 0, e + 1)
-            if 0 < e <= SKEWED:
+            if e == PAIRED + 1:
                 h_quantised[e - 1] = quantise(hb, "h", h_pool)
-            if e >= SKEWED:
+            if e != PAIRED:
                 own = hidden.tile([P, 4 * C], BF16, align_bytes=64, name="hb")
                 gated(own[:], acts[e], banks_b[e])
                 h_quantised[e] = quantise(own[:], "h", h_pool)
-            if e == SKEWED:
+            if e == PAIRED + 1:
                 rounded = hidden.tile([P, 2 * 4 * N], BF16, align_bytes=64, name="rounded_w2")
                 round_w2(rounded, 0, (0, 1))
                 second_layer(psum.tile([P, 2, C], F32, name="bank_y"), quantise(rounded[:], "w2", w2_pool), 0, 2)

@@ -21,6 +21,8 @@ GATHER = 384
 X_SPLIT = 320
 LAST = E - 1
 PAIRED = 8
+LAST_SPLIT = 92
+EARLY_W2 = {9: 0}
 
 
 def tile_moe_tk_glu_gelu_kernel(tc, xT, w1, w3, w2, gate, offs, pos1, pos2, pos3, out):
@@ -37,6 +39,7 @@ def tile_moe_tk_glu_gelu_kernel(tc, xT, w1, w3, w2, gate, offs, pos1, pos2, pos3
         act_pool = ctx.enter_context(tc.tile_pool(name="acts", bufs=3))
         single = ctx.enter_context(tc.tile_pool(name="single", bufs=1))
         psum = ctx.enter_context(tc.psum_pool(name="psum", bufs=2))
+        psum_y = ctx.enter_context(tc.psum_pool(name="psum_y", bufs=4))
 
         offs_t = keep.tile([P, E * C // 16], U16, name="offs_t")
         pos_t = [keep.tile([P, T // 16], U16, name=f"pos_t{r}") for r in range(TOP)]
@@ -118,14 +121,18 @@ def tile_moe_tk_glu_gelu_kernel(tc, xT, w1, w3, w2, gate, offs, pos1, pos2, pos3
             for i in range(count):
                 raw2[first + i] = tile[:, i]
 
-        def round_w2(rounded, first, experts, copy=scopy):
-            for e in experts:
-                at = (e - first) * 4 * N
-                interleave(copy, rounded[:, at : at + 4 * N], raw2[e])
+        def round_w2(rounded, experts):
+            for i, e in enumerate(experts):
+                interleave(scopy, rounded[:, i * 4 * N : (i + 1) * 4 * N], raw2[e])
 
-        def second_layer(bank, quantised, first, count, copy=scopy):
-            for i in range(count):
-                product(bank[:, i, :], quantised, i * N, h_quantised[first + i], 0)
+        def second_layer(parts, first, copy=scopy):
+            count = sum(n for quantised, at, n in parts)
+            bank = psum_y.tile([P, count, C], F32, name="bank_y")
+            i = 0
+            for quantised, at, n in parts:
+                for c in range(at, at + n):
+                    product(bank[:, i, :], quantised, c * N, h_quantised[first + i], 0)
+                    i = i + 1
             copy(y_all[:, first * C : (first + count) * C], bank[:].rearrange("p e n -> p (e n)"))
 
         nc.gpsimd.memset(x_scales[:], 0)
@@ -143,15 +150,17 @@ def tile_moe_tk_glu_gelu_kernel(tc, xT, w1, w3, w2, gate, offs, pos1, pos2, pos3
                 count = 2 if e < PAIRED else 1
                 load_first(raw1, w1, e + 1, count)
                 load_first(raw3, w3, e, count)
-            if e == PAIRED + 1:
-                load_w2(0, 2)
+            if e in EARLY_W2:
+                load_w2(EARLY_W2[e], 2)
             if e == 5:
                 for tile, source in zip(pos_t, (pos1, pos2, pos3)):
                     nc.sync.dma_start(tile[:], source)
-        for first in (2, 4, 6):
-            load_w2(first, 2)
+        load_w2(2, 2)
+        load_w2(6, 2)
+        load_w2(4, 1)
+        load_w2(8, 1)
         load_first(raw3, w3, LAST, 1)
-        for e in (10, 11, 8, 9):
+        for e in (10, 11, 5, 9):
             load_w2(e, 1)
         gate_t = raws.tile([P, TOP, T], F32, align_bytes=64, name="gate_t", tag="raw")
         nc.sync.dma_start(gate_t[:], gate.rearrange("r p t -> p r t"))
@@ -186,43 +195,40 @@ def tile_moe_tk_glu_gelu_kernel(tc, xT, w1, w3, w2, gate, offs, pos1, pos2, pos3
                 own = hidden.tile([P, 4 * C], BF16, align_bytes=64, name="hb")
                 gated(own[:], acts[e], banks_b[e])
                 h_quantised[e] = quantise(own[:], "h", h_pool)
-            if e == PAIRED + 1:
+            if e in EARLY_W2:
+                first = EARLY_W2[e]
                 rounded = hidden.tile([P, 2 * 4 * N], BF16, align_bytes=64, name="rounded_w2")
-                round_w2(rounded, 0, (0, 1))
-                second_layer(psum.tile([P, 2, C], F32, name="bank_y"), quantise(rounded[:], "w2", w2_pool), 0, 2)
+                round_w2(rounded, (first, first + 1))
+                second_layer([(quantise(rounded[:], "w2", w2_pool), 0, 2)], first)
 
         rounded = hidden.tile([P, 4 * 4 * N], BF16, align_bytes=64, name="rounded_w2")
-        round_w2(rounded, 2, range(2, 6))
+        round_w2(rounded, (2, 3, 6, 7))
         w2_a = quantise(rounded[:], "w2", w2_pool)
         rounded = hidden.tile([P, 2 * 4 * N], BF16, align_bytes=64, name="rounded_w2")
-        round_w2(rounded, 6, (6, 7))
+        round_w2(rounded, (4, 8))
         w2_b = quantise(rounded[:], "w2", w2_pool)
-        acts[LAST] = raw2[7].rearrange("p j n -> p (j n)")
+        acts[LAST] = raw2[8].rearrange("p j n -> p (j n)")
         gelu(acts[LAST], banks_a[LAST])
-        second_layer(psum.tile([P, 4, C], F32, name="bank_y"), w2_a, 2, 4)
 
         rounded = rounds.tile([P, 4 * H], BF16, align_bytes=64, name="rounded")
-        interleave_hidden(vcopy, rounded[:], raw3[LAST])
+        interleave_hidden(vcopy, rounded[:], raw3[LAST], slice(0, LAST_SPLIT))
+        interleave_hidden(scopy, rounded[:], raw3[LAST], slice(LAST_SPLIT, P))
         bank = psum.tile([P, 4, C], F32, name="bank_b")
         banks_b[LAST] = first_layer(bank, quantise(rounded[:], "w13"), 0, LAST)
 
         rounded = single.tile([P, 2 * 4 * N], BF16, align_bytes=64, name="rounded_c", tag="before_gated")
-        round_w2(rounded, 10, (10, 11))
+        round_w2(rounded, (10, 11))
         w2_d = quantise(rounded[:], "w2", w2_pool)
         hb = single.tile([P, 4 * C], BF16, align_bytes=64, name="hb_last", tag="before_gated")
         gated(hb[:], acts[LAST], banks_b[LAST])
         rounded = single.tile([P, 2 * 4 * N], BF16, align_bytes=64, name="rounded_d", tag="before_h")
-        round_w2(rounded, 8, (8, 9))
+        round_w2(rounded, (5, 9))
         w2_c = quantise(rounded[:], "w2", w2_pool)
         codes = single.tile([P, C], U32, align_bytes=64, name="codes_last", tag="before_h")
         h_quantised[LAST] = quantise(hb[:], "h", h_pool, codes)
-        bank = psum.tile([P, 4, C], F32, name="bank_y")
-        for i in range(2):
-            product(bank[:, i, :], w2_b, i * N, h_quantised[6 + i], 0)
-        for i in range(2):
-            product(bank[:, 2 + i, :], w2_c, i * N, h_quantised[8 + i], 0)
-        scopy(y_all[:, 6 * C : 10 * C], bank[:].rearrange("p e n -> p (e n)"))
-        second_layer(psum.tile([P, 2, C], F32, name="bank_y"), w2_d, 10, 2, vcopy)
+        second_layer([(w2_a, 0, 2), (w2_b, 0, 1), (w2_c, 0, 1)], 2)
+        second_layer([(w2_a, 2, 2), (w2_b, 1, 1), (w2_c, 1, 1)], 6, vcopy)
+        second_layer([(w2_d, 0, 2)], 10)
 
         prods = raws.tile([P, TOP, T], F32, align_bytes=64, name="prods", tag="raw")
         sums = raws.tile([P, 2, T], F32, align_bytes=64, name="sums", tag="raw")

@@ -20,24 +20,25 @@ GELU = mybir.ActivationFunctionType.Gelu_apprx_tanh
 GATHER = 384
 X_SPLIT = 320
 LAST = E - 1
-PAIRED = 8
-LAST_SPLIT = 92
-EARLY_W2 = {9: 0}
+SKEWED = 8
+LAST_SPLIT = 104
+Y_AT = 4096
+COMBINE = (256, 256)
 
 
 def tile_moe_tk_glu_gelu_kernel(tc, xT, w1, w3, w2, gate, offs, pos1, pos2, pos3, out):
     nc = tc.nc
     with ExitStack() as ctx:
         keep = ctx.enter_context(tc.tile_pool(name="keep", bufs=1))
-        raws = ctx.enter_context(tc.tile_pool(name="raws", bufs=9))
+        raws = ctx.enter_context(tc.tile_pool(name="raws", bufs=12))
         rounds = ctx.enter_context(tc.tile_pool(name="rounds", bufs=3))
-        codes_pool = ctx.enter_context(tc.tile_pool(name="codes", bufs=2))
-        w2_pool = ctx.enter_context(tc.tile_pool(name="w2_codes", bufs=4))
+        codes_pool = ctx.enter_context(tc.tile_pool(name="codes", bufs=3))
+        w2_pool = ctx.enter_context(tc.tile_pool(name="w2_codes", bufs=7))
         h_pool = ctx.enter_context(tc.tile_pool(name="h_codes", bufs=E))
-        slots = ctx.enter_context(tc.tile_pool(name="slots", bufs=2))
-        hidden = ctx.enter_context(tc.tile_pool(name="hidden", bufs=2))
-        act_pool = ctx.enter_context(tc.tile_pool(name="acts", bufs=3))
-        single = ctx.enter_context(tc.tile_pool(name="single", bufs=1))
+        slots = ctx.enter_context(tc.tile_pool(name="slots", bufs=4))
+        hidden = ctx.enter_context(tc.tile_pool(name="hidden", bufs=3))
+        held = ctx.enter_context(tc.tile_pool(name="held", bufs=1))
+        placed = ctx.enter_context(tc.tile_pool(name="placed", bufs=1))
         psum = ctx.enter_context(tc.psum_pool(name="psum", bufs=2))
         psum_y = ctx.enter_context(tc.psum_pool(name="psum_y", bufs=4))
 
@@ -47,14 +48,24 @@ def tile_moe_tk_glu_gelu_kernel(tc, xT, w1, w3, w2, gate, offs, pos1, pos2, pos3
         x_bf = rounds.tile([P, T * 4], BF16, align_bytes=64, name="x_bf", tag="rounded")
         x_codes = keep.tile([P, T], U32, align_bytes=64, name="x_codes")
         x_scales = keep.tile([P, T], U8, align_bytes=64, name="x_scales")
-        y_all = keep.tile([P, E * C], F32, name="y_all")
 
         vcopy, scopy = nc.vector.tensor_copy, nc.scalar.copy
 
-        def load(source, first, count=1):
-            tile = raws.tile([P, count, 4, source.shape[2]], F32, align_bytes=64, name="raw", tag="raw")
-            nc.sync.dma_start(tile[:], source[first : first + count].rearrange("e (p j) i -> p e j i", j=4))
+        def load(source, e, pool=raws, tag="raw"):
+            tile = pool.tile([P, 4, H], F32, align_bytes=64, name="raw", tag=tag)
+            nc.sync.dma_start(tile[:], source[e].rearrange("(p j) i -> p j i", j=4))
             return tile
+
+        raw2 = {}
+
+        def load_w2(first, count, pool=None, offset=None):
+            if pool is None:
+                tile = raws.tile([P, count, 4, N], F32, align_bytes=64, name="raw", tag="raw")
+            else:
+                tile = pool.tile([P, count, 4, N], F32, align_bytes=64, name="raw_last", offset=offset)
+            nc.sync.dma_start(tile[:], w2[first : first + count].rearrange("e (p j) i -> p e j i", j=4))
+            for i in range(count):
+                raw2[first + i] = tile[:, i]
 
         def interleave_hidden(copy, dst, src, part=slice(0, P)):
             copy(
@@ -65,12 +76,12 @@ def tile_moe_tk_glu_gelu_kernel(tc, xT, w1, w3, w2, gate, offs, pos1, pos2, pos3
         def interleave(copy, dst, src):
             copy(dst.rearrange("p (c i j) -> p c j i", i=4, j=4), src.rearrange("p j (c i) -> p c j i", i=4))
 
-        def quantise(src, tag, pool=codes_pool, codes=None):
+        def quantise(src, tag, pool, codes=None):
             width = src.shape[1] // 4
             if codes is None:
-                codes = pool.tile([P, width], U32, align_bytes=64, name=f"codes_{tag}")
+                codes = pool.tile([P, width], U32, align_bytes=64, name=f"codes_{tag}")[:]
             scales = pool.tile([P, width], U8, align_bytes=64, name=f"scales_{tag}")
-            nc.vector.quantize_mx(out=codes[:].bitcast(FP8X4), scales=scales[:], in_=src)
+            nc.vector.quantize_mx(out=codes.bitcast(FP8X4), scales=scales[:], in_=src)
             return codes, scales
 
         def product(bank, stationary, at, moving, start):
@@ -84,8 +95,6 @@ def tile_moe_tk_glu_gelu_kernel(tc, xT, w1, w3, w2, gate, offs, pos1, pos2, pos3
                 stop=True,
             )
 
-        gathered = {}
-
         def gather_tokens(piece):
             lists = offs_t[:, piece * GATHER // 16 : (piece + 1) * GATHER // 16]
             g_codes = slots.tile([P, GATHER], U32, align_bytes=64, name="g_codes")
@@ -94,10 +103,9 @@ def tile_moe_tk_glu_gelu_kernel(tc, xT, w1, w3, w2, gate, offs, pos1, pos2, pos3
             vcopy(g_scales[:], x_scales[:].indirect(lists))
             return g_codes, g_scales
 
-        def first_layer(bank, quantised, at, e):
+        def first_layer(name, quantised, at, e):
+            bank = psum.tile([P, 4, C], F32, name=name)
             piece, place = divmod(e * C, GATHER)
-            if piece not in gathered:
-                gathered[piece] = gather_tokens(piece)
             for t in range(4):
                 product(bank[:, t, :], quantised, at + t * P, gathered[piece], place)
             return bank
@@ -113,133 +121,142 @@ def tile_moe_tk_glu_gelu_kernel(tc, xT, w1, w3, w2, gate, offs, pos1, pos2, pos3
                 MULT,
             )
 
-        raw1, raw3, raw2 = {}, {}, {}
-        h_quantised = {}
+        h_quantised, w2_quantised = {}, {}
 
-        def load_w2(first, count):
-            tile = load(w2, first, count)
-            for i in range(count):
-                raw2[first + i] = tile[:, i]
+        rounded2 = {}
 
-        def round_w2(rounded, experts):
+        def round_w2(rounded, experts, on_vector=None):
             for i, e in enumerate(experts):
-                interleave(scopy, rounded[:, i * 4 * N : (i + 1) * 4 * N], raw2[e])
+                rounded2[e] = (rounded, i)
+                interleave(vcopy if e == on_vector else scopy, rounded[:, i * 4 * N : (i + 1) * 4 * N], raw2[e])
 
-        def second_layer(parts, first, copy=scopy):
-            count = sum(n for quantised, at, n in parts)
-            bank = psum_y.tile([P, count, C], F32, name="bank_y")
-            i = 0
-            for quantised, at, n in parts:
-                for c in range(at, at + n):
-                    product(bank[:, i, :], quantised, c * N, h_quantised[first + i], 0)
-                    i = i + 1
-            copy(y_all[:, first * C : (first + count) * C], bank[:].rearrange("p e n -> p (e n)"))
+        def behind_copy(raw):
+            return raw[:, 1:4, :].rearrange("p j i -> p (j i)").bitcast(BF16)
+
+        def quantise_w2(experts, codes=None):
+            rounded, at = rounded2[experts[0]]
+            quantised = quantise(rounded[:, at * 4 * N : (at + len(experts)) * 4 * N], "w2", w2_pool, codes)
+            for i, e in enumerate(experts):
+                w2_quantised[e] = (quantised, i * N)
+
+        def second_layer(experts, copy):
+            bank = psum_y.tile([P, len(experts), C], F32, name="bank_y")
+            for i, e in enumerate(experts):
+                product(bank[:, i, :], w2_quantised[e][0], w2_quantised[e][1], h_quantised[e], 0)
+            copy(y_all[:].rearrange("p (e n) -> p e n", n=C)[:, experts.start : experts.stop : experts.step, :], bank[:])
 
         nc.gpsimd.memset(x_scales[:], 0)
         nc.sync.dma_start(x_raw[:], xT.rearrange("(p j) t -> p j t", j=4))
         nc.sync.dma_start(offs_t[:], offs)
-
-        def load_first(where, source, first, count):
-            tile = load(source, first, count)
-            for i in range(count):
-                where[first + i] = tile[:, i]
-
-        load_first(raw1, w1, 0, 1)
+        raw1, raw3 = {0: load(w1, 0)}, {}
         for e in range(LAST):
-            if e not in raw3:
-                count = 2 if e < PAIRED else 1
-                load_first(raw1, w1, e + 1, count)
-                load_first(raw3, w3, e, count)
-            if e in EARLY_W2:
-                load_w2(EARLY_W2[e], 2)
-            if e == 5:
-                for tile, source in zip(pos_t, (pos1, pos2, pos3)):
-                    nc.sync.dma_start(tile[:], source)
+            raw1[e + 1] = load(w1, e + 1)
+            raw3[e] = load(w3, e) if e < SKEWED else load(w3, e, held, f"chain_{e}")
+        load_w2(0, 2)
         load_w2(2, 2)
-        load_w2(6, 2)
         load_w2(4, 1)
-        load_w2(8, 1)
-        load_first(raw3, w3, LAST, 1)
-        for e in (10, 11, 5, 9):
+        raw3[LAST] = load(w3, LAST, held, f"chain_{LAST}")
+        for e in range(5, LAST):
             load_w2(e, 1)
-        gate_t = raws.tile([P, TOP, T], F32, align_bytes=64, name="gate_t", tag="raw")
+        load_w2(LAST, 1, placed, Y_AT)
+        for r, source in enumerate((pos1, pos2, pos3)):
+            nc.sync.dma_start(pos_t[r][:], source)
+        gate_t = raws.tile([P, TOP, T], F32, align_bytes=64, name="raw", tag="raw")
         nc.sync.dma_start(gate_t[:], gate.rearrange("r p t -> p r t"))
 
         interleave(vcopy, x_bf[:, : 4 * X_SPLIT], x_raw[:, :, :X_SPLIT])
         interleave(scopy, x_bf[:, 4 * X_SPLIT :], x_raw[:, :, X_SPLIT:])
         nc.vector.quantize_mx(out=x_codes[:].bitcast(FP8X4), scales=x_scales[:], in_=x_bf[:])
+        gathered = [gather_tokens(piece) for piece in range(E * C // GATHER)]
 
         banks_a, banks_b, acts = {}, {}, {}
         rounded = rounds.tile([P, 4 * H], BF16, align_bytes=64, name="rounded")
-        interleave_hidden(scopy, rounded[:], raw1[0])
-        banks_a[0] = first_layer(psum.tile([P, 4, C], F32, name="bank_a"), quantise(rounded[:], "w13"), 0, 0)
+        interleave_hidden(scopy, rounded[:], raw1[0][:])
+        banks_a[0] = first_layer("bank_a", quantise(rounded[:], "w13", codes_pool), 0, 0)
         for e in range(LAST):
             rounded = rounds.tile([P, 8 * H], BF16, align_bytes=64, name="rounded")
-            swapped = e < PAIRED and e % 2 == 1
-            interleave_hidden(vcopy if swapped else scopy, rounded[:, : 4 * H], raw1[e + 1])
-            if e >= PAIRED:
-                acts[e] = raw1[e + 1][:, 0, :]
-            else:
-                acts[e] = act_pool.tile([P, 4 * C], F32, name="act")[:]
+            interleave_hidden(scopy, rounded[:, : 4 * H], raw1[e + 1][:])
+            interleave_hidden(vcopy if e > 0 else scopy, rounded[:, 4 * H :], raw3[e][:])
+            acts[e] = raw1[e + 1][:, 0, :] if e > 0 else raw3[0][:, 0, :]
             gelu(acts[e], banks_a[e])
-            interleave_hidden(scopy if swapped else vcopy, rounded[:, 4 * H :], raw3[e])
-            if e == PAIRED + 1:
+            if 0 < e <= SKEWED:
                 hb = raw3[e][:, 0, : 2 * C].bitcast(BF16)
                 gated(hb, acts[e - 1], banks_b[e - 1])
-            quantised = quantise(rounded[:], "w13")
-            banks_b[e] = first_layer(psum.tile([P, 4, C], F32, name="bank_b"), quantised, H, e)
-            banks_a[e + 1] = first_layer(psum.tile([P, 4, C], F32, name="bank_a"), quantised, 0, e + 1)
-            if e == PAIRED + 1:
-                h_quantised[e - 1] = quantise(hb, "h", h_pool)
-            if e != PAIRED:
+            if e < SKEWED:
+                quantised = quantise(rounded[:], "w13", codes_pool)
+                banks_b[e] = first_layer("bank_b", quantised, H, e)
+                banks_a[e + 1] = first_layer("bank_a", quantised, 0, e + 1)
+                if e > 0:
+                    h_quantised[e - 1] = quantise(hb, "h", h_pool)
+            else:
+                banks_b[e] = first_layer("bank_b", quantise(rounded[:, 4 * H :], "w13", codes_pool), 0, e)
+                if e == SKEWED:
+                    h_quantised[e - 1] = quantise(hb, "h", h_pool)
+                codes = held.tile([P, H], U32, align_bytes=64, name="codes_w1", tag=f"chain_{e}")
+                banks_a[e + 1] = first_layer("bank_a", quantise(rounded[:, : 4 * H], "w13", codes_pool, codes[:]), 0, e + 1)
+                if e == LAST - 1:
+                    round_w2(behind_copy(raw1[LAST]), range(0, 5))
+                    quantise_w2(range(0, 2))
                 own = hidden.tile([P, 4 * C], BF16, align_bytes=64, name="hb")
                 gated(own[:], acts[e], banks_b[e])
+                if e == LAST - 1:
+                    quantise_w2(range(2, 4))
                 h_quantised[e] = quantise(own[:], "h", h_pool)
-            if e in EARLY_W2:
-                first = EARLY_W2[e]
-                rounded = hidden.tile([P, 2 * 4 * N], BF16, align_bytes=64, name="rounded_w2")
-                round_w2(rounded, (first, first + 1))
-                second_layer([(quantise(rounded[:], "w2", w2_pool), 0, 2)], first)
 
-        rounded = hidden.tile([P, 4 * 4 * N], BF16, align_bytes=64, name="rounded_w2")
-        round_w2(rounded, (2, 3, 6, 7))
-        w2_a = quantise(rounded[:], "w2", w2_pool)
-        rounded = hidden.tile([P, 2 * 4 * N], BF16, align_bytes=64, name="rounded_w2")
-        round_w2(rounded, (4, 8))
-        w2_b = quantise(rounded[:], "w2", w2_pool)
-        acts[LAST] = raw2[8].rearrange("p j n -> p (j n)")
+        act_last = held.tile([P, 4 * C], F32, align_bytes=64, name="act_last", tag="chain_act")
+        acts[LAST] = act_last[:]
         gelu(acts[LAST], banks_a[LAST])
 
-        rounded = rounds.tile([P, 4 * H], BF16, align_bytes=64, name="rounded")
-        interleave_hidden(vcopy, rounded[:], raw3[LAST], slice(0, LAST_SPLIT))
-        interleave_hidden(scopy, rounded[:], raw3[LAST], slice(LAST_SPLIT, P))
+        rounded = placed.tile([P, 4 * H], BF16, align_bytes=64, name="rounded_last", offset=0)
+        interleave_hidden(vcopy, rounded[:], raw3[LAST][:], slice(0, LAST_SPLIT))
+        interleave_hidden(scopy, rounded[:], raw3[LAST][:], slice(LAST_SPLIT, P))
+        codes = held.tile([P, N], U32, align_bytes=64, name="codes_a", tag=f"chain_{LAST}")
+        quantise_w2(range(4, 5), codes[:])
         bank = psum.tile([P, 4, C], F32, name="bank_b")
-        banks_b[LAST] = first_layer(bank, quantise(rounded[:], "w13"), 0, LAST)
-
-        rounded = single.tile([P, 2 * 4 * N], BF16, align_bytes=64, name="rounded_c", tag="before_gated")
-        round_w2(rounded, (10, 11))
-        w2_d = quantise(rounded[:], "w2", w2_pool)
-        hb = single.tile([P, 4 * C], BF16, align_bytes=64, name="hb_last", tag="before_gated")
+        piece, place = divmod(LAST * C, GATHER)
+        for half in range(2):
+            quantised = quantise(rounded[:, half * 2 * H : (half + 1) * 2 * H], "w13", codes_pool)
+            for t in range(2):
+                product(bank[:, 2 * half + t, :], quantised, t * P, gathered[piece], place)
+        banks_b[LAST] = bank
+        rounded = held.tile([P, 6 * 4 * N], BF16, align_bytes=64, name="rounded_late")
+        round_w2(rounded[:], range(5, 7))
+        codes = placed.tile([P, 2 * N], U32, align_bytes=64, name="codes_b", offset=0)
+        quantise_w2(range(5, 7), codes[:])
+        pair = placed.tile([P, 2 * 4 * N], BF16, align_bytes=64, name="rounded_pair", offset=2048)
+        round_w2(pair[:], range(7, 9), 7)
+        round_w2(rounded[:, 2 * 4 * N :], range(9, E))
+        hb = hidden.tile([P, 4 * C], BF16, align_bytes=64, name="hb")
         gated(hb[:], acts[LAST], banks_b[LAST])
-        rounded = single.tile([P, 2 * 4 * N], BF16, align_bytes=64, name="rounded_d", tag="before_h")
-        round_w2(rounded, (5, 9))
-        w2_c = quantise(rounded[:], "w2", w2_pool)
-        codes = single.tile([P, C], U32, align_bytes=64, name="codes_last", tag="before_h")
-        h_quantised[LAST] = quantise(hb[:], "h", h_pool, codes)
-        second_layer([(w2_a, 0, 2), (w2_b, 0, 1), (w2_c, 0, 1)], 2)
-        second_layer([(w2_a, 2, 2), (w2_b, 1, 1), (w2_c, 1, 1)], 6, vcopy)
-        second_layer([(w2_d, 0, 2)], 10)
+        codes = held.tile([P, 5 * N], U32, align_bytes=64, name="codes_c", tag="chain_act")
+        quantise_w2(range(7, 9), codes[:, : 2 * N])
+        h_quantised[LAST] = quantise(hb[:], "h", h_pool)
+        quantise_w2(range(9, LAST), codes[:, 2 * N : 4 * N])
+        quantise_w2(range(LAST, E), codes[:, 4 * N :])
+        y_all = placed.tile([P, E * C], F32, align_bytes=64, name="y_all", offset=Y_AT)
+        second_layer(range(0, 4), scopy)
+        second_layer(range(4, 8), vcopy)
+        second_layer(range(8, LAST), scopy)
+        second_layer(range(LAST, E), scopy)
 
-        prods = raws.tile([P, TOP, T], F32, align_bytes=64, name="prods", tag="raw")
-        sums = raws.tile([P, 2, T], F32, align_bytes=64, name="sums", tag="raw")
-        part, result = sums[:, 0, :], sums[:, 1, :]
-        for r in range(2):
-            nc.vector.tensor_tensor(prods[:, r, :], y_all[:].indirect(pos_t[r][:]), gate_t[:, r, :], MULT)
-        for s in range(0, T, T // 2):
-            cols = slice(s, s + T // 2)
-            lists = pos_t[2][:, s // 16 : (s + T // 2) // 16]
-            nc.vector.tensor_tensor(prods[:, 2, cols], y_all[:].indirect(lists), gate_t[:, 2, cols], MULT)
-            if s == 0:
-                nc.vector.tensor_tensor(part, prods[:, 0, :], prods[:, 1, :], ADD)
-            nc.vector.tensor_tensor(result[:, cols], part[:, cols], prods[:, 2, cols], ADD)
+        prods = [keep.tile([P, T], F32, align_bytes=64, name=f"prods{r}") for r in range(TOP)]
+        part = keep.tile([P, T], F32, align_bytes=64, name="part")
+        result = keep.tile([P, T], F32, align_bytes=64, name="result")
+
+        def weighted(r, cols):
+            lists = pos_t[r][:, cols.start // 16 : cols.stop // 16]
+            nc.vector.tensor_tensor(prods[r][:, cols], y_all[:].indirect(lists), gate_t[:, r, cols], MULT)
+
+        def finish(cols):
+            nc.vector.tensor_tensor(result[:, cols], part[:, cols], prods[2][:, cols], ADD)
             nc.sync.dma_start(out[:, cols], result[:, cols])
+
+        pieces = [slice(sum(COMBINE[:i]), sum(COMBINE[: i + 1])) for i in range(len(COMBINE))]
+        weighted(0, slice(0, T))
+        weighted(1, slice(0, T))
+        weighted(2, pieces[0])
+        nc.vector.tensor_tensor(part[:], prods[0][:], prods[1][:], ADD)
+        for before, cols in zip(pieces, pieces[1:]):
+            weighted(2, cols)
+            finish(before)
+        finish(pieces[-1])

@@ -21,6 +21,8 @@ GATHER = 384
 X_SPLIT = 320
 LAST = E - 1
 SKEWED = 8
+PAIRED_W1 = 8
+PAIRED_W3 = 6
 LAST_SPLIT = 104
 Y_AT = 4096
 COMBINE = (256, 256)
@@ -30,7 +32,7 @@ def tile_moe_tk_glu_gelu_kernel(tc, xT, w1, w3, w2, gate, offs, pos1, pos2, pos3
     nc = tc.nc
     with ExitStack() as ctx:
         keep = ctx.enter_context(tc.tile_pool(name="keep", bufs=1))
-        raws = ctx.enter_context(tc.tile_pool(name="raws", bufs=12))
+        raws = ctx.enter_context(tc.tile_pool(name="raws", bufs=5))
         rounds = ctx.enter_context(tc.tile_pool(name="rounds", bufs=3))
         codes_pool = ctx.enter_context(tc.tile_pool(name="codes", bufs=3))
         w2_pool = ctx.enter_context(tc.tile_pool(name="w2_codes", bufs=7))
@@ -56,11 +58,16 @@ def tile_moe_tk_glu_gelu_kernel(tc, xT, w1, w3, w2, gate, offs, pos1, pos2, pos3
             nc.sync.dma_start(tile[:], source[e].rearrange("(p j) i -> p j i", j=4))
             return tile
 
+        def load_pair(where, source, e):
+            tile = raws.tile([P, 2, 4, H], F32, align_bytes=64, name="raw", tag="raw")
+            nc.sync.dma_start(tile[:], source[e : e + 2].rearrange("e (p j) i -> p e j i", j=4))
+            where[e], where[e + 1] = tile[:, 0], tile[:, 1]
+
         raw2 = {}
 
         def load_w2(first, count, pool=None, offset=None):
             if pool is None:
-                tile = raws.tile([P, count, 4, N], F32, align_bytes=64, name="raw", tag="raw")
+                tile = keep.tile([P, count, 4, N], F32, align_bytes=64, name=f"raw_w2_{first}")
             else:
                 tile = pool.tile([P, count, 4, N], F32, align_bytes=64, name="raw_last", offset=offset)
             nc.sync.dma_start(tile[:], w2[first : first + count].rearrange("e (p j) i -> p e j i", j=4))
@@ -150,8 +157,14 @@ def tile_moe_tk_glu_gelu_kernel(tc, xT, w1, w3, w2, gate, offs, pos1, pos2, pos3
         nc.sync.dma_start(offs_t[:], offs)
         raw1, raw3 = {0: load(w1, 0)}, {}
         for e in range(LAST):
-            raw1[e + 1] = load(w1, e + 1)
-            raw3[e] = load(w3, e) if e < SKEWED else load(w3, e, held, f"chain_{e}")
+            if e >= PAIRED_W1:
+                raw1[e + 1] = load(w1, e + 1)
+            elif e % 2 == 0:
+                load_pair(raw1, w1, e + 1)
+            if e >= PAIRED_W3:
+                raw3[e] = load(w3, e) if e < SKEWED else load(w3, e, held, f"chain_{e}")
+            elif e % 2 == 0:
+                load_pair(raw3, w3, e)
         load_w2(0, 2)
         load_w2(2, 2)
         load_w2(4, 1)
@@ -176,8 +189,8 @@ def tile_moe_tk_glu_gelu_kernel(tc, xT, w1, w3, w2, gate, offs, pos1, pos2, pos3
         for e in range(LAST):
             rounded = rounds.tile([P, 8 * H], BF16, align_bytes=64, name="rounded")
             interleave_hidden(scopy, rounded[:, : 4 * H], raw1[e + 1][:])
-            interleave_hidden(vcopy if e > 0 else scopy, rounded[:, 4 * H :], raw3[e][:])
-            acts[e] = raw1[e + 1][:, 0, :] if e > 0 else raw3[0][:, 0, :]
+            interleave_hidden(vcopy, rounded[:, 4 * H :], raw3[e][:])
+            acts[e] = raw1[e + 1][:, 0, :]
             gelu(acts[e], banks_a[e])
             if 0 < e <= SKEWED:
                 hb = raw3[e][:, 0, : 2 * C].bitcast(BF16)

@@ -21,10 +21,17 @@ GATHER = 384
 X_SPLIT = 320
 LAST = E - 1
 SKEWED = 8
-PAIRED_W1 = 8
-PAIRED_W3 = 6
 LAST_SPLIT = 104
-Y_AT = 4096
+SLOT = 4 * H * 4
+W2_BYTES = 4 * N * 4
+RING = 5
+LATE_W2 = 5
+FIRST_AT = 6 * W2_BYTES - 64
+LAST_W3_AT = FIRST_AT + SLOT - 64
+A_AT = [FIRST_AT] + [LAST_W3_AT + (1 + i) * SLOT for i in range(RING - 1)]
+B_RING = 5
+B_AT = [A_AT[-1] + (1 + i) * SLOT for i in range(B_RING)]
+Y_AT = FIRST_AT + 64
 COMBINE = (256, 256)
 
 
@@ -32,7 +39,7 @@ def tile_moe_tk_glu_gelu_kernel(tc, xT, w1, w3, w2, gate, offs, pos1, pos2, pos3
     nc = tc.nc
     with ExitStack() as ctx:
         keep = ctx.enter_context(tc.tile_pool(name="keep", bufs=1))
-        raws = ctx.enter_context(tc.tile_pool(name="raws", bufs=5))
+        ring = ctx.enter_context(tc.tile_pool(name="ring", bufs=1))
         rounds = ctx.enter_context(tc.tile_pool(name="rounds", bufs=3))
         codes_pool = ctx.enter_context(tc.tile_pool(name="codes", bufs=3))
         w2_pool = ctx.enter_context(tc.tile_pool(name="w2_codes", bufs=7))
@@ -46,33 +53,27 @@ def tile_moe_tk_glu_gelu_kernel(tc, xT, w1, w3, w2, gate, offs, pos1, pos2, pos3
 
         offs_t = keep.tile([P, E * C // 16], U16, name="offs_t")
         pos_t = [keep.tile([P, T // 16], U16, name=f"pos_t{r}") for r in range(TOP)]
-        x_raw = raws.tile([P, 4, T], F32, align_bytes=64, name="x_raw", tag="raw")
+        x_raw = ring.tile([P, 4, T], F32, align_bytes=64, name="x_raw", offset=A_AT[0])
         x_bf = rounds.tile([P, T * 4], BF16, align_bytes=64, name="x_bf", tag="rounded")
         x_codes = keep.tile([P, T], U32, align_bytes=64, name="x_codes")
         x_scales = keep.tile([P, T], U8, align_bytes=64, name="x_scales")
 
         vcopy, scopy = nc.vector.tensor_copy, nc.scalar.copy
 
-        def load(source, e, pool=raws, tag="raw"):
-            tile = pool.tile([P, 4, H], F32, align_bytes=64, name="raw", tag=tag)
+        def load(source, e, at, name):
+            tile = ring.tile([P, 4, H], F32, align_bytes=64, name=f"{name}_{e}", offset=at)
             nc.sync.dma_start(tile[:], source[e].rearrange("(p j) i -> p j i", j=4))
             return tile
 
-        def load_pair(where, source, e):
-            tile = raws.tile([P, 2, 4, H], F32, align_bytes=64, name="raw", tag="raw")
-            nc.sync.dma_start(tile[:], source[e : e + 2].rearrange("e (p j) i -> p e j i", j=4))
-            where[e], where[e + 1] = tile[:, 0], tile[:, 1]
-
         raw2 = {}
 
-        def load_w2(first, count, pool=None, offset=None):
-            if pool is None:
-                tile = keep.tile([P, count, 4, N], F32, align_bytes=64, name=f"raw_w2_{first}")
-            else:
-                tile = pool.tile([P, count, 4, N], F32, align_bytes=64, name="raw_last", offset=offset)
-            nc.sync.dma_start(tile[:], w2[first : first + count].rearrange("e (p j) i -> p e j i", j=4))
-            for i in range(count):
-                raw2[first + i] = tile[:, i]
+        def load_w2(tile, base, first, count):
+            nc.sync.dma_start(
+                tile[:, first - base : first - base + count],
+                w2[first : first + count].rearrange("e (p j) i -> p e j i", j=4),
+            )
+            for e in range(first, first + count):
+                raw2[e] = tile[:, e - base]
 
         def interleave_hidden(copy, dst, src, part=slice(0, P)):
             copy(
@@ -132,10 +133,10 @@ def tile_moe_tk_glu_gelu_kernel(tc, xT, w1, w3, w2, gate, offs, pos1, pos2, pos3
 
         rounded2 = {}
 
-        def round_w2(rounded, experts, on_vector=None):
+        def round_w2(rounded, experts):
             for i, e in enumerate(experts):
                 rounded2[e] = (rounded, i)
-                interleave(vcopy if e == on_vector else scopy, rounded[:, i * 4 * N : (i + 1) * 4 * N], raw2[e])
+                interleave(scopy, rounded[:, i * 4 * N : (i + 1) * 4 * N], raw2[e])
 
         def behind_copy(raw):
             return raw[:, 1:4, :].rearrange("p j i -> p (j i)").bitcast(BF16)
@@ -155,27 +156,17 @@ def tile_moe_tk_glu_gelu_kernel(tc, xT, w1, w3, w2, gate, offs, pos1, pos2, pos3
         nc.gpsimd.memset(x_scales[:], 0)
         nc.sync.dma_start(x_raw[:], xT.rearrange("(p j) t -> p j t", j=4))
         nc.sync.dma_start(offs_t[:], offs)
-        raw1, raw3 = {0: load(w1, 0)}, {}
+        at1 = {e: B_AT[e % B_RING] for e in range(1, 10)}
+        at1[0] = A_AT[4]
+        at3 = {e: A_AT[(e + 1) % RING] for e in range(9)}
+        at1[10], at3[9], at1[11], at3[10], at3[11] = A_AT[0], A_AT[1], A_AT[2], A_AT[3], LAST_W3_AT
+        raw1, raw3 = {0: load(w1, 0, at1[0], "raw1")}, {}
+        codes_w1 = {}
         for e in range(LAST):
-            if e >= PAIRED_W1:
-                raw1[e + 1] = load(w1, e + 1)
-            elif e % 2 == 0:
-                load_pair(raw1, w1, e + 1)
-            if e >= PAIRED_W3:
-                raw3[e] = load(w3, e) if e < SKEWED else load(w3, e, held, f"chain_{e}")
-            elif e % 2 == 0:
-                load_pair(raw3, w3, e)
-        load_w2(0, 2)
-        load_w2(2, 2)
-        load_w2(4, 1)
-        raw3[LAST] = load(w3, LAST, held, f"chain_{LAST}")
-        for e in range(5, LAST):
-            load_w2(e, 1)
-        load_w2(LAST, 1, placed, Y_AT)
-        for r, source in enumerate((pos1, pos2, pos3)):
-            nc.sync.dma_start(pos_t[r][:], source)
-        gate_t = raws.tile([P, TOP, T], F32, align_bytes=64, name="raw", tag="raw")
-        nc.sync.dma_start(gate_t[:], gate.rearrange("r p t -> p r t"))
+            raw1[e + 1] = load(w1, e + 1, at1[e + 1], "raw1")
+            raw3[e] = load(w3, e, at3[e], "raw3")
+            if e >= SKEWED:
+                codes_w1[e] = ring.tile([P, H], U32, align_bytes=64, name=f"codes_w1_{e}", offset=at3[e])
 
         interleave(vcopy, x_bf[:, : 4 * X_SPLIT], x_raw[:, :, :X_SPLIT])
         interleave(scopy, x_bf[:, 4 * X_SPLIT :], x_raw[:, :, X_SPLIT:])
@@ -205,9 +196,31 @@ def tile_moe_tk_glu_gelu_kernel(tc, xT, w1, w3, w2, gate, offs, pos1, pos2, pos3
                 banks_b[e] = first_layer("bank_b", quantise(rounded[:, 4 * H :], "w13", codes_pool), 0, e)
                 if e == SKEWED:
                     h_quantised[e - 1] = quantise(hb, "h", h_pool)
-                codes = held.tile([P, H], U32, align_bytes=64, name="codes_w1", tag=f"chain_{e}")
+                codes = codes_w1[e]
                 banks_a[e + 1] = first_layer("bank_a", quantise(rounded[:, : 4 * H], "w13", codes_pool, codes[:]), 0, e + 1)
+                if e == LAST - 3:
+                    early = ring.tile([P, 4, 4, N], F32, align_bytes=64, name="raw2_early", offset=at3[e])
+                    load_w2(early, 0, 0, 1)
+                    load_w2(early, 0, 1, 1)
+                    load_w2(early, 0, 2, 2)
+                if e == LAST - 2:
+                    y_all = ring.tile([P, E * C], F32, align_bytes=64, name="y_all", offset=Y_AT)
+                    raw2[4] = y_all[:, : 4 * N].rearrange("p (j n) -> p j n", j=4)
+                    nc.sync.dma_start(raw2[4], w2[4].rearrange("(p j) i -> p j i", j=4))
+                    raw3[LAST] = load(w3, LAST, at3[LAST], "raw3")
+                    late = ring.tile([P, 6, 4, N], F32, align_bytes=64, name="raw2_late", offset=0)
+                    places = {i: late[:, i - 5] for i in range(5, 11)}
+                    places[11] = y_all[:, 6 * C : 6 * C + 4 * N].rearrange("p (j n) -> p j n", j=4)
+                    for i in range(5, 12):
+                        raw2[i] = places[i]
+                        nc.sync.dma_start(raw2[i], w2[i].rearrange("(p j) i -> p j i", j=4))
+                    nc.sync.dma_start(pos_t[0][:], pos1)
                 if e == LAST - 1:
+                    gate_t = ring.tile([P, TOP, T], F32, align_bytes=64, name="gate_t", offset=at3[e])
+                    nc.sync.dma_start(gate_t[:, 0, :], gate[0])
+                    nc.sync.dma_start(pos_t[1][:], pos2)
+                    nc.sync.dma_start(pos_t[2][:], pos3)
+                    nc.sync.dma_start(gate_t[:, 1:, :], gate[1:].rearrange("r p t -> p r t"))
                     round_w2(behind_copy(raw1[LAST]), range(0, 5))
                     quantise_w2(range(0, 2))
                 own = hidden.tile([P, 4 * C], BF16, align_bytes=64, name="hb")
@@ -223,7 +236,7 @@ def tile_moe_tk_glu_gelu_kernel(tc, xT, w1, w3, w2, gate, offs, pos1, pos2, pos3
         rounded = placed.tile([P, 4 * H], BF16, align_bytes=64, name="rounded_last", offset=0)
         interleave_hidden(vcopy, rounded[:], raw3[LAST][:], slice(0, LAST_SPLIT))
         interleave_hidden(scopy, rounded[:], raw3[LAST][:], slice(LAST_SPLIT, P))
-        codes = held.tile([P, N], U32, align_bytes=64, name="codes_a", tag=f"chain_{LAST}")
+        codes = ring.tile([P, N], U32, align_bytes=64, name="codes_a", offset=at3[LAST])
         quantise_w2(range(4, 5), codes[:])
         bank = psum.tile([P, 4, C], F32, name="bank_b")
         piece, place = divmod(LAST * C, GATHER)
@@ -237,19 +250,19 @@ def tile_moe_tk_glu_gelu_kernel(tc, xT, w1, w3, w2, gate, offs, pos1, pos2, pos3
         codes = placed.tile([P, 2 * N], U32, align_bytes=64, name="codes_b", offset=0)
         quantise_w2(range(5, 7), codes[:])
         pair = placed.tile([P, 2 * 4 * N], BF16, align_bytes=64, name="rounded_pair", offset=2048)
-        round_w2(pair[:], range(7, 9), 7)
+        round_w2(pair[:], range(7, 9))
         round_w2(rounded[:, 2 * 4 * N :], range(9, E))
         hb = hidden.tile([P, 4 * C], BF16, align_bytes=64, name="hb")
         gated(hb[:], acts[LAST], banks_b[LAST])
         codes = held.tile([P, 5 * N], U32, align_bytes=64, name="codes_c", tag="chain_act")
         quantise_w2(range(7, 9), codes[:, : 2 * N])
         h_quantised[LAST] = quantise(hb[:], "h", h_pool)
-        quantise_w2(range(9, LAST), codes[:, 2 * N : 4 * N])
+        quantise_w2(range(9, 10), codes[:, 2 * N : 3 * N])
+        quantise_w2(range(10, 11), codes[:, 3 * N : 4 * N])
         quantise_w2(range(LAST, E), codes[:, 4 * N :])
-        y_all = placed.tile([P, E * C], F32, align_bytes=64, name="y_all", offset=Y_AT)
         second_layer(range(0, 4), scopy)
-        second_layer(range(4, 8), vcopy)
-        second_layer(range(8, LAST), scopy)
+        second_layer(range(4, 8), scopy)
+        second_layer(range(8, LAST), vcopy)
         second_layer(range(LAST, E), scopy)
 
         prods = [keep.tile([P, T], F32, align_bytes=64, name=f"prods{r}") for r in range(TOP)]

@@ -26,12 +26,13 @@ SLOT = 4 * H * 4
 W2_BYTES = 4 * N * 4
 RING = 5
 LATE_W2 = 5
-FIRST_AT = 6 * W2_BYTES - 64
-LAST_W3_AT = FIRST_AT + SLOT - 64
+LINE = 256
+FIRST_AT = 6 * W2_BYTES - LINE
+LAST_W3_AT = FIRST_AT + SLOT - LINE
 A_AT = [FIRST_AT] + [LAST_W3_AT + (1 + i) * SLOT for i in range(RING - 1)]
 B_RING = 5
 B_AT = [A_AT[-1] + (1 + i) * SLOT for i in range(B_RING)]
-Y_AT = FIRST_AT + 64
+Y_AT = FIRST_AT + LINE
 COMBINE = (256, 256)
 
 
@@ -53,7 +54,7 @@ def tile_moe_tk_glu_gelu_kernel(tc, xT, w1, w3, w2, gate, offs, pos1, pos2, pos3
 
         offs_t = keep.tile([P, E * C // 16], U16, name="offs_t")
         pos_t = [keep.tile([P, T // 16], U16, name=f"pos_t{r}") for r in range(TOP)]
-        x_raw = ring.tile([P, 4, T], F32, align_bytes=64, name="x_raw", offset=A_AT[0])
+        x_raw = ring.tile([P, 4, T], F32, align_bytes=LINE, name="x_raw", offset=A_AT[0])
         x_bf = rounds.tile([P, T * 4], BF16, align_bytes=64, name="x_bf", tag="rounded")
         x_codes = keep.tile([P, T], U32, align_bytes=64, name="x_codes")
         x_scales = keep.tile([P, T], U8, align_bytes=64, name="x_scales")
@@ -61,7 +62,7 @@ def tile_moe_tk_glu_gelu_kernel(tc, xT, w1, w3, w2, gate, offs, pos1, pos2, pos3
         vcopy, scopy = nc.vector.tensor_copy, nc.scalar.copy
 
         def load(source, e, at, name):
-            tile = ring.tile([P, 4, H], F32, align_bytes=64, name=f"{name}_{e}", offset=at)
+            tile = ring.tile([P, 4, H], F32, align_bytes=LINE, name=f"{name}_{e}", offset=at)
             nc.sync.dma_start(tile[:], source[e].rearrange("(p j) i -> p j i", j=4))
             return tile
 
@@ -166,7 +167,7 @@ def tile_moe_tk_glu_gelu_kernel(tc, xT, w1, w3, w2, gate, offs, pos1, pos2, pos3
             raw1[e + 1] = load(w1, e + 1, at1[e + 1], "raw1")
             raw3[e] = load(w3, e, at3[e], "raw3")
             if e >= SKEWED:
-                codes_w1[e] = ring.tile([P, H], U32, align_bytes=64, name=f"codes_w1_{e}", offset=at3[e])
+                codes_w1[e] = ring.tile([P, H], U32, align_bytes=LINE, name=f"codes_w1_{e}", offset=at3[e])
 
         interleave(vcopy, x_bf[:, : 4 * X_SPLIT], x_raw[:, :, :X_SPLIT])
         interleave(scopy, x_bf[:, 4 * X_SPLIT :], x_raw[:, :, X_SPLIT:])
@@ -199,16 +200,16 @@ def tile_moe_tk_glu_gelu_kernel(tc, xT, w1, w3, w2, gate, offs, pos1, pos2, pos3
                 codes = codes_w1[e]
                 banks_a[e + 1] = first_layer("bank_a", quantise(rounded[:, : 4 * H], "w13", codes_pool, codes[:]), 0, e + 1)
                 if e == LAST - 3:
-                    early = ring.tile([P, 4, 4, N], F32, align_bytes=64, name="raw2_early", offset=at3[e])
+                    early = ring.tile([P, 4, 4, N], F32, align_bytes=LINE, name="raw2_early", offset=at3[e])
                     load_w2(early, 0, 0, 1)
                     load_w2(early, 0, 1, 1)
                     load_w2(early, 0, 2, 2)
                 if e == LAST - 2:
-                    y_all = ring.tile([P, E * C], F32, align_bytes=64, name="y_all", offset=Y_AT)
+                    y_all = ring.tile([P, E * C], F32, align_bytes=LINE, name="y_all", offset=Y_AT)
                     raw2[4] = y_all[:, : 4 * N].rearrange("p (j n) -> p j n", j=4)
                     nc.sync.dma_start(raw2[4], w2[4].rearrange("(p j) i -> p j i", j=4))
                     raw3[LAST] = load(w3, LAST, at3[LAST], "raw3")
-                    late = ring.tile([P, 6, 4, N], F32, align_bytes=64, name="raw2_late", offset=0)
+                    late = ring.tile([P, 6, 4, N], F32, align_bytes=LINE, name="raw2_late", offset=0)
                     places = {i: late[:, i - 5] for i in range(5, 11)}
                     places[11] = y_all[:, 6 * C : 6 * C + 4 * N].rearrange("p (j n) -> p j n", j=4)
                     for i in range(5, 12):
@@ -216,7 +217,7 @@ def tile_moe_tk_glu_gelu_kernel(tc, xT, w1, w3, w2, gate, offs, pos1, pos2, pos3
                         nc.sync.dma_start(raw2[i], w2[i].rearrange("(p j) i -> p j i", j=4))
                     nc.sync.dma_start(pos_t[0][:], pos1)
                 if e == LAST - 1:
-                    gate_t = ring.tile([P, TOP, T], F32, align_bytes=64, name="gate_t", offset=at3[e])
+                    gate_t = ring.tile([P, TOP, T], F32, align_bytes=LINE, name="gate_t", offset=at3[e])
                     nc.sync.dma_start(gate_t[:, 0, :], gate[0])
                     nc.sync.dma_start(pos_t[1][:], pos2)
                     nc.sync.dma_start(pos_t[2][:], pos3)
@@ -236,7 +237,7 @@ def tile_moe_tk_glu_gelu_kernel(tc, xT, w1, w3, w2, gate, offs, pos1, pos2, pos3
         rounded = placed.tile([P, 4 * H], BF16, align_bytes=64, name="rounded_last", offset=0)
         interleave_hidden(vcopy, rounded[:], raw3[LAST][:], slice(0, LAST_SPLIT))
         interleave_hidden(scopy, rounded[:], raw3[LAST][:], slice(LAST_SPLIT, P))
-        codes = ring.tile([P, N], U32, align_bytes=64, name="codes_a", offset=at3[LAST])
+        codes = ring.tile([P, N], U32, align_bytes=LINE, name="codes_a", offset=at3[LAST])
         quantise_w2(range(4, 5), codes[:])
         bank = psum.tile([P, 4, C], F32, name="bank_b")
         piece, place = divmod(LAST * C, GATHER)
@@ -267,7 +268,7 @@ def tile_moe_tk_glu_gelu_kernel(tc, xT, w1, w3, w2, gate, offs, pos1, pos2, pos3
 
         prods = [keep.tile([P, T], F32, align_bytes=64, name=f"prods{r}") for r in range(TOP)]
         part = keep.tile([P, T], F32, align_bytes=64, name="part")
-        result = keep.tile([P, T], F32, align_bytes=64, name="result")
+        result = keep.tile([P, T], F32, align_bytes=LINE, name="result")
 
         def weighted(r, cols):
             lists = pos_t[r][:, cols.start // 16 : cols.stop // 16]

@@ -1,6 +1,7 @@
 from contextlib import ExitStack
 
 import concourse.mybir as mybir
+from concourse.masks import make_identity
 
 K, T, E, C, H, N = 512, 512, 12, 128, 512, 128
 TOP = 3
@@ -21,7 +22,6 @@ GATHER = 384
 X_SPLIT = 320
 LAST = E - 1
 SKEWED = 8
-LAST_SPLIT = 104
 SLOT = 4 * H * 4
 W2_BYTES = 4 * N * 4
 RING = 5
@@ -32,8 +32,8 @@ LAST_W3_AT = FIRST_AT + SLOT - LINE
 A_AT = [FIRST_AT] + [LAST_W3_AT + (1 + i) * SLOT for i in range(RING - 1)]
 B_RING = 5
 B_AT = [A_AT[-1] + (1 + i) * SLOT for i in range(B_RING)]
+LAST_SPLIT = 88
 Y_AT = FIRST_AT + LINE
-COMBINE = (256, 256)
 
 
 def tile_moe_tk_glu_gelu_kernel(tc, xT, w1, w3, w2, gate, offs, pos1, pos2, pos3, out):
@@ -76,10 +76,10 @@ def tile_moe_tk_glu_gelu_kernel(tc, xT, w1, w3, w2, gate, offs, pos1, pos2, pos3
             for e in range(first, first + count):
                 raw2[e] = tile[:, e - base]
 
-        def interleave_hidden(copy, dst, src, part=slice(0, P)):
+        def interleave_hidden(copy, dst, src, part=slice(0, P), planes=slice(0, 4)):
             copy(
-                dst.rearrange("p (t m j) -> p m j t", t=4, j=4)[:, part],
-                src.rearrange("p j (m t) -> p m j t", t=4)[:, part],
+                dst.rearrange("p (t m j) -> p m j t", t=4, j=4)[:, part, :, planes],
+                src.rearrange("p j (m t) -> p m j t", t=4)[:, part, :, planes],
             )
 
         def interleave(copy, dst, src):
@@ -134,10 +134,10 @@ def tile_moe_tk_glu_gelu_kernel(tc, xT, w1, w3, w2, gate, offs, pos1, pos2, pos3
 
         rounded2 = {}
 
-        def round_w2(rounded, experts):
+        def round_w2(rounded, experts, on_vector=None):
             for i, e in enumerate(experts):
                 rounded2[e] = (rounded, i)
-                interleave(scopy, rounded[:, i * 4 * N : (i + 1) * 4 * N], raw2[e])
+                interleave(vcopy if e == on_vector else scopy, rounded[:, i * 4 * N : (i + 1) * 4 * N], raw2[e])
 
         def behind_copy(raw):
             return raw[:, 1:4, :].rearrange("p j i -> p (j i)").bitcast(BF16)
@@ -155,6 +155,8 @@ def tile_moe_tk_glu_gelu_kernel(tc, xT, w1, w3, w2, gate, offs, pos1, pos2, pos3
             copy(y_all[:].rearrange("p (e n) -> p e n", n=C)[:, experts.start : experts.stop : experts.step, :], bank[:])
 
         nc.gpsimd.memset(x_scales[:], 0)
+        identity = keep.tile([P, P], F32, align_bytes=64, name="identity")
+        make_identity(nc, identity[:])
         nc.sync.dma_start(x_raw[:], xT.rearrange("(p j) t -> p j t", j=4))
         nc.sync.dma_start(offs_t[:], offs)
         at1 = {e: B_AT[e % B_RING] for e in range(1, 10)}
@@ -165,6 +167,9 @@ def tile_moe_tk_glu_gelu_kernel(tc, xT, w1, w3, w2, gate, offs, pos1, pos2, pos3
         codes_w1 = {}
         for e in range(LAST):
             raw1[e + 1] = load(w1, e + 1, at1[e + 1], "raw1")
+            if e == LAST - 2:
+                first_one = ring.tile([P, 1, 4, N], F32, align_bytes=LINE, name="raw2_first", offset=B_AT[0])
+                load_w2(first_one, 0, 0, 1)
             raw3[e] = load(w3, e, at3[e], "raw3")
             if e >= SKEWED:
                 codes_w1[e] = ring.tile([P, H], U32, align_bytes=LINE, name=f"codes_w1_{e}", offset=at3[e])
@@ -200,10 +205,9 @@ def tile_moe_tk_glu_gelu_kernel(tc, xT, w1, w3, w2, gate, offs, pos1, pos2, pos3
                 codes = codes_w1[e]
                 banks_a[e + 1] = first_layer("bank_a", quantise(rounded[:, : 4 * H], "w13", codes_pool, codes[:]), 0, e + 1)
                 if e == LAST - 3:
-                    early = ring.tile([P, 4, 4, N], F32, align_bytes=LINE, name="raw2_early", offset=at3[e])
-                    load_w2(early, 0, 0, 1)
-                    load_w2(early, 0, 1, 1)
-                    load_w2(early, 0, 2, 2)
+                    early = ring.tile([P, 3, 4, N], F32, align_bytes=LINE, name="raw2_early", offset=at3[e])
+                    for i in range(1, 4):
+                        load_w2(early, 1, i, 1)
                 if e == LAST - 2:
                     y_all = ring.tile([P, E * C], F32, align_bytes=LINE, name="y_all", offset=Y_AT)
                     raw2[4] = y_all[:, : 4 * N].rearrange("p (j n) -> p j n", j=4)
@@ -222,12 +226,14 @@ def tile_moe_tk_glu_gelu_kernel(tc, xT, w1, w3, w2, gate, offs, pos1, pos2, pos3
                     nc.sync.dma_start(pos_t[1][:], pos2)
                     nc.sync.dma_start(pos_t[2][:], pos3)
                     nc.sync.dma_start(gate_t[:, 1:, :], gate[1:].rearrange("r p t -> p r t"))
-                    round_w2(behind_copy(raw1[LAST]), range(0, 5))
-                    quantise_w2(range(0, 2))
+                    round_w2(behind_copy(raw1[LAST]), range(1, 5))
+                    quantise_w2(range(1, 3))
+                if e == LAST - 2:
+                    round_w2(behind_copy(raw1[e + 1]), range(0, 1))
                 own = hidden.tile([P, 4 * C], BF16, align_bytes=64, name="hb")
                 gated(own[:], acts[e], banks_b[e])
-                if e == LAST - 1:
-                    quantise_w2(range(2, 4))
+                if e >= LAST - 2:
+                    quantise_w2(range(0, 1) if e == LAST - 2 else range(3, 4))
                 h_quantised[e] = quantise(own[:], "h", h_pool)
 
         act_last = held.tile([P, 4 * C], F32, align_bytes=64, name="act_last", tag="chain_act")
@@ -235,10 +241,9 @@ def tile_moe_tk_glu_gelu_kernel(tc, xT, w1, w3, w2, gate, offs, pos1, pos2, pos3
         gelu(acts[LAST], banks_a[LAST])
 
         rounded = placed.tile([P, 4 * H], BF16, align_bytes=64, name="rounded_last", offset=0)
-        interleave_hidden(vcopy, rounded[:], raw3[LAST][:], slice(0, LAST_SPLIT))
-        interleave_hidden(scopy, rounded[:], raw3[LAST][:], slice(LAST_SPLIT, P))
-        codes = ring.tile([P, N], U32, align_bytes=LINE, name="codes_a", offset=at3[LAST])
-        quantise_w2(range(4, 5), codes[:])
+        interleave_hidden(vcopy, rounded[:], raw3[LAST][:], planes=slice(0, 2))
+        interleave_hidden(vcopy, rounded[:], raw3[LAST][:], slice(0, LAST_SPLIT), slice(2, 4))
+        interleave_hidden(scopy, rounded[:], raw3[LAST][:], slice(LAST_SPLIT, P), slice(2, 4))
         bank = psum.tile([P, 4, C], F32, name="bank_b")
         piece, place = divmod(LAST * C, GATHER)
         for half in range(2):
@@ -246,12 +251,14 @@ def tile_moe_tk_glu_gelu_kernel(tc, xT, w1, w3, w2, gate, offs, pos1, pos2, pos3
             for t in range(2):
                 product(bank[:, 2 * half + t, :], quantised, t * P, gathered[piece], place)
         banks_b[LAST] = bank
+        codes = ring.tile([P, N], U32, align_bytes=LINE, name="codes_a", offset=at3[LAST])
+        quantise_w2(range(4, 5), codes[:])
         rounded = held.tile([P, 6 * 4 * N], BF16, align_bytes=64, name="rounded_late")
         round_w2(rounded[:], range(5, 7))
         codes = placed.tile([P, 2 * N], U32, align_bytes=64, name="codes_b", offset=0)
         quantise_w2(range(5, 7), codes[:])
         pair = placed.tile([P, 2 * 4 * N], BF16, align_bytes=64, name="rounded_pair", offset=2048)
-        round_w2(pair[:], range(7, 9))
+        round_w2(pair[:], range(7, 9), 7)
         round_w2(rounded[:, 2 * 4 * N :], range(9, E))
         hb = hidden.tile([P, 4 * C], BF16, align_bytes=64, name="hb")
         gated(hb[:], acts[LAST], banks_b[LAST])
@@ -274,16 +281,24 @@ def tile_moe_tk_glu_gelu_kernel(tc, xT, w1, w3, w2, gate, offs, pos1, pos2, pos3
             lists = pos_t[r][:, cols.start // 16 : cols.stop // 16]
             nc.vector.tensor_tensor(prods[r][:, cols], y_all[:].indirect(lists), gate_t[:, r, cols], MULT)
 
-        def finish(cols):
-            nc.vector.tensor_tensor(result[:, cols], part[:, cols], prods[2][:, cols], ADD)
-            nc.sync.dma_start(out[:, cols], result[:, cols])
+        backs = [psum.tile([P, T // 2], F32, name="bank_a") for half in range(2)]
 
-        pieces = [slice(sum(COMBINE[:i]), sum(COMBINE[: i + 1])) for i in range(len(COMBINE))]
+        def sum_two(block):
+            cols = slice(block * P, (block + 1) * P)
+            bank = psum_y.tile([P, P], F32, name="bank_y")
+            for r in range(2):
+                nc.tensor.matmul(bank[:], prods[r][:, cols], identity[:], start=r == 0, stop=r == 1, is_transpose=True)
+            scopy(part[:, cols], bank[:])
+            nc.tensor.transpose(backs[block // 2][:, block % 2 * P : (block % 2 + 1) * P], part[:, cols], identity[:])
+
         weighted(0, slice(0, T))
-        weighted(1, slice(0, T))
-        weighted(2, pieces[0])
-        nc.vector.tensor_tensor(part[:], prods[0][:], prods[1][:], ADD)
-        for before, cols in zip(pieces, pieces[1:]):
+        for blocks in ((0, 1), (2,), (3,)):
+            weighted(1, slice(blocks[0] * P, (blocks[-1] + 1) * P))
+            for block in blocks:
+                sum_two(block)
+        halves = [slice(0, T // 2), slice(T // 2, T)]
+        for cols in halves:
             weighted(2, cols)
-            finish(before)
-        finish(pieces[-1])
+        for back, cols in zip(backs, halves):
+            nc.vector.tensor_tensor(result[:, cols], back[:], prods[2][:, cols], ADD)
+            nc.sync.dma_start(out[:, cols], result[:, cols])

@@ -18,22 +18,22 @@ MULT = mybir.AluOpType.mult
 ADD = mybir.AluOpType.add
 GELU = mybir.ActivationFunctionType.Gelu_apprx_tanh
 
+LAST = E - 1
 GATHER = 384
 X_SPLIT = 320
-LAST = E - 1
 SKEWED = 8
-SLOT = 4 * H * 4
+LAST_SPLIT = 100
+FIRST_LATE = 5
+
+LINE = 256
+MATRIX_BYTES = 4 * H * 4
 W2_BYTES = 4 * N * 4
 RING = 5
-LATE_W2 = 5
-LINE = 256
-FIRST_AT = 6 * W2_BYTES - LINE
-LAST_W3_AT = FIRST_AT + SLOT - LINE
-A_AT = [FIRST_AT] + [LAST_W3_AT + (1 + i) * SLOT for i in range(RING - 1)]
-B_RING = 5
-B_AT = [A_AT[-1] + (1 + i) * SLOT for i in range(B_RING)]
-LAST_SPLIT = 88
-Y_AT = FIRST_AT + LINE
+A_FIRST = 6 * W2_BYTES - LINE
+Y_AT = A_FIRST + LINE
+LAST_W3_AT = A_FIRST + MATRIX_BYTES - LINE
+A_AT = [A_FIRST] + [LAST_W3_AT + (1 + i) * MATRIX_BYTES for i in range(RING - 1)]
+B_AT = [A_AT[-1] + (1 + i) * MATRIX_BYTES for i in range(RING)]
 
 
 def tile_moe_tk_glu_gelu_kernel(tc, xT, w1, w3, w2, gate, offs, pos1, pos2, pos3, out):
@@ -45,7 +45,7 @@ def tile_moe_tk_glu_gelu_kernel(tc, xT, w1, w3, w2, gate, offs, pos1, pos2, pos3
         codes_pool = ctx.enter_context(tc.tile_pool(name="codes", bufs=3))
         w2_pool = ctx.enter_context(tc.tile_pool(name="w2_codes", bufs=7))
         h_pool = ctx.enter_context(tc.tile_pool(name="h_codes", bufs=E))
-        slots = ctx.enter_context(tc.tile_pool(name="slots", bufs=4))
+        slots = ctx.enter_context(tc.tile_pool(name="slots", bufs=E * C // GATHER))
         hidden = ctx.enter_context(tc.tile_pool(name="hidden", bufs=3))
         held = ctx.enter_context(tc.tile_pool(name="held", bufs=1))
         placed = ctx.enter_context(tc.tile_pool(name="placed", bufs=1))
@@ -60,26 +60,26 @@ def tile_moe_tk_glu_gelu_kernel(tc, xT, w1, w3, w2, gate, offs, pos1, pos2, pos3
         x_scales = keep.tile([P, T], U8, align_bytes=64, name="x_scales")
 
         vcopy, scopy = nc.vector.tensor_copy, nc.scalar.copy
+        raw1, raw3, raw2 = {}, {}, {}
+        rounded2, w2_quantised, h_quantised = {}, {}, {}
+        banks_a, banks_b, acts = {}, {}, {}
 
         def load(source, e, at, name):
             tile = ring.tile([P, 4, H], F32, align_bytes=LINE, name=f"{name}_{e}", offset=at)
             nc.sync.dma_start(tile[:], source[e].rearrange("(p j) i -> p j i", j=4))
             return tile
 
-        raw2 = {}
+        def load_w2(e, place):
+            raw2[e] = place
+            nc.sync.dma_start(place, w2[e].rearrange("(p j) n -> p j n", j=4))
 
-        def load_w2(tile, base, first, count):
-            nc.sync.dma_start(
-                tile[:, first - base : first - base + count],
-                w2[first : first + count].rearrange("e (p j) i -> p e j i", j=4),
-            )
-            for e in range(first, first + count):
-                raw2[e] = tile[:, e - base]
+        def as_w2(columns):
+            return columns.rearrange("p (j n) -> p j n", j=4)
 
-        def interleave_hidden(copy, dst, src, part=slice(0, P), planes=slice(0, 4)):
+        def interleave_hidden(copy, dst, src, ms=slice(0, P), ts=slice(0, 4)):
             copy(
-                dst.rearrange("p (t m j) -> p m j t", t=4, j=4)[:, part, :, planes],
-                src.rearrange("p j (m t) -> p m j t", t=4)[:, part, :, planes],
+                dst.rearrange("p (t m j) -> p m j t", t=4, j=4)[:, ms, :, ts],
+                src.rearrange("p j (m t) -> p m j t", t=4)[:, ms, :, ts],
             )
 
         def interleave(copy, dst, src):
@@ -130,21 +130,17 @@ def tile_moe_tk_glu_gelu_kernel(tc, xT, w1, w3, w2, gate, offs, pos1, pos2, pos3
                 MULT,
             )
 
-        h_quantised, w2_quantised = {}, {}
-
-        rounded2 = {}
-
-        def round_w2(rounded, experts, on_vector=None):
+        def round_w2(dst, experts, on_vector=None):
             for i, e in enumerate(experts):
-                rounded2[e] = (rounded, i)
-                interleave(vcopy if e == on_vector else scopy, rounded[:, i * 4 * N : (i + 1) * 4 * N], raw2[e])
+                rounded2[e] = (dst, i)
+                interleave(vcopy if e == on_vector else scopy, dst[:, i * 4 * N : (i + 1) * 4 * N], raw2[e])
 
         def behind_copy(raw):
             return raw[:, 1:4, :].rearrange("p j i -> p (j i)").bitcast(BF16)
 
         def quantise_w2(experts, codes=None):
-            rounded, at = rounded2[experts[0]]
-            quantised = quantise(rounded[:, at * 4 * N : (at + len(experts)) * 4 * N], "w2", w2_pool, codes)
+            src, at = rounded2[experts[0]]
+            quantised = quantise(src[:, at * 4 * N : (at + len(experts)) * 4 * N], "w2", w2_pool, codes)
             for i, e in enumerate(experts):
                 w2_quantised[e] = (quantised, i * N)
 
@@ -152,24 +148,26 @@ def tile_moe_tk_glu_gelu_kernel(tc, xT, w1, w3, w2, gate, offs, pos1, pos2, pos3
             bank = psum_y.tile([P, len(experts), C], F32, name="bank_y")
             for i, e in enumerate(experts):
                 product(bank[:, i, :], w2_quantised[e][0], w2_quantised[e][1], h_quantised[e], 0)
-            copy(y_all[:].rearrange("p (e n) -> p e n", n=C)[:, experts.start : experts.stop : experts.step, :], bank[:])
+            copy(y_all[:].rearrange("p (e n) -> p e n", n=C)[:, experts.start : experts.stop, :], bank[:])
 
         nc.gpsimd.memset(x_scales[:], 0)
         identity = keep.tile([P, P], F32, align_bytes=64, name="identity")
         make_identity(nc, identity[:])
+
         nc.sync.dma_start(x_raw[:], xT.rearrange("(p j) t -> p j t", j=4))
         nc.sync.dma_start(offs_t[:], offs)
-        at1 = {e: B_AT[e % B_RING] for e in range(1, 10)}
-        at1[0] = A_AT[4]
-        at3 = {e: A_AT[(e + 1) % RING] for e in range(9)}
-        at1[10], at3[9], at1[11], at3[10], at3[11] = A_AT[0], A_AT[1], A_AT[2], A_AT[3], LAST_W3_AT
-        raw1, raw3 = {0: load(w1, 0, at1[0], "raw1")}, {}
+        at1 = {e: B_AT[e % RING] for e in range(1, LAST - 1)}
+        at3 = {e: A_AT[(e + 1) % RING] for e in range(LAST - 2)}
+        at1[0] = A_AT[RING - 1]
+        at1[LAST - 1], at3[LAST - 2], at1[LAST], at3[LAST - 1] = A_AT[: RING - 1]
+        at3[LAST] = LAST_W3_AT
+        raw1[0] = load(w1, 0, at1[0], "raw1")
         codes_w1 = {}
         for e in range(LAST):
             raw1[e + 1] = load(w1, e + 1, at1[e + 1], "raw1")
             if e == LAST - 2:
-                first_one = ring.tile([P, 1, 4, N], F32, align_bytes=LINE, name="raw2_first", offset=B_AT[0])
-                load_w2(first_one, 0, 0, 1)
+                first_w2 = ring.tile([P, 4, N], F32, align_bytes=LINE, name="raw2_first", offset=B_AT[0])
+                load_w2(0, first_w2[:])
             raw3[e] = load(w3, e, at3[e], "raw3")
             if e >= SKEWED:
                 codes_w1[e] = ring.tile([P, H], U32, align_bytes=LINE, name=f"codes_w1_{e}", offset=at3[e])
@@ -179,7 +177,6 @@ def tile_moe_tk_glu_gelu_kernel(tc, xT, w1, w3, w2, gate, offs, pos1, pos2, pos3
         nc.vector.quantize_mx(out=x_codes[:].bitcast(FP8X4), scales=x_scales[:], in_=x_bf[:])
         gathered = [gather_tokens(piece) for piece in range(E * C // GATHER)]
 
-        banks_a, banks_b, acts = {}, {}, {}
         rounded = rounds.tile([P, 4 * H], BF16, align_bytes=64, name="rounded")
         interleave_hidden(scopy, rounded[:], raw1[0][:])
         banks_a[0] = first_layer("bank_a", quantise(rounded[:], "w13", codes_pool), 0, 0)
@@ -190,106 +187,103 @@ def tile_moe_tk_glu_gelu_kernel(tc, xT, w1, w3, w2, gate, offs, pos1, pos2, pos3
             acts[e] = raw1[e + 1][:, 0, :]
             gelu(acts[e], banks_a[e])
             if 0 < e <= SKEWED:
-                hb = raw3[e][:, 0, : 2 * C].bitcast(BF16)
-                gated(hb, acts[e - 1], banks_b[e - 1])
+                h_before = raw3[e][:, 0, : 2 * C].bitcast(BF16)
+                gated(h_before, acts[e - 1], banks_b[e - 1])
             if e < SKEWED:
                 quantised = quantise(rounded[:], "w13", codes_pool)
                 banks_b[e] = first_layer("bank_b", quantised, H, e)
                 banks_a[e + 1] = first_layer("bank_a", quantised, 0, e + 1)
                 if e > 0:
-                    h_quantised[e - 1] = quantise(hb, "h", h_pool)
-            else:
-                banks_b[e] = first_layer("bank_b", quantise(rounded[:, 4 * H :], "w13", codes_pool), 0, e)
-                if e == SKEWED:
-                    h_quantised[e - 1] = quantise(hb, "h", h_pool)
-                codes = codes_w1[e]
-                banks_a[e + 1] = first_layer("bank_a", quantise(rounded[:, : 4 * H], "w13", codes_pool, codes[:]), 0, e + 1)
-                if e == LAST - 3:
-                    early = ring.tile([P, 3, 4, N], F32, align_bytes=LINE, name="raw2_early", offset=at3[e])
-                    for i in range(1, 4):
-                        load_w2(early, 1, i, 1)
-                if e == LAST - 2:
-                    y_all = ring.tile([P, E * C], F32, align_bytes=LINE, name="y_all", offset=Y_AT)
-                    raw2[4] = y_all[:, : 4 * N].rearrange("p (j n) -> p j n", j=4)
-                    nc.sync.dma_start(raw2[4], w2[4].rearrange("(p j) i -> p j i", j=4))
-                    raw3[LAST] = load(w3, LAST, at3[LAST], "raw3")
-                    late = ring.tile([P, 6, 4, N], F32, align_bytes=LINE, name="raw2_late", offset=0)
-                    places = {i: late[:, i - 5] for i in range(5, 11)}
-                    places[11] = y_all[:, 6 * C : 6 * C + 4 * N].rearrange("p (j n) -> p j n", j=4)
-                    for i in range(5, 12):
-                        raw2[i] = places[i]
-                        nc.sync.dma_start(raw2[i], w2[i].rearrange("(p j) i -> p j i", j=4))
-                    nc.sync.dma_start(pos_t[0][:], pos1)
-                if e == LAST - 1:
-                    gate_t = ring.tile([P, TOP, T], F32, align_bytes=LINE, name="gate_t", offset=at3[e])
-                    nc.sync.dma_start(gate_t[:, 0, :], gate[0])
-                    nc.sync.dma_start(pos_t[1][:], pos2)
-                    nc.sync.dma_start(pos_t[2][:], pos3)
-                    nc.sync.dma_start(gate_t[:, 1:, :], gate[1:].rearrange("r p t -> p r t"))
-                    round_w2(behind_copy(raw1[LAST]), range(1, 5))
-                    quantise_w2(range(1, 3))
-                if e == LAST - 2:
-                    round_w2(behind_copy(raw1[e + 1]), range(0, 1))
-                own = hidden.tile([P, 4 * C], BF16, align_bytes=64, name="hb")
-                gated(own[:], acts[e], banks_b[e])
-                if e >= LAST - 2:
-                    quantise_w2(range(0, 1) if e == LAST - 2 else range(3, 4))
-                h_quantised[e] = quantise(own[:], "h", h_pool)
+                    h_quantised[e - 1] = quantise(h_before, "h", h_pool)
+                continue
+
+            banks_b[e] = first_layer("bank_b", quantise(rounded[:, 4 * H :], "w13", codes_pool), 0, e)
+            if e == SKEWED:
+                h_quantised[e - 1] = quantise(h_before, "h", h_pool)
+            banks_a[e + 1] = first_layer("bank_a", quantise(rounded[:, : 4 * H], "w13", codes_pool, codes_w1[e][:]), 0, e + 1)
+
+            if e == LAST - 3:
+                early_w2 = ring.tile([P, 3, 4, N], F32, align_bytes=LINE, name="raw2_early", offset=at3[e])
+                for i in range(1, 4):
+                    load_w2(i, early_w2[:, i - 1])
+            if e == LAST - 2:
+                y_all = ring.tile([P, E * C], F32, align_bytes=LINE, name="y_all", offset=Y_AT)
+                load_w2(4, as_w2(y_all[:, : 4 * C]))
+                raw3[LAST] = load(w3, LAST, at3[LAST], "raw3")
+                late_w2 = ring.tile([P, LAST - FIRST_LATE, 4, N], F32, align_bytes=LINE, name="raw2_late", offset=0)
+                for i in range(FIRST_LATE, LAST):
+                    load_w2(i, late_w2[:, i - FIRST_LATE])
+                load_w2(LAST, as_w2(y_all[:, 6 * C : 10 * C]))
+                nc.sync.dma_start(pos_t[0][:], pos1)
+                round_w2(behind_copy(raw1[e + 1]), range(0, 1))
+            if e == LAST - 1:
+                gate_t = ring.tile([P, TOP, T], F32, align_bytes=LINE, name="gate_t", offset=at3[e])
+                nc.sync.dma_start(gate_t[:, 0, :], gate[0])
+                nc.sync.dma_start(pos_t[1][:], pos2)
+                nc.sync.dma_start(pos_t[2][:], pos3)
+                nc.sync.dma_start(gate_t[:, 1:, :], gate[1:].rearrange("r p t -> p r t"))
+                round_w2(behind_copy(raw1[e + 1]), range(1, FIRST_LATE))
+                quantise_w2(range(1, 3))
+
+            h_own = hidden.tile([P, 4 * C], BF16, align_bytes=64, name="hb")
+            gated(h_own[:], acts[e], banks_b[e])
+            if e == LAST - 2:
+                quantise_w2(range(0, 1))
+            if e == LAST - 1:
+                quantise_w2(range(3, 4))
+            h_quantised[e] = quantise(h_own[:], "h", h_pool)
 
         act_last = held.tile([P, 4 * C], F32, align_bytes=64, name="act_last", tag="chain_act")
-        acts[LAST] = act_last[:]
-        gelu(acts[LAST], banks_a[LAST])
+        gelu(act_last[:], banks_a[LAST])
 
-        rounded = placed.tile([P, 4 * H], BF16, align_bytes=64, name="rounded_last", offset=0)
-        interleave_hidden(vcopy, rounded[:], raw3[LAST][:], planes=slice(0, 2))
-        interleave_hidden(vcopy, rounded[:], raw3[LAST][:], slice(0, LAST_SPLIT), slice(2, 4))
-        interleave_hidden(scopy, rounded[:], raw3[LAST][:], slice(LAST_SPLIT, P), slice(2, 4))
-        bank = psum.tile([P, 4, C], F32, name="bank_b")
+        rounded_last = placed.tile([P, 4 * H], BF16, align_bytes=64, name="rounded_last", offset=0)
+        interleave_hidden(vcopy, rounded_last[:], raw3[LAST][:], ts=slice(0, 2))
+        interleave_hidden(vcopy, rounded_last[:], raw3[LAST][:], slice(0, LAST_SPLIT), slice(2, 4))
+        interleave_hidden(scopy, rounded_last[:], raw3[LAST][:], slice(LAST_SPLIT, P), slice(2, 4))
+        bank_last = psum.tile([P, 4, C], F32, name="bank_b")
         piece, place = divmod(LAST * C, GATHER)
         for half in range(2):
-            quantised = quantise(rounded[:, half * 2 * H : (half + 1) * 2 * H], "w13", codes_pool)
+            quantised = quantise(rounded_last[:, half * 2 * H : (half + 1) * 2 * H], "w13", codes_pool)
             for t in range(2):
-                product(bank[:, 2 * half + t, :], quantised, t * P, gathered[piece], place)
-        banks_b[LAST] = bank
-        codes = ring.tile([P, N], U32, align_bytes=LINE, name="codes_a", offset=at3[LAST])
-        quantise_w2(range(4, 5), codes[:])
-        rounded = held.tile([P, 6 * 4 * N], BF16, align_bytes=64, name="rounded_late")
-        round_w2(rounded[:], range(5, 7))
-        codes = placed.tile([P, 2 * N], U32, align_bytes=64, name="codes_b", offset=0)
-        quantise_w2(range(5, 7), codes[:])
-        pair = placed.tile([P, 2 * 4 * N], BF16, align_bytes=64, name="rounded_pair", offset=2048)
-        round_w2(pair[:], range(7, 9), 7)
-        round_w2(rounded[:, 2 * 4 * N :], range(9, E))
-        hb = hidden.tile([P, 4 * C], BF16, align_bytes=64, name="hb")
-        gated(hb[:], acts[LAST], banks_b[LAST])
-        codes = held.tile([P, 5 * N], U32, align_bytes=64, name="codes_c", tag="chain_act")
-        quantise_w2(range(7, 9), codes[:, : 2 * N])
-        h_quantised[LAST] = quantise(hb[:], "h", h_pool)
-        quantise_w2(range(9, 10), codes[:, 2 * N : 3 * N])
-        quantise_w2(range(10, 11), codes[:, 3 * N : 4 * N])
-        quantise_w2(range(LAST, E), codes[:, 4 * N :])
+                product(bank_last[:, 2 * half + t, :], quantised, t * P, gathered[piece], place)
+
+        codes_4 = ring.tile([P, N], U32, align_bytes=LINE, name="codes_a", offset=at3[LAST])
+        quantise_w2(range(4, 5), codes_4[:])
+        rounded_late = held.tile([P, 5 * 4 * N], BF16, align_bytes=64, name="rounded_late")
+        round_w2(rounded_late[:], range(5, 7))
+        codes_56 = placed.tile([P, 2 * N], U32, align_bytes=64, name="codes_b", offset=0)
+        quantise_w2(range(5, 7), codes_56[:])
+        rounded_78 = placed.tile([P, 2 * 4 * N], BF16, align_bytes=64, name="rounded_pair", offset=W2_BYTES)
+        round_w2(rounded_78[:], range(7, 9), on_vector=7)
+        round_w2(rounded_late[:, 2 * 4 * N :], range(9, E))
+        h_last = hidden.tile([P, 4 * C], BF16, align_bytes=64, name="hb")
+        gated(h_last[:], act_last[:], bank_last)
+        codes_late = held.tile([P, 5 * N], U32, align_bytes=64, name="codes_c", tag="chain_act")
+        quantise_w2(range(7, 9), codes_late[:, : 2 * N])
+        h_quantised[LAST] = quantise(h_last[:], "h", h_pool)
+        for e in range(9, E):
+            quantise_w2(range(e, e + 1), codes_late[:, (e - 7) * N : (e - 6) * N])
         second_layer(range(0, 4), scopy)
         second_layer(range(4, 8), scopy)
         second_layer(range(8, LAST), vcopy)
         second_layer(range(LAST, E), scopy)
 
         prods = [keep.tile([P, T], F32, align_bytes=64, name=f"prods{r}") for r in range(TOP)]
-        part = keep.tile([P, T], F32, align_bytes=64, name="part")
+        turned = keep.tile([P, T], F32, align_bytes=64, name="part")
         result = keep.tile([P, T], F32, align_bytes=LINE, name="result")
+        sums = [psum.tile([P, T // 2], F32, name="bank_a") for half in range(2)]
 
         def weighted(r, cols):
             lists = pos_t[r][:, cols.start // 16 : cols.stop // 16]
             nc.vector.tensor_tensor(prods[r][:, cols], y_all[:].indirect(lists), gate_t[:, r, cols], MULT)
-
-        backs = [psum.tile([P, T // 2], F32, name="bank_a") for half in range(2)]
 
         def sum_two(block):
             cols = slice(block * P, (block + 1) * P)
             bank = psum_y.tile([P, P], F32, name="bank_y")
             for r in range(2):
                 nc.tensor.matmul(bank[:], prods[r][:, cols], identity[:], start=r == 0, stop=r == 1, is_transpose=True)
-            scopy(part[:, cols], bank[:])
-            nc.tensor.transpose(backs[block // 2][:, block % 2 * P : (block % 2 + 1) * P], part[:, cols], identity[:])
+            scopy(turned[:, cols], bank[:])
+            nc.tensor.transpose(sums[block // 2][:, block % 2 * P : (block % 2 + 1) * P], turned[:, cols], identity[:])
 
         weighted(0, slice(0, T))
         for blocks in ((0, 1), (2,), (3,)):
@@ -299,6 +293,6 @@ def tile_moe_tk_glu_gelu_kernel(tc, xT, w1, w3, w2, gate, offs, pos1, pos2, pos3
         halves = [slice(0, T // 2), slice(T // 2, T)]
         for cols in halves:
             weighted(2, cols)
-        for back, cols in zip(backs, halves):
-            nc.vector.tensor_tensor(result[:, cols], back[:], prods[2][:, cols], ADD)
+        for two, cols in zip(sums, halves):
+            nc.vector.tensor_tensor(result[:, cols], two[:], prods[2][:, cols], ADD)
             nc.sync.dma_start(out[:, cols], result[:, cols])

@@ -17,6 +17,10 @@ FP8X4 = mybir.dt.float8_e4m3fn_x4
 MULT = mybir.AluOpType.mult
 ADD = mybir.AluOpType.add
 GELU = mybir.ActivationFunctionType.Gelu_apprx_tanh
+COPY = mybir.ActivationFunctionType.Copy
+BLOCKS = T // P
+DIRECT = 384
+TURNED = BLOCKS + (T - DIRECT) // P
 
 LAST = E - 1
 GATHER = 384
@@ -153,9 +157,17 @@ def tile_moe_tk_glu_gelu_kernel(tc, xT, w1, w3, w2, gate, offs, pos1, pos2, pos3
         nc.gpsimd.memset(x_scales[:], 0)
         identity = keep.tile([P, P], F32, align_bytes=64, name="identity")
         make_identity(nc, identity[:])
+        gate_rows = keep.tile([P, P], F32, align_bytes=LINE, name="gate_rows")
+        gate_cols = keep.tile([P, 8], F32, align_bytes=64, name="gate_cols")
+        nc.gpsimd.memset(gate_rows[:], 0)
 
         nc.sync.dma_start(x_raw[:], xT.rearrange("(p j) t -> p j t", j=4))
         nc.sync.dma_start(offs_t[:], offs)
+        rows = gate.rearrange("r p (b t) -> (r p b) t", t=P)
+        nc.sync.dma_start(gate_rows[:TURNED, :], rows[(TOP * BLOCKS - TURNED) * (P + 1) :: P + 1, :])
+        bank_gate = psum_y.tile([P, P], F32, name="bank_y")
+        nc.tensor.transpose(bank_gate[:], gate_rows[:], identity[:])
+        scopy(gate_cols[:, :TURNED], bank_gate[:, :TURNED])
         at1 = {e: B_AT[e % RING] for e in range(1, LAST - 1)}
         at3 = {e: A_AT[(e + 1) % RING] for e in range(LAST - 2)}
         at1[0] = A_AT[RING - 1]
@@ -215,13 +227,13 @@ def tile_moe_tk_glu_gelu_kernel(tc, xT, w1, w3, w2, gate, offs, pos1, pos2, pos3
                     load_w2(i, late_w2[:, i - FIRST_LATE])
                 load_w2(LAST, as_w2(y_all[:, 6 * C : 10 * C]))
                 nc.sync.dma_start(pos_t[0][:], pos1)
+                nc.sync.dma_start(pos_t[2][:], pos3)
                 round_w2(behind_copy(raw1[e + 1]), range(0, 1))
             if e == LAST - 1:
-                gate_t = ring.tile([P, TOP, T], F32, align_bytes=LINE, name="gate_t", offset=at3[e])
+                gate_t = ring.tile([P, 2, T], F32, align_bytes=LINE, name="gate_t", offset=at3[e])
                 nc.sync.dma_start(gate_t[:, 0, :], gate[0])
                 nc.sync.dma_start(pos_t[1][:], pos2)
-                nc.sync.dma_start(pos_t[2][:], pos3)
-                nc.sync.dma_start(gate_t[:, 1:, :], gate[1:].rearrange("r p t -> p r t"))
+                nc.sync.dma_start(gate_t[:, 1, :DIRECT], gate[1, :, :DIRECT])
                 round_w2(behind_copy(raw1[e + 1]), range(1, FIRST_LATE))
                 quantise_w2(range(1, 3))
 
@@ -268,31 +280,44 @@ def tile_moe_tk_glu_gelu_kernel(tc, xT, w1, w3, w2, gate, offs, pos1, pos2, pos3
         second_layer(range(8, LAST), vcopy)
         second_layer(range(LAST, E), scopy)
 
-        prods = [keep.tile([P, T], F32, align_bytes=64, name=f"prods{r}") for r in range(TOP)]
-        turned = keep.tile([P, T], F32, align_bytes=64, name="part")
+        first = keep.tile([P, T], F32, align_bytes=64, name="first")
+        second = keep.tile([P, T], F32, align_bytes=64, name="second")
+        third = keep.tile([P, T], F32, align_bytes=64, name="third")
+        turned = keep.tile([P, TURNED, P], F32, align_bytes=64, name="turned")
+        both = keep.tile([P, DIRECT], F32, align_bytes=64, name="both")
         result = keep.tile([P, T], F32, align_bytes=LINE, name="result")
-        sums = [psum.tile([P, T // 2], F32, name="bank_a") for half in range(2)]
 
-        def weighted(r, cols):
-            lists = pos_t[r][:, cols.start // 16 : cols.stop // 16]
-            nc.vector.tensor_tensor(prods[r][:, cols], y_all[:].indirect(lists), gate_t[:, r, cols], MULT)
+        def lists(r, cols):
+            return pos_t[r][:, cols.start // 16 : cols.stop // 16]
 
-        def sum_two(block):
+        def weighted(dst, r, cols):
+            nc.vector.tensor_tensor(dst[:, cols], y_all[:].indirect(lists(r, cols)), gate_t[:, r, cols], MULT)
+
+        def fetched(dst, r, cols):
+            nc.scalar.activation(dst[:, cols], y_all[:].indirect(lists(r, cols)), COPY)
+
+        pieces = [slice(0, 2 * P), slice(2 * P, DIRECT), slice(DIRECT, T)]
+        weighted(first, 0, slice(0, T))
+        weighted(second, 1, pieces[0])
+        weighted(second, 1, pieces[1])
+        fetched(third, 2, slice(0, T // 2))
+        fetched(third, 2, slice(T // 2, T))
+        fetched(second, 1, pieces[2])
+        sums = [psum.tile([P, piece.stop - piece.start], F32, name=name) for piece, name in zip(pieces, ("bank_a", "bank_a", "bank_b"))]
+        for block in range(BLOCKS):
             cols = slice(block * P, (block + 1) * P)
-            bank = psum_y.tile([P, P], F32, name="bank_y")
-            for r in range(2):
-                nc.tensor.matmul(bank[:], prods[r][:, cols], identity[:], start=r == 0, stop=r == 1, is_transpose=True)
-            scopy(turned[:, cols], bank[:])
-            nc.tensor.transpose(sums[block // 2][:, block % 2 * P : (block % 2 + 1) * P], turned[:, cols], identity[:])
-
-        weighted(0, slice(0, T))
-        for blocks in ((0, 1), (2,), (3,)):
-            weighted(1, slice(blocks[0] * P, (blocks[-1] + 1) * P))
-            for block in blocks:
-                sum_two(block)
-        halves = [slice(0, T // 2), slice(T // 2, T)]
-        for cols in halves:
-            weighted(2, cols)
-        for two, cols in zip(sums, halves):
-            nc.vector.tensor_tensor(result[:, cols], two[:], prods[2][:, cols], ADD)
+            items = [(third, block + 1)] + ([(second, 0)] if cols.start >= DIRECT else [])
+            bank = psum_y.tile([P, len(items), P], F32, name="bank_y")
+            for i, (values, column) in enumerate(items):
+                nc.tensor.transpose(bank[:, i, :], values[:, cols], identity[:])
+            for i, (values, column) in enumerate(items):
+                nc.scalar.activation(turned[:, column, :], bank[:, i, :], COPY, scale=gate_cols[:, column : column + 1])
+            piece = max(block - 1, 0)
+            at = cols.start - pieces[piece].start
+            for i, (values, column) in enumerate(items):
+                nc.tensor.matmul(sums[piece][:, at : at + P], turned[:, column, :], identity[:], start=i == 0, stop=i == len(items) - 1, is_transpose=True)
+        for cols in pieces[:2]:
+            nc.vector.tensor_tensor(both[:, cols], first[:, cols], second[:, cols], ADD)
+        for piece, cols in enumerate(pieces):
+            nc.vector.tensor_tensor(result[:, cols], sums[piece][:], (both if piece < 2 else first)[:, cols], ADD)
             nc.sync.dma_start(out[:, cols], result[:, cols])

@@ -25,19 +25,21 @@ TURNED = BLOCKS + (T - DIRECT) // P
 LAST = E - 1
 GATHER = 384
 X_SPLIT = 320
+AHEAD = 2
 SKEWED = 8
-LAST_SPLIT = 100
-FIRST_LATE = 5
+FIRST_LATE = 2
 
 LINE = 256
 MATRIX_BYTES = 4 * H * 4
 W2_BYTES = 4 * N * 4
-RING = 5
-A_FIRST = 6 * W2_BYTES - LINE
+RING_A, RING_B = 5, 7
+A_FIRST = 8 * W2_BYTES - LINE
 Y_AT = A_FIRST + LINE
-LAST_W3_AT = A_FIRST + MATRIX_BYTES - LINE
-A_AT = [A_FIRST] + [LAST_W3_AT + (1 + i) * MATRIX_BYTES for i in range(RING - 1)]
-B_AT = [A_AT[-1] + (1 + i) * MATRIX_BYTES for i in range(RING)]
+LAST_W2_AT = Y_AT + E * C * 4
+ACT_AT = LAST_W2_AT + W2_BYTES
+LAST_W3_AT = ACT_AT + 4 * C * 4
+A_AT = [A_FIRST] + [LAST_W3_AT + (1 + i) * MATRIX_BYTES for i in range(RING_A - 1)]
+B_AT = [A_AT[-1] + (1 + i) * MATRIX_BYTES for i in range(RING_B)]
 
 
 def tile_moe_tk_glu_gelu_kernel(tc, xT, w1, w3, w2, gate, offs, pos1, pos2, pos3, out):
@@ -47,11 +49,10 @@ def tile_moe_tk_glu_gelu_kernel(tc, xT, w1, w3, w2, gate, offs, pos1, pos2, pos3
         ring = ctx.enter_context(tc.tile_pool(name="ring", bufs=1))
         rounds = ctx.enter_context(tc.tile_pool(name="rounds", bufs=3))
         codes_pool = ctx.enter_context(tc.tile_pool(name="codes", bufs=3))
-        w2_pool = ctx.enter_context(tc.tile_pool(name="w2_codes", bufs=7))
+        w2_pool = ctx.enter_context(tc.tile_pool(name="w2_codes", bufs=8))
         h_pool = ctx.enter_context(tc.tile_pool(name="h_codes", bufs=E))
         slots = ctx.enter_context(tc.tile_pool(name="slots", bufs=E * C // GATHER))
         hidden = ctx.enter_context(tc.tile_pool(name="hidden", bufs=3))
-        held = ctx.enter_context(tc.tile_pool(name="held", bufs=1))
         placed = ctx.enter_context(tc.tile_pool(name="placed", bufs=1))
         psum = ctx.enter_context(tc.psum_pool(name="psum", bufs=2))
         psum_y = ctx.enter_context(tc.psum_pool(name="psum_y", bufs=4))
@@ -65,13 +66,14 @@ def tile_moe_tk_glu_gelu_kernel(tc, xT, w1, w3, w2, gate, offs, pos1, pos2, pos3
 
         vcopy, scopy = nc.vector.tensor_copy, nc.scalar.copy
         raw1, raw3, raw2 = {}, {}, {}
-        rounded2, w2_quantised, h_quantised = {}, {}, {}
+        w2_quantised, h_quantised = {}, {}
         banks_a, banks_b, acts = {}, {}, {}
 
-        def load(source, e, at, name):
-            tile = ring.tile([P, 4, H], F32, align_bytes=LINE, name=f"{name}_{e}", offset=at)
-            nc.sync.dma_start(tile[:], source[e].rearrange("(p j) i -> p j i", j=4))
-            return tile
+        def load(source, e, at, name, spare=0):
+            tile = ring.tile([P, 4 * H + spare], F32, align_bytes=LINE, name=f"{name}_{e}", offset=at)
+            rows = tile[:, : 4 * H].rearrange("p (j i) -> p j i", j=4)
+            nc.sync.dma_start(rows, source[e].rearrange("(p j) i -> p j i", j=4))
+            return rows
 
         def load_w2(e, place):
             raw2[e] = place
@@ -134,17 +136,27 @@ def tile_moe_tk_glu_gelu_kernel(tc, xT, w1, w3, w2, gate, offs, pos1, pos2, pos3
                 MULT,
             )
 
-        def round_w2(dst, experts, on_vector=None):
-            for i, e in enumerate(experts):
-                rounded2[e] = (dst, i)
-                interleave(vcopy if e == on_vector else scopy, dst[:, i * 4 * N : (i + 1) * 4 * N], raw2[e])
+        def round_half(copy, dst, src, half):
+            copy(
+                dst.rearrange("p (t m j) -> p m j t", t=2, j=4),
+                src.rearrange("p j (m t) -> p m j t", t=4)[:, :, :, 2 * half : 2 * half + 2],
+            )
 
-        def behind_copy(raw):
-            return raw[:, 1:4, :].rearrange("p j i -> p (j i)").bitcast(BF16)
+        def round_halves(dst, src):
+            round_half(vcopy, dst[:, : 2 * H], src, 0)
+            round_half(scopy, dst[:, 2 * H :], src, 1)
 
-        def quantise_w2(experts, codes=None):
-            src, at = rounded2[experts[0]]
-            quantised = quantise(src[:, at * 4 * N : (at + len(experts)) * 4 * N], "w2", w2_pool, codes)
+        def first_layer_halves(halves, e):
+            bank = psum.tile([P, 4, C], F32, name="bank_b")
+            piece, place = divmod(e * C, GATHER)
+            for half in range(2):
+                quantised = quantise(halves[half], "w13", codes_pool)
+                for t in range(2):
+                    product(bank[:, 2 * half + t, :], quantised, t * P, gathered[piece], place)
+            return bank
+
+        def quantise_w2(experts, src, codes=None):
+            quantised = quantise(src, "w2", w2_pool, codes)
             for i, e in enumerate(experts):
                 w2_quantised[e] = (quantised, i * N)
 
@@ -168,124 +180,153 @@ def tile_moe_tk_glu_gelu_kernel(tc, xT, w1, w3, w2, gate, offs, pos1, pos2, pos3
         bank_gate = psum_y.tile([P, P], F32, name="bank_y")
         nc.tensor.transpose(bank_gate[:], gate_rows[:], identity[:])
         scopy(gate_cols[:, :TURNED], bank_gate[:, :TURNED])
-        at1 = {e: B_AT[e % RING] for e in range(1, LAST - 1)}
-        at3 = {e: A_AT[(e + 1) % RING] for e in range(LAST - 2)}
-        at1[0] = A_AT[RING - 1]
-        at1[LAST - 1], at3[LAST - 2], at1[LAST], at3[LAST - 1] = A_AT[: RING - 1]
-        at3[LAST] = LAST_W3_AT
-        raw1[0] = load(w1, 0, at1[0], "raw1")
-        codes_w1 = {}
-        for e in range(LAST):
-            raw1[e + 1] = load(w1, e + 1, at1[e + 1], "raw1")
-            if e == LAST - 2:
-                first_w2 = ring.tile([P, 4, N], F32, align_bytes=LINE, name="raw2_first", offset=B_AT[0])
-                load_w2(0, first_w2[:])
-            raw3[e] = load(w3, e, at3[e], "raw3")
-            if e >= SKEWED:
-                codes_w1[e] = ring.tile([P, H], U32, align_bytes=LINE, name=f"codes_w1_{e}", offset=at3[e])
+        at1 = {e: B_AT[(e - 1) % RING_B] for e in range(1, E)}
+        at1[0] = A_AT[1]
+        at3 = {e: A_AT[(e + 2) % RING_A] for e in range(LAST)}
+        for e in range(AHEAD):
+            raw1[e] = load(w1, e, at1[e], "raw1")
+        for e in range(E - AHEAD):
+            raw1[e + AHEAD] = load(w1, e + AHEAD, at1[e + AHEAD], "raw1")
+            raw3[e] = load(w3, e, at3[e], "raw3", (LAST_W3_AT + LINE - A_FIRST - MATRIX_BYTES) // 4 if e == SKEWED else 0)
+        raw3[LAST - 1] = load(w3, LAST - 1, at3[LAST - 1], "raw3")
 
         interleave(vcopy, x_bf[:, : 4 * X_SPLIT], x_raw[:, :, :X_SPLIT])
         interleave(scopy, x_bf[:, 4 * X_SPLIT :], x_raw[:, :, X_SPLIT:])
         nc.vector.quantize_mx(out=x_codes[:].bitcast(FP8X4), scales=x_scales[:], in_=x_bf[:])
         gathered = [gather_tokens(piece) for piece in range(E * C // GATHER)]
 
-        rounded = rounds.tile([P, 4 * H], BF16, align_bytes=64, name="rounded")
-        interleave_hidden(scopy, rounded[:], raw1[0][:])
-        banks_a[0] = first_layer("bank_a", quantise(rounded[:], "w13", codes_pool), 0, 0)
-        for e in range(LAST):
+        rounded = rounds.tile([P, 8 * H], BF16, align_bytes=64, name="rounded")
+        for e in range(AHEAD):
+            interleave_hidden(scopy, rounded[:, e * 4 * H : (e + 1) * 4 * H], raw1[e])
+        quantised = quantise(rounded[:], "w13", codes_pool)
+        for e in range(AHEAD):
+            banks_a[e] = first_layer("bank_a", quantised, e * H, e)
+        for e in range(SKEWED + 1):
             rounded = rounds.tile([P, 8 * H], BF16, align_bytes=64, name="rounded")
-            interleave_hidden(scopy, rounded[:, : 4 * H], raw1[e + 1][:])
-            interleave_hidden(vcopy, rounded[:, 4 * H :], raw3[e][:])
-            acts[e] = raw1[e + 1][:, 0, :]
-            gelu(acts[e], banks_a[e])
-            if 0 < e <= SKEWED:
+            if e == SKEWED:
+                h_before = hidden.tile([P, 4 * C], BF16, align_bytes=64, name="hb")[:]
+                gated(h_before, acts[e - 1], banks_b[e - 1])
+            interleave_hidden(scopy, rounded[:, : 4 * H], raw1[e + AHEAD])
+            if e < SKEWED:
+                interleave_hidden(vcopy, rounded[:, 4 * H :], raw3[e])
+            else:
+                rounded_w3 = placed.tile([P, 4 * H], BF16, align_bytes=64, name="rounded_8", offset=4 * H * 2)
+                round_halves(rounded_w3[:], raw3[e])
+            for done in range(e + 1 if e else 0, e + 2):
+                acts[done] = raw1[e + AHEAD][:, e + 1 - done, :]
+                if e == SKEWED:
+                    acts[done] = ring.tile([P, 4 * C], F32, align_bytes=LINE, name="act_9", offset=ACT_AT)[:]
+                gelu(acts[done], banks_a[done])
+            if 0 < e < SKEWED:
                 h_before = raw3[e][:, 0, : 2 * C].bitcast(BF16)
                 gated(h_before, acts[e - 1], banks_b[e - 1])
             if e < SKEWED:
                 quantised = quantise(rounded[:], "w13", codes_pool)
                 banks_b[e] = first_layer("bank_b", quantised, H, e)
-                banks_a[e + 1] = first_layer("bank_a", quantised, 0, e + 1)
+                banks_a[e + AHEAD] = first_layer("bank_a", quantised, 0, e + AHEAD)
                 if e > 0:
                     h_quantised[e - 1] = quantise(h_before, "h", h_pool)
-                continue
 
-            banks_b[e] = first_layer("bank_b", quantise(rounded[:, 4 * H :], "w13", codes_pool), 0, e)
-            if e == SKEWED:
-                h_quantised[e - 1] = quantise(h_before, "h", h_pool)
-            banks_a[e + 1] = first_layer("bank_a", quantise(rounded[:, : 4 * H], "w13", codes_pool, codes_w1[e][:]), 0, e + 1)
+        h_quantised[7] = quantise(h_before, "h", h_pool)
+        banks_b[8] = first_layer("bank_b", quantise(rounded_w3[:], "w13", codes_pool), 0, 8)
+        codes_w1 = placed.tile([P, H], U32, align_bytes=64, name="codes_w1", offset=4 * H * 2)
+        banks_a[10] = first_layer("bank_a", quantise(rounded[:, : 4 * H], "w13", codes_pool, codes_w1[:]), 0, 10)
+        h_8 = hidden.tile([P, 4 * C], BF16, align_bytes=64, name="hb")
+        gated(h_8[:], acts[8], banks_b[8])
 
-            if e == LAST - 3:
-                early_w2 = ring.tile([P, 3, 4, N], F32, align_bytes=LINE, name="raw2_early", offset=at3[e])
-                for i in range(1, 4):
-                    load_w2(i, early_w2[:, i - 1])
-            if e == LAST - 2:
-                y_all = ring.tile([P, E * C], F32, align_bytes=LINE, name="y_all", offset=Y_AT)
-                load_w2(4, as_w2(y_all[:, : 4 * C]))
-                raw3[LAST] = load(w3, LAST, at3[LAST], "raw3")
-                late_w2 = ring.tile([P, LAST - FIRST_LATE, 4, N], F32, align_bytes=LINE, name="raw2_late", offset=0)
-                for i in range(FIRST_LATE, LAST):
-                    load_w2(i, late_w2[:, i - FIRST_LATE])
-                load_w2(LAST, as_w2(y_all[:, 6 * C : 10 * C]))
-                nc.sync.dma_start(pos_t[0][:], pos1)
-                nc.sync.dma_start(pos_t[2][:], pos3)
-                round_w2(behind_copy(raw1[e + 1]), range(0, 1))
-            if e == LAST - 1:
-                gate_t = ring.tile([P, 2, T], F32, align_bytes=LINE, name="gate_t", offset=at3[e])
-                nc.sync.dma_start(gate_t[:, 0, :], gate[0])
-                nc.sync.dma_start(pos_t[1][:], pos2)
-                nc.sync.dma_start(gate_t[:, 1, :DIRECT], gate[1, :, :DIRECT])
-                round_w2(behind_copy(raw1[e + 1]), range(1, FIRST_LATE))
-                quantise_w2(range(1, 3))
+        early_w2 = ring.tile([P, FIRST_LATE, 4, N], F32, align_bytes=LINE, name="raw2_early", offset=at3[7])
+        for e in range(FIRST_LATE):
+            load_w2(e, early_w2[:, e])
+        raw3[LAST] = load(w3, LAST, LAST_W3_AT, "raw3")
+        y_all = ring.tile([P, E * C], F32, align_bytes=LINE, name="y_all", offset=Y_AT)
+        late_w2 = ring.tile([P, 8, 4, N], F32, align_bytes=LINE, name="raw2_late", offset=0)
+        last_w2 = ring.tile([P, 4, N], F32, align_bytes=LINE, name="raw2_last", offset=LAST_W2_AT)
+        places = {e: late_w2[:, e - FIRST_LATE] for e in range(FIRST_LATE, 10)}
+        places[10], places[LAST] = as_w2(y_all[:, : 4 * C]), last_w2[:]
+        for e in range(FIRST_LATE, E):
+            load_w2(e, places[e])
 
-            h_own = hidden.tile([P, 4 * C], BF16, align_bytes=64, name="hb")
-            gated(h_own[:], acts[e], banks_b[e])
-            if e == LAST - 2:
-                quantise_w2(range(0, 1))
-            if e == LAST - 1:
-                quantise_w2(range(3, 4))
-            h_quantised[e] = quantise(h_own[:], "h", h_pool)
-
-        act_last = held.tile([P, 4 * C], F32, align_bytes=64, name="act_last", tag="chain_act")
+        rounded = rounds.tile([P, 4 * H], BF16, align_bytes=64, name="rounded")
+        interleave_hidden(scopy, rounded[:], raw1[LAST])
+        rounded_w3 = ring.tile([P, 4 * H], BF16, align_bytes=LINE, name="rounded_9", offset=at1[9])
+        round_halves(rounded_w3[:], raw3[9])
+        h_quantised[8] = quantise(h_8[:], "h", h_pool)
+        acts[10] = ring.tile([P, 4 * C], F32, align_bytes=LINE, name="act_10", offset=at3[9] + MATRIX_BYTES // 2 - LINE)[:]
+        gelu(acts[10], banks_a[10])
+        banks_b[9] = first_layer_halves([rounded_w3[:, : 2 * H], rounded_w3[:, 2 * H :]], 9)
+        banks_a[LAST] = first_layer("bank_a", quantise(rounded[:], "w13", codes_pool), 0, LAST)
+        rounded_w3 = placed.tile([P, 4 * H], BF16, align_bytes=64, name="rounded_10", offset=4 * H * 2)
+        round_halves(rounded_w3[:], raw3[10])
+        act_last = ring.tile([P, 4 * C], F32, align_bytes=LINE, name="act_last", offset=at3[10])
+        early = ring.tile([P, FIRST_LATE, 4 * N], BF16, align_bytes=LINE, name="rounded_early", offset=at3[10] + MATRIX_BYTES // 2)
+        interleave(scopy, early[:, 0, :], raw2[0])
         gelu(act_last[:], banks_a[LAST])
+        interleave(scopy, early[:, 1, :], raw2[1])
+        banks_b[10] = first_layer_halves([rounded_w3[:, : 2 * H], rounded_w3[:, 2 * H :]], 10)
+        h_9 = placed.tile([P, 4 * C], BF16, align_bytes=64, name="h_9", offset=4 * H * 2)
+        gated(h_9[:], acts[9], banks_b[9])
+        quantise_w2([0], early[:, 0, :])
+        h_quantised[9] = quantise(h_9[:], "h", h_pool)
+        h_10 = hidden.tile([P, 4 * C], BF16, align_bytes=64, name="hb")
+        gated(h_10[:], acts[10], banks_b[10])
 
-        rounded_last = placed.tile([P, 4 * H], BF16, align_bytes=64, name="rounded_last", offset=0)
-        interleave_hidden(vcopy, rounded_last[:], raw3[LAST][:], ts=slice(0, 2))
-        interleave_hidden(vcopy, rounded_last[:], raw3[LAST][:], slice(0, LAST_SPLIT), slice(2, 4))
-        interleave_hidden(scopy, rounded_last[:], raw3[LAST][:], slice(LAST_SPLIT, P), slice(2, 4))
-        bank_last = psum.tile([P, 4, C], F32, name="bank_b")
-        piece, place = divmod(LAST * C, GATHER)
-        for half in range(2):
-            quantised = quantise(rounded_last[:, half * 2 * H : (half + 1) * 2 * H], "w13", codes_pool)
-            for t in range(2):
-                product(bank_last[:, 2 * half + t, :], quantised, t * P, gathered[piece], place)
+        gate_t = ring.tile([P, 2, T], F32, align_bytes=LINE, name="gate_t", offset=at3[9])
+        nc.sync.dma_start(pos_t[0][:], pos1)
+        nc.sync.dma_start(pos_t[2][:], pos3)
+        nc.sync.dma_start(gate_t[:, 0, :], gate[0])
+        nc.sync.dma_start(pos_t[1][:], pos2)
+        nc.sync.dma_start(gate_t[:, 1, :DIRECT], gate[1, :, :DIRECT])
 
-        codes_4 = ring.tile([P, N], U32, align_bytes=LINE, name="codes_a", offset=at3[LAST])
-        quantise_w2(range(4, 5), codes_4[:])
-        rounded_late = held.tile([P, 5 * 4 * N], BF16, align_bytes=64, name="rounded_late")
-        round_w2(rounded_late[:], range(5, 7))
-        codes_56 = placed.tile([P, 2 * N], U32, align_bytes=64, name="codes_b", offset=0)
-        quantise_w2(range(5, 7), codes_56[:])
-        rounded_78 = placed.tile([P, 2 * 4 * N], BF16, align_bytes=64, name="rounded_pair", offset=W2_BYTES)
-        round_w2(rounded_78[:], range(7, 9), on_vector=7)
-        round_w2(rounded_late[:, 2 * 4 * N :], range(9, E))
+        halves = [
+            ring.tile([P, 2 * H], BF16, align_bytes=LINE, name="rounded_last_0", offset=at3[9] + MATRIX_BYTES // 2)[:],
+            ring.tile([P, 2 * H], BF16, align_bytes=LINE, name="rounded_last_1", offset=at3[7])[:],
+        ]
+        round_half(vcopy, halves[0], raw3[LAST], 0)
+        round_half(scopy, halves[1], raw3[LAST], 1)
+        h_quantised[10] = quantise(h_10[:], "h", h_pool)
+        bank_last = first_layer_halves(halves, LAST)
+
+        late = ring.tile([P, 3, 4 * N], BF16, align_bytes=LINE, name="rounded_late", offset=at3[7] + W2_BYTES)
+        pair = ring.tile([P, 2, 4 * N], BF16, align_bytes=LINE, name="rounded_pair", offset=at3[7])
+        pair_78 = y_all[:, 6 * C : 10 * C].bitcast(BF16)
+
+        def flat(rows):
+            return rows.rearrange("p e c -> p (e c)")
+
+        interleave(scopy, late[:, 0, :], raw2[2])
+        interleave(scopy, late[:, 1, :], raw2[3])
+        interleave(scopy, pair[:, 1, :], raw2[5])
+        interleave(scopy, pair_78[:, : 4 * N], raw2[7])
+        interleave(scopy, pair_78[:, 4 * N :], raw2[8])
+        quantise_w2([1], early[:, 1, :])
+        interleave(vcopy, pair[:, 0, :], raw2[4])
+        quantise_w2([2, 3], flat(late[:, :2, :]))
         h_last = hidden.tile([P, 4 * C], BF16, align_bytes=64, name="hb")
         gated(h_last[:], act_last[:], bank_last)
-        codes_late = held.tile([P, 5 * N], U32, align_bytes=64, name="codes_c", tag="chain_act")
-        quantise_w2(range(7, 9), codes_late[:, : 2 * N])
+        codes_late = ring.tile([P, 7 * N], U32, align_bytes=LINE, name="codes_c", offset=at3[10])
+        quantise_w2([4, 5], flat(pair[:]), codes_late[:, : 2 * N])
         h_quantised[LAST] = quantise(h_last[:], "h", h_pool)
-        for e in range(9, E):
-            quantise_w2(range(e, e + 1), codes_late[:, (e - 7) * N : (e - 6) * N])
+        interleave(vcopy, pair[:, 0, :], raw2[6])
+        interleave(scopy, pair[:, 1, :], raw2[9])
+        interleave(scopy, late[:, 2, :], raw2[10])
+        quantise_w2([7, 8], pair_78, codes_late[:, 2 * N : 4 * N])
+        quantise_w2([6, 9], flat(pair[:]), codes_late[:, 4 * N : 6 * N])
+        interleave(vcopy, pair_78[:, 4 * N :], raw2[LAST])
+        codes_10 = ring.tile([P, N], U32, align_bytes=LINE, name="codes_d", offset=LAST_W2_AT)
+        quantise_w2([10], late[:, 2, :], codes_10[:])
+        quantise_w2([LAST], pair_78[:, 4 * N :], codes_late[:, 6 * N :])
         second_layer(range(0, 4), scopy)
         second_layer(range(4, 8), scopy)
-        second_layer(range(8, LAST), vcopy)
+        second_layer(range(8, 10), vcopy)
+        second_layer(range(10, LAST), scopy)
         second_layer(range(LAST, E), scopy)
 
         first = keep.tile([P, T], F32, align_bytes=64, name="first")
         second = keep.tile([P, T], F32, align_bytes=64, name="second")
         third = keep.tile([P, T], F32, align_bytes=64, name="third")
         turned = keep.tile([P, TURNED, P], F32, align_bytes=64, name="turned")
-        both = keep.tile([P, DIRECT], F32, align_bytes=64, name="both")
-        result = keep.tile([P, T], F32, align_bytes=LINE, name="result")
+        both = keep.tile([P, DIRECT], F32, align_bytes=LINE, name="both")
+        result = keep.tile([P, DIRECT], F32, align_bytes=LINE, name="result")
 
         def lists(r, cols):
             return pos_t[r][:, cols.start // 16 : cols.stop // 16]
@@ -303,21 +344,28 @@ def tile_moe_tk_glu_gelu_kernel(tc, xT, w1, w3, w2, gate, offs, pos1, pos2, pos3
         fetched(third, 2, slice(0, T // 2))
         fetched(third, 2, slice(T // 2, T))
         fetched(second, 1, pieces[2])
-        sums = [psum.tile([P, piece.stop - piece.start], F32, name=name) for piece, name in zip(pieces, ("bank_a", "bank_a", "bank_b"))]
-        for block in range(BLOCKS):
-            cols = slice(block * P, (block + 1) * P)
-            items = [(third, block + 1)] + ([(second, 0)] if cols.start >= DIRECT else [])
-            bank = psum_y.tile([P, len(items), P], F32, name="bank_y")
-            for i, (values, column) in enumerate(items):
-                nc.tensor.transpose(bank[:, i, :], values[:, cols], identity[:])
-            for i, (values, column) in enumerate(items):
-                nc.scalar.activation(turned[:, column, :], bank[:, i, :], COPY, scale=gate_cols[:, column : column + 1])
-            piece = max(block - 1, 0)
-            at = cols.start - pieces[piece].start
-            for i, (values, column) in enumerate(items):
-                nc.tensor.matmul(sums[piece][:, at : at + P], turned[:, column, :], identity[:], start=i == 0, stop=i == len(items) - 1, is_transpose=True)
         for cols in pieces[:2]:
             nc.vector.tensor_tensor(both[:, cols], first[:, cols], second[:, cols], ADD)
+        sums = [psum.tile([P, piece.stop - piece.start], F32, name=name) for piece, name in zip(pieces, ("bank_a", "bank_a", "bank_b"))]
+        items = [(third, block, block + 1) for block in range(BLOCKS)] + [(second, BLOCKS - 1, 0)]
+        banks = [psum_y.tile([P, P], F32, name="bank_y") for block in range(BLOCKS)] + [psum.tile([P, P], F32, name="bank_b")]
+        for bank, (values, block, column) in zip(banks, items):
+            nc.tensor.transpose(bank[:], values[:, block * P : (block + 1) * P], identity[:])
+        for bank, (values, block, column) in zip(banks, items):
+            nc.scalar.activation(turned[:, column, :], bank[:], COPY, scale=gate_cols[:, column : column + 1])
+        for values, block, column in items:
+            piece = max(block - 1, 0)
+            at = block * P - pieces[piece].start
+            alone = block < BLOCKS - 1
+            nc.tensor.matmul(
+                sums[piece][:, at : at + P],
+                turned[:, column, :],
+                identity[:],
+                start=values is third,
+                stop=alone or values is second,
+                is_transpose=True,
+            )
+        finished = [result[:, pieces[0]], result[:, pieces[1]], both[:, pieces[1]]]
         for piece, cols in enumerate(pieces):
-            nc.vector.tensor_tensor(result[:, cols], sums[piece][:], (both if piece < 2 else first)[:, cols], ADD)
-            nc.sync.dma_start(out[:, cols], result[:, cols])
+            nc.vector.tensor_tensor(finished[piece], sums[piece][:], (both if piece < 2 else first)[:, cols], ADD)
+            nc.sync.dma_start(out[:, cols], finished[piece])

@@ -365,7 +365,7 @@ def tile_moe_tk_glu_gelu_kernel(tc, xT, w1, w3, w2, gate, offs, pos1, pos2, pos3
                 stop=alone or values is second,
                 is_transpose=True,
             )
-        finished = [result[:, pieces[0]], result[:, pieces[1]], both[:, pieces[1]]]
+        finished = [result[:, pieces[0]], result[:, pieces[1]], both[:, :P]]
         for piece, cols in enumerate(pieces):
             nc.vector.tensor_tensor(finished[piece], sums[piece][:], (both if piece < 2 else first)[:, cols], ADD)
             nc.sync.dma_start(out[:, cols], finished[piece])

@@ -27,6 +27,7 @@ GATHER = 384
 X_SPLIT = 320
 AHEAD = 2
 SKEWED = 8
+LAST_SPLIT = 56
 FIRST_LATE = 2
 
 LINE = 256
@@ -160,8 +161,8 @@ def tile_moe_tk_glu_gelu_kernel(tc, xT, w1, w3, w2, gate, offs, pos1, pos2, pos3
             for i, e in enumerate(experts):
                 w2_quantised[e] = (quantised, i * N)
 
-        def second_layer(experts, copy):
-            bank = psum_y.tile([P, len(experts), C], F32, name="bank_y")
+        def second_layer(experts, copy, pool=psum_y, name="bank_y"):
+            bank = pool.tile([P, len(experts), C], F32, name=name)
             for i, e in enumerate(experts):
                 product(bank[:, i, :], w2_quantised[e][0], w2_quantised[e][1], h_quantised[e], 0)
             copy(y_all[:].rearrange("p (e n) -> p e n", n=C)[:, experts.start : experts.stop, :], bank[:])
@@ -303,7 +304,7 @@ def tile_moe_tk_glu_gelu_kernel(tc, xT, w1, w3, w2, gate, offs, pos1, pos2, pos3
         quantise_w2([2, 3], flat(late[:, :2, :]))
         h_last = hidden.tile([P, 4 * C], BF16, align_bytes=64, name="hb")
         gated(h_last[:], act_last[:], bank_last)
-        codes_late = ring.tile([P, 7 * N], U32, align_bytes=LINE, name="codes_c", offset=at3[10])
+        codes_late = ring.tile([P, 8 * N], U32, align_bytes=LINE, name="codes_c", offset=at3[10])
         quantise_w2([4, 5], flat(pair[:]), codes_late[:, : 2 * N])
         h_quantised[LAST] = quantise(h_last[:], "h", h_pool)
         interleave(vcopy, pair[:, 0, :], raw2[6])
@@ -311,15 +312,15 @@ def tile_moe_tk_glu_gelu_kernel(tc, xT, w1, w3, w2, gate, offs, pos1, pos2, pos3
         interleave(scopy, late[:, 2, :], raw2[10])
         quantise_w2([7, 8], pair_78, codes_late[:, 2 * N : 4 * N])
         quantise_w2([6, 9], flat(pair[:]), codes_late[:, 4 * N : 6 * N])
-        interleave(vcopy, pair_78[:, 4 * N :], raw2[LAST])
-        codes_10 = ring.tile([P, N], U32, align_bytes=LINE, name="codes_d", offset=LAST_W2_AT)
-        quantise_w2([10], late[:, 2, :], codes_10[:])
-        quantise_w2([LAST], pair_78[:, 4 * N :], codes_late[:, 6 * N :])
+        interleave(vcopy, pair_78[:, 4 * N : 4 * (N + LAST_SPLIT)], raw2[LAST][:, :, :LAST_SPLIT])
+        interleave(scopy, pair_78[:, 4 * (N + LAST_SPLIT) :], raw2[LAST][:, :, LAST_SPLIT:])
+        quantise_w2([10], late[:, 2, :], codes_late[:, 7 * N :])
+        quantise_w2([LAST], pair_78[:, 4 * N :], codes_late[:, 6 * N : 7 * N])
         second_layer(range(0, 4), scopy)
-        second_layer(range(4, 8), scopy)
-        second_layer(range(8, 10), vcopy)
+        second_layer(range(4, 7), scopy)
+        second_layer(range(7, 10), vcopy)
         second_layer(range(10, LAST), scopy)
-        second_layer(range(LAST, E), scopy)
+        second_layer(range(LAST, E), scopy, psum, "bank_a")
 
         first = keep.tile([P, T], F32, align_bytes=64, name="first")
         second = keep.tile([P, T], F32, align_bytes=64, name="second")

@@ -176,16 +176,16 @@ def tile_moe_tk_glu_gelu_kernel(tc, xT, w1, w3, w2, gate, offs, pos1, pos2, pos3
 
         nc.sync.dma_start(x_raw[:], xT.rearrange("(p j) t -> p j t", j=4))
         nc.sync.dma_start(offs_t[:], offs)
-        rows = gate.rearrange("r p (b t) -> (r p b) t", t=P)
-        nc.sync.dma_start(gate_rows[:TURNED, :], rows[(TOP * BLOCKS - TURNED) * (P + 1) :: P + 1, :])
-        bank_gate = psum_y.tile([P, P], F32, name="bank_y")
-        nc.tensor.transpose(bank_gate[:], gate_rows[:], identity[:])
-        scopy(gate_cols[:, :TURNED], bank_gate[:, :TURNED])
         at1 = {e: B_AT[(e - 1) % RING_B] for e in range(1, E)}
         at1[0] = A_AT[1]
         at3 = {e: A_AT[(e + 2) % RING_A] for e in range(LAST)}
         for e in range(AHEAD):
             raw1[e] = load(w1, e, at1[e], "raw1")
+        rows = gate.rearrange("r p (b t) -> (r p b) t", t=P)
+        nc.sync.dma_start(gate_rows[:TURNED, :], rows[(TOP * BLOCKS - TURNED) * (P + 1) :: P + 1, :])
+        bank_gate = psum_y.tile([P, P], F32, name="bank_y")
+        nc.tensor.transpose(bank_gate[:], gate_rows[:], identity[:])
+        scopy(gate_cols[:, :TURNED], bank_gate[:, :TURNED])
         for e in range(E - AHEAD):
             raw1[e + AHEAD] = load(w1, e + AHEAD, at1[e + AHEAD], "raw1")
             raw3[e] = load(w3, e, at3[e], "raw3", (LAST_W3_AT + LINE - A_FIRST - MATRIX_BYTES) // 4 if e == SKEWED else 0)

from contextlib import ExitStack

import concourse.mybir as mybir
from concourse.masks import make_identity

K, T, E, C, H, N = 512, 512, 12, 128, 512, 128
TOP = 3
FLOPS = 2 * E * C * (2 * K * H + H * N)

P = 128
F32 = mybir.dt.float32
BF16 = mybir.dt.bfloat16
U32 = mybir.dt.uint32
U16 = mybir.dt.uint16
U8 = mybir.dt.uint8
FP8X4 = mybir.dt.float8_e4m3fn_x4
MULT = mybir.AluOpType.mult
ADD = mybir.AluOpType.add
GELU = mybir.ActivationFunctionType.Gelu_apprx_tanh
COPY = mybir.ActivationFunctionType.Copy
BLOCKS = T // P
DIRECT = 384
TURNED = BLOCKS + (T - DIRECT) // P

LAST = E - 1
GATHER = 384
X_SPLIT = 320
AHEAD = 2
SKEWED = 8
LAST_SPLIT = 56
FIRST_LATE = 2

LINE = 256
MATRIX_BYTES = 4 * H * 4
W2_BYTES = 4 * N * 4
RING_A, RING_B = 5, 7
A_FIRST = 8 * W2_BYTES - LINE
Y_AT = A_FIRST + LINE
LAST_W2_AT = Y_AT + E * C * 4
ACT_AT = LAST_W2_AT + W2_BYTES
LAST_W3_AT = ACT_AT + 4 * C * 4
A_AT = [A_FIRST] + [LAST_W3_AT + (1 + i) * MATRIX_BYTES for i in range(RING_A - 1)]
B_AT = [A_AT[-1] + (1 + i) * MATRIX_BYTES for i in range(RING_B)]


def tile_moe_tk_glu_gelu_kernel(tc, xT, w1, w3, w2, gate, offs, pos1, pos2, pos3, out):
    nc = tc.nc
    with ExitStack() as ctx:
        keep = ctx.enter_context(tc.tile_pool(name="keep", bufs=1))
        ring = ctx.enter_context(tc.tile_pool(name="ring", bufs=1))
        rounds = ctx.enter_context(tc.tile_pool(name="rounds", bufs=3))
        codes_pool = ctx.enter_context(tc.tile_pool(name="codes", bufs=3))
        w2_pool = ctx.enter_context(tc.tile_pool(name="w2_codes", bufs=8))
        h_pool = ctx.enter_context(tc.tile_pool(name="h_codes", bufs=E))
        slots = ctx.enter_context(tc.tile_pool(name="slots", bufs=E * C // GATHER))
        hidden = ctx.enter_context(tc.tile_pool(name="hidden", bufs=3))
        placed = ctx.enter_context(tc.tile_pool(name="placed", bufs=1))
        psum = ctx.enter_context(tc.psum_pool(name="psum", bufs=2))
        psum_y = ctx.enter_context(tc.psum_pool(name="psum_y", bufs=4))

        offs_t = keep.tile([P, E * C // 16], U16, name="offs_t")
        pos_t = [keep.tile([P, T // 16], U16, name=f"pos_t{r}") for r in range(TOP)]
        x_raw = ring.tile([P, 4, T], F32, align_bytes=LINE, name="x_raw", offset=A_AT[0])
        x_bf = rounds.tile([P, T * 4], BF16, align_bytes=64, name="x_bf", tag="rounded")
        x_codes = keep.tile([P, T], U32, align_bytes=64, name="x_codes")
        x_scales = keep.tile([P, T], U8, align_bytes=64, name="x_scales")

        vcopy, scopy = nc.vector.tensor_copy, nc.scalar.copy
        raw1, raw3, raw2 = {}, {}, {}
        w2_quantised, h_quantised = {}, {}
        banks_a, banks_b, acts = {}, {}, {}

        def load(source, e, at, name, spare=0):
            tile = ring.tile([P, 4 * H + spare], F32, align_bytes=LINE, name=f"{name}_{e}", offset=at)
            rows = tile[:, : 4 * H].rearrange("p (j i) -> p j i", j=4)
            nc.sync.dma_start(rows, source[e].rearrange("(p j) i -> p j i", j=4))
            return rows

        def load_w2(e, place):
            raw2[e] = place
            nc.sync.dma_start(place, w2[e].rearrange("(p j) n -> p j n", j=4))

        def as_w2(columns):
            return columns.rearrange("p (j n) -> p j n", j=4)

        def interleave_hidden(copy, dst, src, ms=slice(0, P), ts=slice(0, 4)):
            copy(
                dst.rearrange("p (t m j) -> p m j t", t=4, j=4)[:, ms, :, ts],
                src.rearrange("p j (m t) -> p m j t", t=4)[:, ms, :, ts],
            )

        def interleave(copy, dst, src):
            copy(dst.rearrange("p (c i j) -> p c j i", i=4, j=4), src.rearrange("p j (c i) -> p c j i", i=4))

        def quantise(src, tag, pool, codes=None):
            width = src.shape[1] // 4
            if codes is None:
                codes = pool.tile([P, width], U32, align_bytes=64, name=f"codes_{tag}")[:]
            scales = pool.tile([P, width], U8, align_bytes=64, name=f"scales_{tag}")
            nc.vector.quantize_mx(out=codes.bitcast(FP8X4), scales=scales[:], in_=src)
            return codes, scales

        def product(bank, stationary, at, moving, start):
            nc.tensor.matmul_mx(
                out=bank,
                lhsT=stationary[0][:, at : at + P].bitcast(FP8X4),
                lhsT_scale=stationary[1][:, at : at + P],
                rhs=moving[0][:, start : start + C].bitcast(FP8X4),
                rhs_scale=moving[1][:, start : start + C],
                start=True,
                stop=True,
            )

        def gather_tokens(piece):
            lists = offs_t[:, piece * GATHER // 16 : (piece + 1) * GATHER // 16]
            g_codes = slots.tile([P, GATHER], U32, align_bytes=64, name="g_codes")
            g_scales = slots.tile([P, GATHER], U8, align_bytes=64, name="g_scales")
            vcopy(g_codes[:], x_codes[:].indirect(lists))
            vcopy(g_scales[:], x_scales[:].indirect(lists))
            return g_codes, g_scales

        def first_layer(name, quantised, at, e):
            bank = psum.tile([P, 4, C], F32, name=name)
            piece, place = divmod(e * C, GATHER)
            for t in range(4):
                product(bank[:, t, :], quantised, at + t * P, gathered[piece], place)
            return bank

        def gelu(act, bank):
            nc.scalar.activation(act.rearrange("p (n t) -> p n t", t=4), bank[:].rearrange("p t n -> p n t"), GELU)

        def gated(hb, act, bank):
            nc.vector.tensor_tensor(
                hb.rearrange("p (n t) -> p n t", t=4),
                act.rearrange("p (n t) -> p n t", t=4),
                bank[:].rearrange("p t n -> p n t"),
                MULT,
            )

        def round_half(copy, dst, src, half):
            copy(
                dst.rearrange("p (t m j) -> p m j t", t=2, j=4),
                src.rearrange("p j (m t) -> p m j t", t=4)[:, :, :, 2 * half : 2 * half + 2],
            )

        def round_halves(dst, src):
            round_half(vcopy, dst[:, : 2 * H], src, 0)
            round_half(scopy, dst[:, 2 * H :], src, 1)

        def first_layer_halves(halves, e):
            bank = psum.tile([P, 4, C], F32, name="bank_b")
            piece, place = divmod(e * C, GATHER)
            for half in range(2):
                quantised = quantise(halves[half], "w13", codes_pool)
                for t in range(2):
                    product(bank[:, 2 * half + t, :], quantised, t * P, gathered[piece], place)
            return bank

        def quantise_w2(experts, src, codes=None):
            quantised = quantise(src, "w2", w2_pool, codes)
            for i, e in enumerate(experts):
                w2_quantised[e] = (quantised, i * N)

        def second_layer(experts, copy, pool=psum_y, name="bank_y"):
            bank = pool.tile([P, len(experts), C], F32, name=name)
            for i, e in enumerate(experts):
                product(bank[:, i, :], w2_quantised[e][0], w2_quantised[e][1], h_quantised[e], 0)
            copy(y_all[:].rearrange("p (e n) -> p e n", n=C)[:, experts.start : experts.stop, :], bank[:])

        nc.gpsimd.memset(x_scales[:], 0)
        identity = keep.tile([P, P], F32, align_bytes=64, name="identity")
        make_identity(nc, identity[:])
        gate_rows = keep.tile([P, P], F32, align_bytes=LINE, name="gate_rows")
        gate_cols = keep.tile([P, 8], F32, align_bytes=64, name="gate_cols")
        nc.gpsimd.memset(gate_rows[:], 0)

        nc.sync.dma_start(x_raw[:], xT.rearrange("(p j) t -> p j t", j=4))
        nc.sync.dma_start(offs_t[:], offs)
        at1 = {e: B_AT[(e - 1) % RING_B] for e in range(1, E)}
        at1[0] = A_AT[1]
        at3 = {e: A_AT[(e + 2) % RING_A] for e in range(LAST)}
        for e in range(AHEAD):
            raw1[e] = load(w1, e, at1[e], "raw1")
        rows = gate.rearrange("r p (b t) -> (r p b) t", t=P)
        nc.sync.dma_start(gate_rows[:TURNED, :], rows[(TOP * BLOCKS - TURNED) * (P + 1) :: P + 1, :])
        bank_gate = psum_y.tile([P, P], F32, name="bank_y")
        nc.tensor.transpose(bank_gate[:], gate_rows[:], identity[:])
        scopy(gate_cols[:, :TURNED], bank_gate[:, :TURNED])
        for e in range(E - AHEAD):
            raw1[e + AHEAD] = load(w1, e + AHEAD, at1[e + AHEAD], "raw1")
            raw3[e] = load(w3, e, at3[e], "raw3", (LAST_W3_AT + LINE - A_FIRST - MATRIX_BYTES) // 4 if e == SKEWED else 0)
        raw3[LAST - 1] = load(w3, LAST - 1, at3[LAST - 1], "raw3")

        interleave(vcopy, x_bf[:, : 4 * X_SPLIT], x_raw[:, :, :X_SPLIT])
        interleave(scopy, x_bf[:, 4 * X_SPLIT :], x_raw[:, :, X_SPLIT:])
        nc.vector.quantize_mx(out=x_codes[:].bitcast(FP8X4), scales=x_scales[:], in_=x_bf[:])
        gathered = [gather_tokens(piece) for piece in range(E * C // GATHER)]

        rounded = rounds.tile([P, 8 * H], BF16, align_bytes=64, name="rounded")
        for e in range(AHEAD):
            interleave_hidden(scopy, rounded[:, e * 4 * H : (e + 1) * 4 * H], raw1[e])
        quantised = quantise(rounded[:], "w13", codes_pool)
        for e in range(AHEAD):
            banks_a[e] = first_layer("bank_a", quantised, e * H, e)
        for e in range(SKEWED + 1):
            rounded = rounds.tile([P, 8 * H], BF16, align_bytes=64, name="rounded")
            if e == SKEWED:
                h_before = hidden.tile([P, 4 * C], BF16, align_bytes=64, name="hb")[:]
                gated(h_before, acts[e - 1], banks_b[e - 1])
            interleave_hidden(scopy, rounded[:, : 4 * H], raw1[e + AHEAD])
            if e < SKEWED:
                interleave_hidden(vcopy, rounded[:, 4 * H :], raw3[e])
            else:
                rounded_w3 = placed.tile([P, 4 * H], BF16, align_bytes=64, name="rounded_8", offset=4 * H * 2)
                round_halves(rounded_w3[:], raw3[e])
            for done in range(e + 1 if e else 0, e + 2):
                acts[done] = raw1[e + AHEAD][:, e + 1 - done, :]
                if e == SKEWED:
                    acts[done] = ring.tile([P, 4 * C], F32, align_bytes=LINE, name="act_9", offset=ACT_AT)[:]
                gelu(acts[done], banks_a[done])
            if 0 < e < SKEWED:
                h_before = raw3[e][:, 0, : 2 * C].bitcast(BF16)
                gated(h_before, acts[e - 1], banks_b[e - 1])
            if e < SKEWED:
                quantised = quantise(rounded[:], "w13", codes_pool)
                banks_b[e] = first_layer("bank_b", quantised, H, e)
                banks_a[e + AHEAD] = first_layer("bank_a", quantised, 0, e + AHEAD)
                if e > 0:
                    h_quantised[e - 1] = quantise(h_before, "h", h_pool)

        h_quantised[7] = quantise(h_before, "h", h_pool)
        banks_b[8] = first_layer("bank_b", quantise(rounded_w3[:], "w13", codes_pool), 0, 8)
        codes_w1 = placed.tile([P, H], U32, align_bytes=64, name="codes_w1", offset=4 * H * 2)
        banks_a[10] = first_layer("bank_a", quantise(rounded[:, : 4 * H], "w13", codes_pool, codes_w1[:]), 0, 10)
        h_8 = hidden.tile([P, 4 * C], BF16, align_bytes=64, name="hb")
        gated(h_8[:], acts[8], banks_b[8])

        early_w2 = ring.tile([P, FIRST_LATE, 4, N], F32, align_bytes=LINE, name="raw2_early", offset=at3[7])
        for e in range(FIRST_LATE):
            load_w2(e, early_w2[:, e])
        raw3[LAST] = load(w3, LAST, LAST_W3_AT, "raw3")
        y_all = ring.tile([P, E * C], F32, align_bytes=LINE, name="y_all", offset=Y_AT)
        late_w2 = ring.tile([P, 8, 4, N], F32, align_bytes=LINE, name="raw2_late", offset=0)
        last_w2 = ring.tile([P, 4, N], F32, align_bytes=LINE, name="raw2_last", offset=LAST_W2_AT)
        places = {e: late_w2[:, e - FIRST_LATE] for e in range(FIRST_LATE, 10)}
        places[10], places[LAST] = as_w2(y_all[:, : 4 * C]), last_w2[:]
        for e in range(FIRST_LATE, E):
            load_w2(e, places[e])

        rounded = rounds.tile([P, 4 * H], BF16, align_bytes=64, name="rounded")
        interleave_hidden(scopy, rounded[:], raw1[LAST])
        rounded_w3 = ring.tile([P, 4 * H], BF16, align_bytes=LINE, name="rounded_9", offset=at1[9])
        round_halves(rounded_w3[:], raw3[9])
        h_quantised[8] = quantise(h_8[:], "h", h_pool)
        acts[10] = ring.tile([P, 4 * C], F32, align_bytes=LINE, name="act_10", offset=at3[9] + MATRIX_BYTES // 2 - LINE)[:]
        gelu(acts[10], banks_a[10])
        banks_b[9] = first_layer_halves([rounded_w3[:, : 2 * H], rounded_w3[:, 2 * H :]], 9)
        banks_a[LAST] = first_layer("bank_a", quantise(rounded[:], "w13", codes_pool), 0, LAST)
        rounded_w3 = placed.tile([P, 4 * H], BF16, align_bytes=64, name="rounded_10", offset=4 * H * 2)
        round_halves(rounded_w3[:], raw3[10])
        act_last = ring.tile([P, 4 * C], F32, align_bytes=LINE, name="act_last", offset=at3[10])
        early = ring.tile([P, FIRST_LATE, 4 * N], BF16, align_bytes=LINE, name="rounded_early", offset=at3[10] + MATRIX_BYTES // 2)
        interleave(scopy, early[:, 0, :], raw2[0])
        gelu(act_last[:], banks_a[LAST])
        interleave(scopy, early[:, 1, :], raw2[1])
        banks_b[10] = first_layer_halves([rounded_w3[:, : 2 * H], rounded_w3[:, 2 * H :]], 10)
        h_9 = placed.tile([P, 4 * C], BF16, align_bytes=64, name="h_9", offset=4 * H * 2)
        gated(h_9[:], acts[9], banks_b[9])
        quantise_w2([0], early[:, 0, :])
        h_quantised[9] = quantise(h_9[:], "h", h_pool)
        h_10 = hidden.tile([P, 4 * C], BF16, align_bytes=64, name="hb")
        gated(h_10[:], acts[10], banks_b[10])

        gate_t = ring.tile([P, 2, T], F32, align_bytes=LINE, name="gate_t", offset=at3[9])
        nc.sync.dma_start(pos_t[0][:], pos1)
        nc.sync.dma_start(pos_t[2][:], pos3)
        nc.sync.dma_start(gate_t[:, 0, :], gate[0])
        nc.sync.dma_start(pos_t[1][:], pos2)
        nc.sync.dma_start(gate_t[:, 1, :DIRECT], gate[1, :, :DIRECT])

        halves = [
            ring.tile([P, 2 * H], BF16, align_bytes=LINE, name="rounded_last_0", offset=at3[9] + MATRIX_BYTES // 2)[:],
            ring.tile([P, 2 * H], BF16, align_bytes=LINE, name="rounded_last_1", offset=at3[7])[:],
        ]
        round_half(vcopy, halves[0], raw3[LAST], 0)
        round_half(scopy, halves[1], raw3[LAST], 1)
        h_quantised[10] = quantise(h_10[:], "h", h_pool)
        bank_last = first_layer_halves(halves, LAST)

        late = ring.tile([P, 3, 4 * N], BF16, align_bytes=LINE, name="rounded_late", offset=at3[7] + W2_BYTES)
        pair = ring.tile([P, 2, 4 * N], BF16, align_bytes=LINE, name="rounded_pair", offset=at3[7])
        pair_78 = y_all[:, 6 * C : 10 * C].bitcast(BF16)

        def flat(rows):
            return rows.rearrange("p e c -> p (e c)")

        interleave(scopy, late[:, 0, :], raw2[2])
        interleave(scopy, late[:, 1, :], raw2[3])
        interleave(scopy, pair[:, 1, :], raw2[5])
        interleave(scopy, pair_78[:, : 4 * N], raw2[7])
        interleave(scopy, pair_78[:, 4 * N :], raw2[8])
        quantise_w2([1], early[:, 1, :])
        interleave(vcopy, pair[:, 0, :], raw2[4])
        quantise_w2([2, 3], flat(late[:, :2, :]))
        h_last = hidden.tile([P, 4 * C], BF16, align_bytes=64, name="hb")
        gated(h_last[:], act_last[:], bank_last)
        codes_late = ring.tile([P, 8 * N], U32, align_bytes=LINE, name="codes_c", offset=at3[10])
        quantise_w2([4, 5], flat(pair[:]), codes_late[:, : 2 * N])
        h_quantised[LAST] = quantise(h_last[:], "h", h_pool)
        interleave(vcopy, pair[:, 0, :], raw2[6])
        interleave(scopy, pair[:, 1, :], raw2[9])
        interleave(scopy, late[:, 2, :], raw2[10])
        quantise_w2([7, 8], pair_78, codes_late[:, 2 * N : 4 * N])
        quantise_w2([6, 9], flat(pair[:]), codes_late[:, 4 * N : 6 * N])
        interleave(vcopy, pair_78[:, 4 * N : 4 * (N + LAST_SPLIT)], raw2[LAST][:, :, :LAST_SPLIT])
        interleave(scopy, pair_78[:, 4 * (N + LAST_SPLIT) :], raw2[LAST][:, :, LAST_SPLIT:])
        quantise_w2([10], late[:, 2, :], codes_late[:, 7 * N :])
        quantise_w2([LAST], pair_78[:, 4 * N :], codes_late[:, 6 * N : 7 * N])
        second_layer(range(0, 4), scopy)
        second_layer(range(4, 7), scopy)
        second_layer(range(7, 10), vcopy)
        second_layer(range(10, LAST), scopy)
        second_layer(range(LAST, E), scopy, psum, "bank_a")

        first = keep.tile([P, T], F32, align_bytes=64, name="first")
        second = keep.tile([P, T], F32, align_bytes=64, name="second")
        third = keep.tile([P, T], F32, align_bytes=64, name="third")
        turned = keep.tile([P, TURNED, P], F32, align_bytes=64, name="turned")
        both = keep.tile([P, DIRECT], F32, align_bytes=LINE, name="both")
        result = keep.tile([P, DIRECT], F32, align_bytes=LINE, name="result")

        def lists(r, cols):
            return pos_t[r][:, cols.start // 16 : cols.stop // 16]

        def weighted(dst, r, cols):
            nc.vector.tensor_tensor(dst[:, cols], y_all[:].indirect(lists(r, cols)), gate_t[:, r, cols], MULT)

        def fetched(dst, r, cols):
            nc.scalar.activation(dst[:, cols], y_all[:].indirect(lists(r, cols)), COPY)

        pieces = [slice(0, 2 * P), slice(2 * P, DIRECT), slice(DIRECT, T)]
        weighted(first, 0, slice(0, T))
        weighted(second, 1, pieces[0])
        weighted(second, 1, pieces[1])
        fetched(third, 2, slice(0, T // 2))
        fetched(third, 2, slice(T // 2, T))
        fetched(second, 1, pieces[2])
        for cols in pieces[:2]:
            nc.vector.tensor_tensor(both[:, cols], first[:, cols], second[:, cols], ADD)
        sums = [psum.tile([P, piece.stop - piece.start], F32, name=name) for piece, name in zip(pieces, ("bank_a", "bank_a", "bank_b"))]
        items = [(third, block, block + 1) for block in range(BLOCKS)] + [(second, BLOCKS - 1, 0)]
        banks = [psum_y.tile([P, P], F32, name="bank_y") for block in range(BLOCKS)] + [psum.tile([P, P], F32, name="bank_b")]
        for bank, (values, block, column) in zip(banks, items):
            nc.tensor.transpose(bank[:], values[:, block * P : (block + 1) * P], identity[:])
        for bank, (values, block, column) in zip(banks, items):
            nc.scalar.activation(turned[:, column, :], bank[:], COPY, scale=gate_cols[:, column : column + 1])
        for values, block, column in items:
            piece = max(block - 1, 0)
            at = block * P - pieces[piece].start
            alone = block < BLOCKS - 1
            nc.tensor.matmul(
                sums[piece][:, at : at + P],
                turned[:, column, :],
                identity[:],
                start=values is third,
                stop=alone or values is second,
                is_transpose=True,
            )
        finished = [result[:, pieces[0]], result[:, pieces[1]], both[:, :P]]
        for piece, cols in enumerate(pieces):
            nc.vector.tensor_tensor(finished[piece], sums[piece][:], (both if piece < 2 else first)[:, cols], ADD)
            nc.sync.dma_start(out[:, cols], finished[piece])
